import numpy as np, ml_dtypes
CORES = [6,15,38,47]
N = 4
import mx_ref
BF = ml_dtypes.bfloat16
def gcols(t, e):
    v = np.concatenate([t.reshape(8, 16, -1, 4), np.zeros((8, 16, 1, 4), BF)], axis=2)
    return np.ascontiguousarray(np.stack([v[g][:, e[g]] for g in range(8)])).reshape(128, -1)
def tile(rs):
    return np.stack(rs, axis=2).reshape(128, -1).astype(BF)
def pick(q, e):
    c = np.concatenate([q[0].reshape(128, -1, 4), np.zeros((128, 1, 4), np.uint8)], axis=1); s = np.concatenate([q[1], np.ones((16, 1), np.uint8)], axis=1)
    return (np.ascontiguousarray(c[:, e].reshape(128, -1)), np.ascontiguousarray(s[:, e]))
def join(*qs):
    return (np.concatenate([q[0] for q in qs], axis=1), np.concatenate([q[1] for q in qs], axis=1))
def put(q, e, v):
    c, s = q[0].reshape(128, -1, 4).copy(), q[1].copy(); c[:, e] = v[0].reshape(128, -1, 4); s[:, e] = v[1]
    return (c.reshape(128, -1), s)
def pk(c, s):
    return (np.ascontiguousarray(c), mx_ref.live(s))
def emit(q):
    return q[0], q[1]
def packed(v, rng):
    q = [mx_ref.quantize(np.ascontiguousarray(v[r])) for r in range(N)]
    return np.stack([a for a, b in q]), np.stack([mx_ref.plane(b, rng) for a, b in q])
def values_of_codes():
    e, c = np.zeros((128, 128, 4), np.float32), np.zeros((128, 2, 4), np.uint8)
    e[np.arange(128), np.arange(128), 0] = 1
    c[:127, :, 0] = np.arange(256).reshape(2, 128).T[:127]
    return mx_ref.matmul(mx_ref.quantize(e.reshape(128, 512).astype(BF)), (c.reshape(128, 8), np.full((16, 2), 127, np.uint8))).T.reshape(-1).astype(np.float64)
CODE_VALUE, SCALE_VALUE = values_of_codes(), 2.0 ** (np.arange(256) - 127.0)
def decode(q):
    return (CODE_VALUE[q[0]].reshape(16, 8, -1, 4) * SCALE_VALUE[q[1]][:, None, :, None] + 0.0).reshape(128, -1).astype(np.float32)
def f(rng, *shape):
    return mx_ref.flush((rng.standard_normal(shape, dtype=np.float32) * np.exp2(rng.integers(-2, 3, shape[:-1] + (1,)))).astype(BF))
def wide(rng, *shape, cols=0):
    v = rng.standard_normal(shape, dtype=np.float32) * np.exp2(rng.integers(-12, 13, shape)).astype(np.float32)
    if cols: v *= np.repeat(np.exp2(rng.integers(-cols, cols + 1, shape[:-2] + (1, shape[-1] // 4))) * (rng.random(shape[:-2] + (1, shape[-1] // 4)) > 0.0625), 4, axis=-1).astype(np.float32)
    return mx_ref.flush(v.astype(BF))
C, M, R = 256, 96, 3
HALF = np.arange(C) // 2
def order(p):
    return np.argsort(-(p + np.float32(0.0)), axis=1, kind="stable")
def gput(t, e, h):
    a, b = t.reshape(8, 16, -1, 4).copy(), h.reshape(8, 16, -1, 4)
    for g in range(8): a[g][:, e[g]] = b[g]
    return a.reshape(128, -1)
def trials(q, t, o):
    s = []
    for g in range(0, 8, 2):
        e = np.concatenate([np.where(np.arange(8)[:, None] == k, o, o[:, HALF]) for k in (g, g + 1)], axis=1)
        p = mx_ref.matmul(q, mx_ref.quantize(gcols(t, e)))
        s += [p[16 * g, :C], p[16 * g + 16, C:]]
    return np.stack(s)
def big(v):
    v = v.astype(np.float32)
    v[np.abs(v) < np.float32(2.0 ** -16)] = 0
    return v.astype(BF)
def numbers_of(rng):
    return {"x": big(f(rng, N, 128, 4 * C)), "u": np.array(f(rng, N, 128, 512)), "v": np.array(f(rng, N, 128, 512))}
def layers(rng):
    return big(f(rng, N, 128, 2048)).reshape(N, 8, 16, 4, 8, 16, 4)
def weights(rng, w):
    c, p = packed(np.ascontiguousarray(w).reshape(N, 128, 2048), rng)
    return {"wc": c, "ws": p}
def signs(rng):
    return np.stack([rng.permutation(8) % 2 * 2.0 - 1.0 for r in range(N)])
def setup_inputs(rng):
    return {**numbers_of(rng), **weights(rng, layers(rng))}
def setup_inputs_ties(rng):
    d = numbers_of(rng)
    e = rng.permutation(N)
    x = d["x"].reshape(N, 8, 16, C, 4)
    u = d["u"].reshape(N, 8, 16, 128, 4)
    u[:, :, 8:, ::16] = 0
    for r in range(N):
        k = np.zeros(C, int) if r == e[0] else rng.permutation(C) % 3
        a = x[r][:, :8, :3].copy()
        a[:, :, 2] = 0
        x[r][:, :8] = a[:, :, k]
        for g in rng.permutation(8)[:4]: u[r, g, :, 16 * g] = 0
    x[e[1]] = 0
    w = layers(rng)
    w[:, :, :, :, :, :8] = 0
    return {"x": x.reshape(N, 128, 4 * C), "u": u.reshape(N, 128, 512), "v": d["v"], **weights(rng, w)}
def setup_inputs_near(rng):
    d = numbers_of(rng)
    x = d["x"].astype(np.float32).reshape(N, 8, 16, C, 4)
    u = d["u"].reshape(N, 128, 128, 4)
    u[:, :, ::16] = 0
    o, c, j = rng.permutation(N) % 4, signs(rng), np.arange(C)
    upper = j // (C // 2)
    own = np.arange(128)[:, None, None] // 16 == np.arange(8)[:, None]
    for r in range(N):
        if o[r] == 3:
            k = rng.choice([-1.0, 1.0], (128, 8, 4)) * rng.integers(8, 16, (128, 8, 4)) * 0.125
            u[r, :, ::16] = (k * np.where(own, 2.0 ** -18, 1.0)).astype(np.float32).astype(BF)
            continue
        a = rng.integers(0, C, (8, 1))
        s = (j + a) % (C // 2) if o[r] == 2 else (j + a) % C // 2
        size = 2.0 ** -4 if o[r] == 2 else 1.0
        z = ((s[:, :, None] >> np.arange(8)) & 1) * np.exp2(np.arange(8) - 23.0) * size
        x[r] = 0
        if o[r] == 2:
            x[r, :, 0, :, 0] = np.where(c[r][:, None] > 0, (8 + upper) * 2.0 ** -30, 9 * upper * 2.0 ** -33)
            x[r, :, 1, :, 0] = np.where(c[r][:, None] > 0, 0.0, 10 * (1 - upper) * 2.0 ** -33)
        else:
            x[r, :, 0, :, 0] = c[r][:, None]
            for i in rng.permutation(8)[:4]: x[r, i, 0, rng.integers(C), 0] *= np.float32(2.0 ** 30)
        x[r, :, 8] = z[:, :, :4]
        x[r, :, 9] = z[:, :, 4:]
        x[r, :, 10:] = rng.integers(4, 8, (8, 6, C, 4)) * 2.0 ** -20 * size
        k = 1.0 if o[r] == 0 else 2.0 ** -30
        for h in range(0, 128, 16):
            u[r, h, h, 0] = k
            u[r, h + 8:h + 10, h] = k
            if o[r] == 2 and c[r, h // 16] < 0:
                u[r, h, h, 0] = 9 * 2.0 ** -33
                u[r, h + 1, h, 0] = 2.0 ** -30
    w = layers(rng)
    w[:, :, :10] = 0
    w[:, :, :, :, :, :10] = 0
    return {"x": x.reshape(N, 128, 4 * C).astype(BF), "u": u.reshape(N, 128, 512), "v": d["v"], **weights(rng, w)}
def setup_inputs_huge(rng):
    d = numbers_of(rng)
    c = np.stack([rng.permutation(C) % 2 * 2.0 - 1.0 for r in range(N)])
    c[rng.permutation(N) < N // 2] = -1
    x = (0.6 + 0.2 * rng.random((N, 128, C, 4))) * np.where(c < 0, -2.0 ** 30, 2.0 ** 28)[:, None, :, None]
    u = d["u"].reshape(N, 128, 128, 4)
    s = signs(rng)
    a = 2.0 ** 30 * (1 - 0.25 * rng.random((N, 128, 8, 4))) * s[:, None, :, None]
    for r in range(N):
        if (c[r] < 0).all():
            x[r, :, rng.integers(C)] = -2.0 ** 30
            a[r, :, rng.choice(np.flatnonzero(s[r] > 0))] = 2.0 ** 30
    u[:, :, ::16] = a.astype(np.float32).astype(BF)
    w = np.zeros((N, 128, 4, 128, 4), np.float32)
    i = np.arange(128)
    for b in range(4): w[:, i, b, i, b] = 16
    return {"x": x.astype(np.float32).reshape(N, 128, 4 * C).astype(BF), "u": u.reshape(N, 128, 512), "v": d["v"], **weights(rng, w.astype(BF))}
def setup_inputs_twice(rng):
    d = numbers_of(rng)
    e = 2 + np.arange(32).reshape(8, 4) // 2
    n = (N, 16, 8, C, 4)
    x = rng.choice([-1.0, 1.0], n) * (9 + 2 * rng.integers(0, 4, n)) * 0.125 * np.exp2(0.0 - e)[:, None]
    x[:, :, 0] = 0
    x[:, :, 0, :, 0] = 1.96875 * rng.choice([-1.0, 1.0], (N, 16, C))
    x *= np.exp2(rng.integers(1, 5, (N, 16, 1, C, 1)))
    u = d["u"].reshape(N, 16, 8, 128, 4)
    k = rng.choice([-1.0, 1.0], (N, 16, 8, 8, 4)) * rng.integers(8, 16, (N, 16, 8, 8, 4)) * 0.125 * np.exp2(e - 17.0)[:, None]
    k[:, :, 0] = 0
    u[:, :, :, ::16] = k.astype(np.float32).astype(BF)
    return {"x": x.astype(np.float32).reshape(N, 128, 4 * C).astype(BF), "u": u.reshape(N, 128, 512), "v": d["v"], **weights(rng, layers(rng))}
def setup_inputs_spread(rng):
    d = setup_inputs(rng)
    d["x"] = big(wide(rng, N, 128, 4 * C, cols=6))
    return d
def check_inputs(d):
    b = []
    for k in ("x", "u", "v"):
        a = np.abs(d[k].astype(np.float32))
        if not (np.isfinite(a).all() and ((a == 0) | (a >= 2.0 ** -30) & (a <= 2.0 ** 30)).all()): b.append("a value of " + k)
    none, least, most = [emit(mx_ref.quantize(np.full((128, 16), k, np.float32).astype(BF)))[1][0, 0] for k in (0.0, 2.0 ** -30, 2.0 ** 30)]
    for r in range(N):
        if ((d["wc"][r] == 0x7F) | (d["wc"][r] == 0xFF)).any(): b.append("wc: a code that is no number")
        s = mx_ref.live(d["ws"][r])
        if ((s != none) & ((s < least) | (s > most))).any(): b.append("ws: a scale out of range")
    return b
def reference(x, u, v, wc, ws):
    qu = [mx_ref.quantize(u[r]) for r in range(N)]
    lay = [pk(wc[r], ws[r]) for r in range(N)]
    now = [x[r] for r in range(N)]
    o = [order(mx_ref.matmul(qu[r], mx_ref.quantize(x[r]))[::16]) for r in range(N)]
    for t in range(R):
        sent = []
        for r in range(N):
            now[r] = decode(mx_ref.quantize(now[r])).astype(BF)
            score = np.zeros((8, C), np.float32)
            np.put_along_axis(score, o[r], trials(qu[r], now[r], o[r]), axis=1)
            o[r] = order(score)
            sent.append(mx_ref.quantize(gcols(now[r], o[r][:, :M])))
        for r in range(N):
            q = sent[(r - 1 - t) % N]
            c = decode(q)
            h = tile([np.maximum(mx_ref.matmul(pick(lay[r], np.arange(128 * b, 128 * b + 128)), q), np.float32(0.0)) * np.float32(0.03125) + c[:, b::4] for b in range(4)])
            now[r] = gput(now[r], o[r][:, C - M:], h)
    y, ol = np.zeros((N, 128, C), np.float32), np.zeros((N, 8, C), np.float32)
    oc, osc = np.zeros((N, 128, 4 * C), np.uint8), np.zeros((N, 16, C), np.uint8)
    for r in range(N):
        q = mx_ref.quantize(now[r])
        y[r] = mx_ref.matmul(mx_ref.quantize(v[r]), q)
        ol[r] = o[r]
        oc[r], osc[r] = emit(q)
    return {"y": y, "ol": ol, "oc": oc, "osc": osc}

@@ -1,0 +1,642 @@
+from concourse.mybir import dt, AluOpType as ALU, ActivationFunctionType as ACT, AxisListType as AX
+
+C, M, R = 256, 96, 3
+K = C - M
+F32, BF, U16, I32, X4, U8 = "float32", "bfloat16", "uint16", "int32", "float8_e4m3fn_x4", "uint8"
+BIG = 2.0 ** 90
+CT_A, CT_E, CT_B, CT_C, CT_D, CT_N = 0, 256, 384, 592, 736, 864
+SLOT = {"q": (CT_A, 0), 15: (CT_A, 1), 14: (CT_A, 2), 13: (CT_A, 3), 0: (CT_E, 0)}
+for _k, _base in enumerate((CT_B, CT_C, CT_D)):
+    for _t in range(4):
+        SLOT[12 - 4 * _k - _t] = (_base, _t)
+ON_SCALAR = (15, 14)
+SUM_ON_VECTOR = (3, 2, 1)
+EO_A, EO_E, EO_O, EO_L, EO_N = 0, 128, 128 + K, 128 + 2 * K, 128 + 2 * C
+GATHER, SCATTER, S_FIX, PE_COL, LOAD, SLACK, TRIES = 1.56, 3.8, 60, 0.6, 2000, 100, 3000
+CASES = ((80, 3000, 1.0, 1.0), (60, 2000, 0.7, 0.8), (120, 4000, 1.3, 1.2))
+BK = {"a": (0, 1, 2, 3), "e": (4, 5, 0, 1), "o": (2, 3, 4, 5), "se": (6, 7, 6, 7), "w": (0, 1, 2, 3), "d": (4, 5, 0, 1),
+      "le": (2, 3, 4, 5), "lo": (0, 1, 2, 3), "sl": (4, 5, 6, 7)}
+
+SCRATCH = {
+    "ps": ("psum", [128, 4096], F32),
+    "xt": ("sbuf", [128, 4 * C], BF), "ut": ("sbuf", [128, 512], BF), "vt": ("sbuf", [128, 512], BF),
+    "sh": ("sbuf", [128, 16 * C], BF), "tt": ("sbuf", [128, 4 * C], BF),
+    "ct": ("sbuf", [128, 4 * CT_N], BF), "gs": ("sbuf", [128, 3 * C], BF), "junk": ("sbuf", [128, 2 * C], BF),
+    "ones": ("sbuf", [128, 528], BF),
+    "zf": ("sbuf", [128, 528], BF), "ze": ("sbuf", [128, 528], BF), "zo": ("sbuf", [128, 528], BF),
+    "bd0": ("sbuf", [128, 512], BF), "bd": ("sbuf", [128, 512], BF),
+    "pi": ("sbuf", [128, 1], I32), "pci": ("sbuf", [128, 8], I32), "pc": ("sbuf", [128, 16], F32),
+    "j16": ("sbuf", [128, C], F32), "j4": ("sbuf", [128, C], F32), "i256": ("sbuf", [128, C], F32),
+    "i16": ("sbuf", [128, 16], F32), "ia": ("sbuf", [128, 160], F32), "plf": ("sbuf", [128, 128], F32),
+    "tmp": ("sbuf", [128, 3 * C], F32), "mk": ("sbuf", [128, C], F32),
+    "d0": ("sbuf", [128, C], F32), "w16": ("sbuf", [128, C], F32), "w4": ("sbuf", [128, C], F32),
+    "tab": ("sbuf", [128, C], F32), "cj": ("sbuf", [128, 16], F32),
+    "ul": ("sbuf", [128, 16], U16), "a2l": ("sbuf", [128, 16], U16), "pl": ("sbuf", [128, 128], U16),
+    "r2": ("sbuf", [128, 2 * C], F32), "rr": ("sbuf", [128, C], F32), "inj": ("sbuf", [128, C], F32),
+    "zs": ("sbuf", [128, C], F32), "uw": ("sbuf", [128, C], F32), "rs": ("sbuf", [128, 16], F32),
+    "rs2": ("sbuf", [128, 16], F32), "rkf": ("sbuf", [128, 16], F32), "rku": ("sbuf", [128, 16], U16),
+    "r2l": ("sbuf", [128, 16], U16), "vrow": ("sbuf", [128, 4 * C], F32), "lrow": ("sbuf", [128, C], F32),
+    "u4": ("sbuf", [128, 2 * C], F32), "off": ("sbuf", [128, 64], U16), "off2": ("sbuf", [128, 64], U16),
+    "orow": ("sbuf", [128, C], F32), "rel": ("sbuf", [128, 4 * M], F32), "yt": ("sbuf", [128, C], F32),
+}
+_PAIRS = {"x": C, "u": 128, "us": 128, "v": 128, "w": 512, "e": 12 * 128, "bd": 128, "ct": CT_N, "land": 3 * M + 128, "t": C}
+for _t in range(R + 1):
+    _PAIRS["b%d" % _t] = K
+for _t in range(R):
+    _PAIRS["m%d" % _t] = C
+    _PAIRS["n%d" % _t] = 128
+    _PAIRS["eo%d" % _t] = EO_N
+    _PAIRS["y%d" % _t] = 8 * C
+    SCRATCH["eo%d" % _t] = ("sbuf", [128, 4 * EO_N], BF)
+for _n, _w in _PAIRS.items():
+    SCRATCH["q_" + _n] = ("sbuf", [128, _w], X4)
+    SCRATCH["s_" + _n] = ("sbuf", [128, _w], U8)
+
+DMAS = ["dx", "du", "dv", "dwc", "dws", "dy0", "dol", "doc", "ds0", "ds1", "ds2", "ds3"]
+SEMAPHORES = ["cV", "cS", "cP", "cG", "sent"] + DMAS + ["arr%d" % _t for _t in range(R)]
+
+
+def V(buf, c0=0, c1=None, step=1, p0=0, p1=128):
+    return (buf, p0, p1, c0, SCRATCH[buf][1][1] if c1 is None else c1, step)
+
+
+def bank(b, c0, c1, step=1, p0=0, p1=128):
+    return V("ps", 512 * b + c0, 512 * b + c1, step, p0, p1)
+
+
+def _mask(v):
+    if v[0] == "ps":
+        return 1 << (v[3] // 512)
+    if v[5] == 1:
+        return ((1 << (v[4] - v[3])) - 1) << v[3]
+    m = 0
+    for c in range(v[3], v[4], v[5]):
+        m |= 1 << c
+    return m
+
+
+_ORDER = []
+
+
+def arrange(ops):
+    if not _ORDER:
+        _ORDER.extend(search(ops))
+    return [ops[i] if k == 0 else ops[i][7] for i, k in _ORDER]
+
+
+def search(ops):
+    n = len(ops)
+    seen, before, sends, own = {}, [], [], []
+    for i, o in enumerate(ops):
+        deps = {}
+        for vs, wr in ((o[2], False), (o[3], True)):
+            for v in vs:
+                m = _mask(v)
+                for (j, w2, p0, p1, m2) in seen.get(v[0], ()):
+                    if (m2 & m) and (wr or w2) and p0 < v[2] and v[1] < p1:
+                        both_pe = o[0] == "P" and ops[j][0] == "P"
+                        deps[j] = (0, 0, 0) if both_pe else (1, LOAD, 0) if ops[j][4] else (1, 60, 0) if ops[j][0] == "P" else (1, 0, 0)
+        for vs, wr in ((o[2], False), (o[3], True)):
+            for v in vs:
+                seen.setdefault(v[0], []).append((i, wr, v[1], v[2], _mask(v)))
+        if o[0] == "G":
+            if own:
+                deps.setdefault(own[-1], (0, 0, 0))
+            own.append(i)
+        if o[4] == "remote":
+            sends.append(i)
+        if o[5]:
+            deps[sends[-1]] = (1, 0, 1)
+        before.append(deps)
+    reach = []
+    for i, d in enumerate(before):
+        r = 0
+        for j in sorted(d, reverse=True):
+            if r >> j & 1 and d[j] == (1, 0, 0):
+                del d[j]
+            r |= reach[j] | 1 << j
+        reach.append(r)
+    after = [[] for _ in ops]
+    for i, d in enumerate(before):
+        for j in d:
+            after[j].append(i)
+    forms = [[o for o in (ops[i], ops[i][7]) if o is not None] for i in range(n)]
+    banks = [[_mask(v) for v in o[2] if v[0] == "ps"] for o in ops]
+    cases = []
+    for (wake, flight, pe, ga) in CASES:
+        lag = [[(j, w[0] * wake + w[1] + w[2] * flight) for j, w in d.items()] for d in before]
+        cost = [[o[6] * (pe if o[0] == "P" else 1.0) * (ga if o[8] else 1.0) for o in f] for f in forms]
+        cases.append((wake, lag, cost))
+    wake, lag, cost = cases[0]
+    tail = [0.0] * n
+    for i in range(n - 1, -1, -1):
+        tail[i] += cost[i][0] + (LOAD if ops[i][4] else 0)
+        for j, w in lag[i]:
+            tail[j] = max(tail[j], w + tail[i])
+
+    def start(i, k, t, free, busy, wake):
+        q = forms[i][k][0]
+        t = max(t, free[q])
+        for m in banks[i]:
+            q2, t2 = busy.get(m, (q, 0.0))
+            if q2 != q:
+                t = max(t, t2 + wake)
+        return t
+
+    def build(bias, pref):
+        left = [len(d) for d in before]
+        ready = {i: 0.0 for i in range(n) if not left[i]}
+        free, busy, end, order = {q: 0.0 for q in "VSPGY"}, {}, [0.0] * n, []
+        while ready:
+            cand = [(start(i, k, t0, free, busy, wake), i, k) for i, t0 in ready.items()
+                    for k in range(len(forms[i])) if pref[i] in (-1, k)]
+            first = min(cand)
+            q = forms[first[1]][first[2]][0]
+            t, i, k = max([c for c in cand if c[0] <= first[0] + SLACK and forms[c[1]][c[2]][0] == q],
+                          key=lambda c: tail[c[1]] + bias[c[1]])
+            end[i] = free[q] = t + cost[i][k]
+            for m in banks[i]:
+                busy[m] = (q, end[i])
+            order.append((i, k))
+            del ready[i]
+            for j in after[i]:
+                left[j] -= 1
+                if not left[j]:
+                    ready[j] = max(end[x] + w for x, w in lag[j])
+        return order
+
+    def length(order):
+        total = 0.0
+        for wake_, lag_, cost_ in cases:
+            free, busy, end = {q: 0.0 for q in "VSPGY"}, {}, [0.0] * n
+            for i, k in order:
+                q = forms[i][k][0]
+                t = start(i, k, max([end[x] + w for x, w in lag_[i]] + [0.0]), free, busy, wake_)
+                end[i] = free[q] = t + cost_[i][k]
+                for m in banks[i]:
+                    busy[m] = (q, end[i])
+            total += max(end[i] + (LOAD if ops[i][4] else 0) for i in range(n))
+        return total
+    seed = [12345]
+
+    def rnd(m):
+        seed[0] = (seed[0] * 1103515245 + 12345) % 2147483648
+        return (seed[0] >> 8) % m
+    bias, pref = [0.0] * n, [-1] * n
+    order = build(bias, pref)
+    best = length(order)
+    for _ in range(TRIES):
+        b2, p2 = list(bias), list(pref)
+        at = rnd(n)
+        for _k in range(1 + rnd(6)):
+            i = order[min(n - 1, at + rnd(40))][0]
+            b2[i] = float(rnd(2001) - 1000)
+            if len(forms[i]) > 1:
+                p2[i] = rnd(3) - 1
+        o2 = build(b2, p2)
+        l2 = length(o2)
+        if l2 <= best:
+            bias, pref, order, best = b2, p2, o2, l2
+    return order
+
+
+def rank_program(g, core, T, topo):
+    rank = T.rank_of(core)
+    if rank is None:
+        return
+    n_ranks = len(T.cores)
+    ops = []
+
+    def ap(v):
+        if not isinstance(v, tuple):
+            return v
+        if v[0] == "ind":
+            return ap(v[1]).indirect(ap(v[2]))
+        if v[0] == "ind32":
+            return ap(v[1]).bitcast(dt.uint32).indirect(ap(v[2]))
+        return T[v[0]][v[1]:v[2], v[3]:v[4]:v[5]] if v[5] != 1 else T[v[0]][v[1]:v[2], v[3]:v[4]]
+
+    def parts(vs):
+        out = []
+        for v in vs:
+            if isinstance(v, tuple):
+                out += [v[1], v[2]] if v[0] in ("ind", "ind32") else [v]
+        return out
+
+    def span(q, reads, writes, rate=1.0):
+        a = reads[0] if reads else writes[0]
+        if a[0] in ("ind", "ind32"):
+            return 60 + GATHER * 16 * (a[2][4] - a[2][3])
+        n = len(range(a[3], a[4], a[5]))
+        if q == "V":
+            if SCRATCH[a[0]][2] == BF and SCRATCH[writes[0][0]][2] == BF:
+                rate *= 0.5
+            return max(64, n * rate)
+        return (S_FIX + n) if q == "S" else 150 + 2 * n
+
+    def op(q, emit, reads, writes, dma=None, ext=(), cost=None, other=None):
+        if cost is None:
+            cost = span(q, reads, writes)
+        ops.append((q, emit, parts(reads), parts(writes), dma, ext, cost, other, bool(reads) and reads[0][0] in ("ind", "ind32")))
+
+    def ind(win, off):
+        return ("ind", win, off)
+
+    def ts(out, a, s1, s2, o0, o1=None):
+        if o1 is None:
+            op("V", lambda: g.vector.tensor_scalar(ap(out), ap(a), ap(s1), None, o0), [a, s1], [out])
+        else:
+            op("V", lambda: g.vector.tensor_scalar(ap(out), ap(a), ap(s1), ap(s2), o0, o1), [a, s1, s2], [out])
+
+    def tt(out, a, b, o):
+        op("V", lambda: g.vector.tensor_tensor(ap(out), ap(a), ap(b), o), [a, b], [out],
+           cost=span("V", [b], [out], 1.0 if a[0] == "ps" else 2.0))
+
+    def cp(out, a):
+        op("V", lambda: g.vector.tensor_copy(ap(out), ap(a)), [a], [out])
+
+    def scatter(win, off, a):
+        op("V", lambda: g.vector.tensor_copy(ap(ind(win, off)), ap(a)), [a, off], [win], cost=60 + SCATTER * C)
+
+    def scan(out, a, b, o0, o1, init=0.0):
+        op("V", lambda: g.vector.tensor_tensor_scan(ap(out), ap(a), ap(b), init, o0, o1), [a, b], [out])
+
+    def reduce_add(out, a):
+        op("V", lambda: g.vector.tensor_reduce(ap(out), ap(a), AX.X, ALU.add), [a], [out])
+
+    def fill(out, c):
+        op("V", lambda: g.vector.memset(ap(out), c), [], [out])
+
+    def act(out, a, f, bias=None, scale=None, acc=None):
+        kw = {}
+        if bias is not None:
+            kw["bias"] = bias
+        if scale is not None:
+            kw["scale"] = scale
+        if acc is not None:
+            kw["accum_out"] = acc
+        op("S", lambda: g.scalar.activation(ap(out), ap(a), f, **{k: ap(x) for k, x in kw.items()}),
+           [a, bias, scale], [out, acc])
+
+    def affine(out, a, scale, bias):
+        act(out, a, ACT.Identity, bias=bias, scale=scale)
+
+    def move(q, out, a):
+        if q == "F":
+            act(out, a, ACT.Copy)
+            other = ops.pop()
+            op("V", lambda: g.vector.tensor_copy(ap(out), ap(a)), [a], [out], other=other)
+        elif q == "V":
+            cp(out, a)
+        else:
+            act(out, a, ACT.Copy)
+
+    def iota(out, pattern, base=0, cm=0):
+        if SCRATCH[out[0]][2] == I32:
+            op("G", lambda: g.iota(ap(out), pattern, base, cm), [], [out])
+        else:
+            op("G", lambda: g.iota(ap(out), pattern, base, cm, allow_small_or_imprecise_dtypes=True), [], [out])
+
+    def keep(out, a, pattern, cmp_, base, cm):
+        op("G", lambda: g.affine_select(ap(out), ap(a), pattern, cmp_, 0.0, base, cm), [a], [out])
+
+    def quant(name, c0, tile, e0, n):
+        qv, sv, tv = V("q_" + name, c0, c0 + n), V("s_" + name, c0, c0 + n), V(tile, e0, e0 + 4 * n)
+        op("V", lambda: g.vector.quantize_mx(ap(qv), ap(sv), ap(tv)), [tv], [qv, sv], cost=15 + 1.06 * n)
+
+    def mm(b, w, w0, x, x0, n, start=True, stop=True, ext=()):
+        o, a = bank(b, 0, n), [V("q_" + w, w0, w0 + 128), V("s_" + w, w0, w0 + 128), V("q_" + x, x0, x0 + n), V("s_" + x, x0, x0 + n)]
+        op("P", lambda: g.tensor.matmul_mx(ap(o), ap(a[0]), ap(a[1]), ap(a[2]), ap(a[3]), start, stop), a, [o], ext=ext,
+           cost=PE_COL * (n + 16))
+
+    def pick(dst, d0, n, src, w1, off):
+        o, w = V("q_" + dst, d0, d0 + n), ("ind32", V("q_" + src, 0, w1), off)
+        op("V", lambda: g.vector.tensor_copy(ap(o).bitcast(dt.uint32), ap(w)), [w], [o])
+        move("S", V("s_" + dst, d0, d0 + n), ind(V("s_" + src, 0, w1), off))
+
+    def dma(q, sem, out, in_, reads, writes):
+        eng = g.sync if q == "Y" else g.scalar
+        op(q, lambda: eng.dma_start(out(), in_()), reads, writes, dma=sem, cost=50)
+
+    def col(k, **p):
+        return V("pc", k, k + 1, **p)
+
+    def run32(a):
+        return dict(p0=32 * a, p1=32 * a + 32)
+    P_L, P_E, P_L2, P_LH, P_LQ, P_L4, P_MK, P_EV, P_CJ, P_O4, P_OL, P_T0, P_T1, P_NQ, P_X = range(15)
+    FULL, EVEN, ODD = 0, 4, 8
+
+    dma("Y", "dx", lambda: T.xt[:], lambda: T.x[:], [], [V("xt")])
+    dma("S", "du", lambda: T.ut[:], lambda: T.u[:], [], [V("ut")])
+    dma("Y", "dwc", lambda: T.q_w[:].bitcast(dt.uint8), lambda: T.wc[:], [], [V("q_w")])
+    dma("Y", "dws", lambda: T.s_w[:], lambda: T.ws[:], [], [V("s_w")])
+    dma("Y", "dv", lambda: T.vt[:], lambda: T.v[:], [], [V("vt")])
+
+    iota(V("pi"), [[0, 1]], 0, 1)
+    iota(V("i16"), [[16, 16]])
+    iota(V("j16"), [[0, 16], [1, 16]])
+    iota(V("ones"), [[0, 528]], 1)
+    keep(V("bd0"), V("ones", 0, 512), [[-16, 8], [0, 64]], ALU.is_ge, 0, 1)
+    keep(V("bd"), V("bd0"), [[16, 8], [0, 64]], ALU.is_ge, 15, -1)
+    keep(V("zf"), V("ones"), [[1, 528]], ALU.is_equal, -3, -4)
+    iota(V("i256"), [[1, C]])
+    iota(V("j4"), [[0, 64], [1, 4]])
+    iota(V("ia", 0, 80), [[0, 8], [8, 10]])
+    iota(V("ia", 80, 128), [[0, 4], [4, 12]], K // 2)
+    iota(V("ia", 128, 148), [[K, 2], [16, 10]], EO_E)
+    iota(V("ia", 148, 160), [[8, 12]], EO_L)
+    fill(V("ct", 4 * (CT_A + 224), 4 * CT_B), 0.0)
+    fill(V("ct", 4 * (CT_B + 160), 4 * CT_C), 0.0)
+    fill(V("ct", 4 * (CT_C + 96), 4 * CT_D), 0.0)
+    fill(V("ct", 4 * CT_D, 4 * CT_N), 0.0)
+    fill(V("rs", 0, 1), 0.0)
+    for k, (by, low) in enumerate(((0, 15), (4, 1), (0, 1), (1, 7), (2, 3), (0, 3))):
+        ts(V("pci", k, k + 1), V("pi"), by, low, ALU.logical_shift_right, ALU.bitwise_and)
+    cp(col(P_L), V("pci", 0, 1))
+    cp(V("pc", 1, 6), V("pci", 1, 6))
+    cp(V("ul"), V("i16"))
+    quant("ct", CT_E, "ct", 4 * CT_E, 128)
+    quant("land", 3 * M, "ct", 4 * CT_E, 128)
+    quant("ct", CT_D, "ct", 4 * CT_D, 128)
+    ts(V("a2l"), V("i16"), 0.5, col(P_LH), ALU.mult, ALU.add)
+    affine(col(P_MK), col(P_L), -BIG, 0.0)
+    affine(col(P_CJ), col(P_L), 512.0, -7681.0)
+    act(V("mk"), V("j16"), ACT.Abs, bias=col(P_MK), scale=BIG)
+    act(V("d0"), V("j16"), ACT.Relu, bias=64 * BIG, scale=-64 * BIG)
+    act(V("tmp", 0, C), V("mk"), ACT.Sign)
+    affine(V("cj"), V("i16"), 1.0, col(P_CJ))
+    affine(V("w16"), V("tmp", 0, C), 16896.0, -16384.0)
+    affine(col(P_NQ), col(P_LQ), -1.0, 0.0)
+    affine(col(P_EV), col(P_E), -1.0, 1.0)
+    affine(col(P_X), col(P_L4), 1.0, -12288.0)
+    affine(col(P_O4), col(P_LQ), 4096.0, col(P_X))
+    affine(col(P_OL), col(P_L2), float(M), col(P_LH))
+    act(V("tmp", C, 2 * C), V("j4"), ACT.Sign, bias=col(P_NQ))
+    act(V("tmp", 2 * C, 3 * C), V("tmp", C, 2 * C), ACT.Abs, scale=17408.0)
+    affine(V("w4"), V("tmp", 2 * C, 3 * C), 1.0, -16384.0)
+    act(V("ze"), V("zf"), ACT.Identity, scale=col(P_EV))
+    act(V("zo"), V("zf"), ACT.Identity, scale=col(P_E))
+    for first, tile in ((FULL, "zf"), (EVEN, "ze"), (ODD, "zo")):
+        for b in range(4):
+            quant("e", (first + b) * 128, tile, 3 - b, 128)
+    quant("bd", 0, "bd", 0, 128)
+    affine(V("plf", 0, 80), V("ia", 0, 80), 1.0, col(P_LH))
+    affine(V("plf", 80, 128), V("ia", 80, 128), 1.0, col(P_LQ))
+    for e in range(2):
+        for a in range(4):
+            c0 = 40 * e + 10 * a
+            affine(V("plf", c0, c0 + 10, **run32(a)), V("ia", 128 + 10 * e, 138 + 10 * e, **run32(a)), 1.0, col(P_L, **run32(a)))
+    for a in range(4):
+        affine(V("plf", 80 + 12 * a, 92 + 12 * a, **run32(a)), V("ia", 148, 160, **run32(a)), 1.0, col(P_OL, **run32(a)))
+    cp(V("pl"), V("plf"))
+    affine(col(P_T0), col(P_E), float(K), float(EO_E))
+    affine(col(P_T1), col(P_E), float(M), float(EO_L - K))
+    affine(V("tab", 0, K), V("i256", 0, K), 1.0, col(P_T0))
+    affine(V("tab", K, C), V("i256", K, C), 1.0, col(P_T1))
+    quant("u", 0, "ut", 0, 128)
+    pick("us", 0, 128, "u", 128, V("ul", 0, 8))
+    quant("x", 0, "xt", 0, C)
+    quant("v", 0, "vt", 0, 128)
+    mm(6, "us", 0, "x", 0, C)
+    mm(7, "us", 0, "x", 0, C)
+
+    def slot(j, c0, c1):
+        base, t = SLOT[j]
+        return V("ct", 4 * (base + c0) + t, 4 * (base + c1), 4)
+
+    def key(j):
+        return V("zs", 16 * j + 15, 16 * j + 16)
+
+    def ranks(first):
+        for c0, c1 in ((128, C), (0, 128)):
+            if first:
+                tt(V("inj", c0, c1), bank(6, c0, c1), V("mk", c0, c1), ALU.add)
+            else:
+                tt(V("inj", c0, c1), ind(V("r2"), V("r2l", c0 // 16, c1 // 16)), V("mk", c0, c1), ALU.add)
+            scan(V("zs", c0, c1), V("d0", c0, c1), V("inj", c0, c1), ALU.add, ALU.min)
+        act(V("rr"), bank(7, 0, C) if first else ind(V("r2"), V("r2l")), ACT.Copy)
+        for j in range(15, -1, -1):
+            n = 16 * j
+            c0 = 0
+            if j in ON_SCALAR:
+                i = ON_SCALAR.index(j)
+                act(V("gs", i * C, i * C + n), V("rr", 0, n), ACT.Sign, bias=key(j), scale=-1.0)
+                act(slot(j, 0, n), V("gs", i * C, i * C + n), ACT.Relu, acc=V("rs", j, j + 1))
+                c0 = n
+            ts(slot(j, c0, n + 16), V("rr", c0, n + 16), key(j), None, ALU.is_lt)
+            if j in SUM_ON_VECTOR:
+                reduce_add(V("rs", j, j + 1), slot(j, 0, n))
+            elif c0 == 0 and j:
+                act(V("junk", C * (j % 2), C * (j % 2) + n), slot(j, 0, n), ACT.Copy, acc=V("rs", j, j + 1))
+        tt(slot("q", 0, C), V("rr"), V("zs"), ALU.is_equal)
+        quant("ct", CT_A, "ct", 4 * CT_A, 272)
+        quant("ct", CT_B, "ct", 4 * CT_B, 208)
+        quant("ct", CT_C, "ct", 4 * CT_C, 224)
+        mm(0, "bd", 0, "ct", CT_A, 256, True, False)
+        mm(0, "bd", 0, "ct", CT_E, 128, False, False)
+        mm(0, "bd", 0, "ct", CT_B, 208, False, False)
+        mm(0, "bd", 0, "ct", CT_C, 144, False, False)
+        mm(0, "bd", 0, "ct", CT_D, 128, False, True)
+        tt(V("rs2"), V("cj"), V("rs"), ALU.subtract)
+        scan(V("uw"), V("w16"), bank(0, 0, C), ALU.add, ALU.max)
+        tt(V("rkf"), V("uw", 15, C, 16), V("rs2"), ALU.add)
+        cp(V("rku"), V("rkf"))
+
+    def wrap4(row, n, off, u0):
+        scan(V("u4", u0, u0 + n), V("w4", 0, n), row, ALU.add, ALU.max)
+        ts(V(off, 0, n // 4), V("u4", u0 + 3, u0 + n, 4), 4.0, col(P_O4), ALU.mult, ALU.add)
+
+    def sh0(s):
+        return 4 * C * s
+
+    def vrow(s):
+        return V("vrow", C * s, C * s + C)
+
+    def gather(q, s, win, c0, c1):
+        move(q, V("sh", sh0(s) + 4 * c0, sh0(s) + 4 * c1), ind(win, V("off", c0 // 4, c1 // 4)))
+
+    def send(t):
+        dst = T.cores[(rank + 1 + t) % n_ranks]
+        rid, pid = topo.addr(dst)[:2]
+        mask = topo.mask(core, dst)
+        l0 = (R - 1 - t) * M
+        b = "b%d" % (t + 1)
+        op("G", lambda: g.remote_dma(T.q_land[:, l0:l0 + M].bitcast(dt.uint8), T["q_" + b][:, 0:M].bitcast(dt.uint8),
+                                     T.sem["arr%d" % t], T.sem.sent, pid, rid, mask), [V("q_" + b)], [], dma="remote", cost=300)
+        op("G", lambda: g.remote_dma(T.s_land[:, l0:l0 + M], T["s_" + b][:, 0:M],
+                                     T.sem["arr%d" % t], T.sem.sent, pid, rid, mask), [V("s_" + b)], [], dma="remote", cost=300)
+        return 2 * len(topo.engines(core, dst))
+
+    def h_tile(t):
+        src = T.cores[(rank - 1 - t) % n_ranks]
+        arrived = (("arr%d" % t, 2 * len(topo.engines(src, core))),)
+        l0 = (R - 1 - t) * M
+        e0 = sh0(t + 1) + 4 * K
+        for b in range(4):
+            mm(BK["w"][b], "w", 128 * b, "land", l0, 128, ext=arrived)
+        for b in range(4):
+            act(V("rel", M * b, M * b + M), bank(BK["w"][b], 0, M), ACT.Relu, scale=0.03125)
+        for b in range(4):
+            bk = BK["d"][b] if t < R - 1 else 4 + b
+            mm(bk, "e", (FULL + b) * 128, "land", l0, 128, ext=arrived)
+            tt(V("sh", e0 + b, e0 + 4 * M, 4), bank(bk, 0, M), V("rel", M * b, M * b + M), ALU.add)
+
+    sent = 0
+    ranks(True)
+    for s in range(R + 1):
+        win = V("xt") if s == 0 else V("eo%d" % (s - 1))
+        scatter(V("lrow"), V("rku"), V("i256") if s == 0 else vrow(s - 1))
+        act(vrow(s), ind(V("tab" if s < R else "i256"), V("rku")), ACT.Copy)
+        n_now = C if s == 0 else K
+        wrap4(V("lrow", 0, n_now), n_now, "off", 0)
+        b, m, n, eo, y = ["%s%d" % (k, s) for k in ("b", "m", "n", "eo", "y")]
+        if s == R:
+            gather("V", s, win, 0, 64)
+            gather("S", s, win, 64, 128)
+            gather("S", s, win, 128, K)
+            quant(b, 0, "sh", sh0(s), 128)
+            sent += send(s - 1)
+            break
+        gather("V", s, win, 0, K // 2)
+        gather("S", s, win, K // 2, K)
+        quant(b, 0, "sh", sh0(s), K)
+        if s > 0:
+            sent += send(s - 1)
+        else:
+            gather("F", s, win, K, C)
+
+        def out(k, bk, c0, c1, first=0):
+            move("F", V(eo, 4 * c0 + k, 4 * c1, 4), bank(bk, first, first + c1 - c0))
+
+        def both(bk, k, kind, own, a0, w):
+            mm(bk, "e", (kind + k) * 128, own, 0, w, True, False)
+            mm(bk, "e", (EVEN + ODD - kind + k) * 128, m, a0, w, False, True)
+            two, one = ops.pop(), ops.pop()
+            ops.append(("P", lambda: (one[1](), two[1]())[1], one[2] + two[2], one[3], None, (), one[6] + two[6], None, False))
+
+        def early(e, h):
+            c0, bk = 640 * e + 320 * h, BK["se"][2 * e + h]
+            pick(y, c0, 320, eo, EO_O + K * e, V("pl", 40 * e + 20 * h, 40 * e + 20 * h + 20))
+            mm(bk, "us", 0, y, c0, 320)
+            for a in (2 * h, 2 * h + 1):
+                move("F", V("r2", e, 2 * K, 2, **run32(a)), bank(bk, K * (a % 2), K * (a % 2) + K, **run32(a)))
+
+        def late(a):
+            c0 = 8 * K + 2 * M * a
+            pick(y, c0, 2 * M, eo, EO_N, V("pl", 80 + 12 * a, 92 + 12 * a))
+            mm(BK["sl"][a], "us", 0, y, c0, 2 * M)
+            move("F", V("r2", 2 * K, 2 * C, **run32(a)), bank(BK["sl"][a], 0, 2 * M, **run32(a)))
+
+        ts(V("r2l"), V("rkf"), 2.0, col(P_E), ALU.mult, ALU.add)
+        pick(m, 0, K, b, 128, V("a2l", 0, 10))
+        pick(m, K, M, b, 128, V("a2l", 10, 16))
+        for k, bk in enumerate(BK["a"]):
+            mm(bk, "e", (FULL + k) * 128, b, 0, 128)
+            out(k, bk, EO_A, EO_E)
+        quant(eo, EO_A, eo, 4 * EO_A, 128)
+        for k, bk in enumerate(BK["e"]):
+            both(bk, k, EVEN, b, 0, K)
+            out(k, bk, EO_E, EO_O)
+        quant(eo, EO_E, eo, 4 * EO_E, K)
+        for k, bk in enumerate(BK["o"]):
+            both(bk, k, ODD, b, 0, K)
+            out(k, bk, EO_O, EO_L)
+        quant(eo, EO_O, eo, 4 * EO_O, K)
+        early(0, 0)
+        early(0, 1)
+        early(1, 0)
+        early(1, 1)
+        if s > 0:
+            h_tile(s - 1)
+        quant(n, 0, "sh", sh0(s) + 4 * 128, 128)
+        for k, bk in enumerate(BK["le"]):
+            both(bk, k, EVEN, n, 128, 128)
+            out(k, bk, EO_L, EO_L + M, 32)
+        for k, bk in enumerate(BK["lo"]):
+            both(bk, k, ODD, n, 128, 128)
+            out(k, bk, EO_L + M, EO_N, 32)
+        quant(eo, EO_L, eo, 4 * EO_L, 2 * M)
+        for a in range(4):
+            late(a)
+        ranks(False)
+
+    wrap4(vrow(R), C, "off2", C)
+    scatter(V("orow"), V("rku"), V("i256"))
+    dma("Y", "dol", lambda: T.ol[:], lambda: T.orow[0:128:16, :], [V("orow")], [])
+    h_tile(R - 1)
+    last = V("sh", sh0(R), sh0(R) + 4 * C)
+    move("V", V("tt", 0, 2 * C), ind(last, V("off2", 0, 32)))
+    move("S", V("tt", 2 * C, 4 * C), ind(last, V("off2", 32, 64)))
+    quant("t", 0, "tt", 0, C)
+    dma("Y", "doc", lambda: T.oc[:], lambda: T.q_t[:].bitcast(dt.uint8), [V("q_t")], [])
+    mm(6, "v", 0, "t", 0, C)
+
+    def store_scales(k, q):
+        dma(q, "ds%d" % k, lambda: T.osc[4 * k:4 * k + 4, :], lambda: T.s_t[32 * k:32 * k + 4, :], [V("s_t")], [])
+    cp(V("yt"), bank(6, 0, C))
+    store_scales(0, "S")
+    store_scales(1, "S")
+    store_scales(2, "S")
+    store_scales(3, "Y")
+    dma("Y", "dy0", lambda: T.y[:], lambda: T.yt[:], [V("yt")], [])
+
+    ops = arrange(ops)
+
+    src = [o[4] if o[4] else o[0] for o in ops]
+    seen = {}
+    know = {q: {} for q in "VSPGY"}
+    clock, waits, needed = [], [], set()
+    for i, o in enumerate(ops):
+        q, deps = o[0], set()
+        for vs, wr in ((o[2], False), (o[3], True)):
+            for v in vs:
+                mk_ = _mask(v)
+                psum = v[0] == "ps"
+                for (j, w2, p0, p1, m2) in seen.get(v[0], ()):
+                    if not (m2 & mk_):
+                        continue
+                    if psum:
+                        if src[j] != q:
+                            deps.add(j)
+                    elif (wr or w2) and p0 < v[2] and v[1] < p1:
+                        deps.add(j)
+        for vs, wr in ((o[2], False), (o[3], True)):
+            for v in vs:
+                seen.setdefault(v[0], []).append((i, wr, v[1], v[2], _mask(v)))
+        best = {}
+        for j in deps:
+            best[src[j]] = max(best.get(src[j], -1), j)
+        mine = []
+        for j in sorted(best.values(), reverse=True):
+            if know[q].get(src[j], -1) < j:
+                mine.append(j)
+                know[q][src[j]] = j
+                for k2, x in clock[j].items():
+                    know[q][k2] = max(know[q].get(k2, -1), x)
+        needed.update(mine)
+        waits.append(mine)
+        clock.append(dict(know[q]))
+    queue = {"V": g.vector, "S": g.scalar, "P": g.tensor, "G": g, "Y": g.sync}
+    count, value, waited = {q: 0 for q in "VSPG"}, {}, set()
+    for i, o in enumerate(ops):
+        q, sem = o[0], o[4]
+        for e in o[5]:
+            if (q, e) not in waited:
+                waited.add((q, e))
+                queue[q].wait_ge(T.sem[e[0]], e[1])
+        for j in waits[i]:
+            queue[q].wait_ge(T.sem[value[j][0]], value[j][1])
+        ins = o[1]()
+        if sem == "remote":
+            continue
+        if sem:
+            ins.then_inc(T.sem[sem], 16)
+            value[i] = (sem, 16)
+        elif i in needed:
+            count[q] += 1
+            ins.then_inc(T.sem["c" + q], 1)
+            value[i] = ("c" + q, count[q])
+    g.wait_ge(T.sem.sent, sent)
+    for o in ops:
+        if o[4] and o[4] != "remote":
+            g.wait_ge(T.sem[o[4]], 16)

@@ -10,10 +10,10 @@ for _k, _base in enumerate((CT_B, CT_C, CT_D)):
     for _t in range(4):
         SLOT[12 - 4 * _k - _t] = (_base, _t)
 ON_SCALAR = (15, 14)
-SUM_ON_VECTOR = (3, 2, 1)
-EO_A, EO_E, EO_O, EO_L, EO_N = 0, 128, 128 + K, 128 + 2 * K, 128 + 2 * C
-GATHER, SCATTER, S_FIX, PE_COL, LOAD, SLACK, TRIES = 1.56, 3.8, 60, 0.6, 2000, 100, 3000
-CASES = ((80, 3000, 1.0, 1.0), (60, 2000, 0.7, 0.8), (120, 4000, 1.3, 1.2))
+SUM_ON_VECTOR = (4, 3, 2, 1)
+EO_A, EO_E, EO_O, EO_L, EO_N = 0, 128, 128 + K, 128 + 2 * K, 384 + 2 * K
+GATHER, SCATTER, S_FIX, PE_COL, LOAD, SLACK, TRIES = 1.56, 3.8, 80, 0.6, 2400, 120, 5000
+CASES = ((120, 3200, 1.0, 1.0), (80, 2200, 0.8, 0.8), (180, 4500, 1.3, 1.2))
 BK = {"a": (0, 1, 2, 3), "e": (4, 5, 0, 1), "o": (2, 3, 4, 5), "se": (6, 7, 6, 7), "w": (0, 1, 2, 3), "d": (4, 5, 0, 1),
       "le": (2, 3, 4, 5), "lo": (0, 1, 2, 3), "sl": (4, 5, 6, 7)}
 
@@ -22,7 +22,7 @@ SCRATCH = {
     "xt": ("sbuf", [128, 4 * C], BF), "ut": ("sbuf", [128, 512], BF), "vt": ("sbuf", [128, 512], BF),
     "sh": ("sbuf", [128, 16 * C], BF), "tt": ("sbuf", [128, 4 * C], BF),
     "ct": ("sbuf", [128, 4 * CT_N], BF), "gs": ("sbuf", [128, 3 * C], BF), "junk": ("sbuf", [128, 2 * C], BF),
-    "ones": ("sbuf", [128, 528], BF),
+    "ones": ("sbuf", [128, 512], BF), "dj": ("sbuf", [128, 128], F32),
     "zf": ("sbuf", [128, 528], BF), "ze": ("sbuf", [128, 528], BF), "zo": ("sbuf", [128, 528], BF),
     "bd0": ("sbuf", [128, 512], BF), "bd": ("sbuf", [128, 512], BF),
     "pi": ("sbuf", [128, 1], I32), "pci": ("sbuf", [128, 8], I32), "pc": ("sbuf", [128, 16], F32),
@@ -34,7 +34,7 @@ SCRATCH = {
     "ul": ("sbuf", [128, 16], U16), "a2l": ("sbuf", [128, 16], U16), "pl": ("sbuf", [128, 128], U16),
     "r2": ("sbuf", [128, 2 * C], F32), "rr": ("sbuf", [128, C], F32), "inj": ("sbuf", [128, C], F32),
     "zs": ("sbuf", [128, C], F32), "uw": ("sbuf", [128, C], F32), "rs": ("sbuf", [128, 16], F32),
-    "rs2": ("sbuf", [128, 16], F32), "rkf": ("sbuf", [128, 16], F32), "rku": ("sbuf", [128, 16], U16),
+    "rku": ("sbuf", [128, 16], U16),
     "r2l": ("sbuf", [128, 16], U16), "vrow": ("sbuf", [128, 4 * C], F32), "lrow": ("sbuf", [128, C], F32),
     "u4": ("sbuf", [128, 2 * C], F32), "off": ("sbuf", [128, 64], U16), "off2": ("sbuf", [128, 64], U16),
     "orow": ("sbuf", [128, C], F32), "rel": ("sbuf", [128, 4 * M], F32), "yt": ("sbuf", [128, C], F32),
@@ -281,15 +281,17 @@ def rank_program(g, core, T, topo):
     def affine(out, a, scale, bias):
         act(out, a, ACT.Identity, bias=bias, scale=scale)
 
+    def either():
+        on_v, on_s = ops.pop(), ops.pop()
+        ops.append(on_v[:7] + (on_s,) + on_v[8:])
+
     def move(q, out, a):
-        if q == "F":
+        if q != "V":
             act(out, a, ACT.Copy)
-            other = ops.pop()
-            op("V", lambda: g.vector.tensor_copy(ap(out), ap(a)), [a], [out], other=other)
-        elif q == "V":
+        if q != "S":
             cp(out, a)
-        else:
-            act(out, a, ACT.Copy)
+        if q == "F":
+            either()
 
     def iota(out, pattern, base=0, cm=0):
         if SCRATCH[out[0]][2] == I32:
@@ -323,54 +325,58 @@ def rank_program(g, core, T, topo):
 
     def run32(a):
         return dict(p0=32 * a, p1=32 * a + 32)
-    P_L, P_E, P_L2, P_LH, P_LQ, P_L4, P_MK, P_EV, P_CJ, P_O4, P_OL, P_T0, P_T1, P_NQ, P_X = range(15)
+    P_L, P_E, P_LH, P_LQ, P_L4, P_MK, P_EV, P_CJ, P_O4, P_T0, P_T1, P_NQ, P_X, P_Y, P_R2 = range(15)
     FULL, EVEN, ODD = 0, 4, 8
 
+    first_loads = [V("xt"), V("ut")]
     dma("Y", "dx", lambda: T.xt[:], lambda: T.x[:], [], [V("xt")])
     dma("S", "du", lambda: T.ut[:], lambda: T.u[:], [], [V("ut")])
-    dma("Y", "dwc", lambda: T.q_w[:].bitcast(dt.uint8), lambda: T.wc[:], [], [V("q_w")])
-    dma("Y", "dws", lambda: T.s_w[:], lambda: T.ws[:], [], [V("s_w")])
-    dma("Y", "dv", lambda: T.vt[:], lambda: T.v[:], [], [V("vt")])
+    dma("Y", "dwc", lambda: T.q_w[:].bitcast(dt.uint8), lambda: T.wc[:], first_loads, [V("q_w")])
+    dma("Y", "dws", lambda: T.s_w[:], lambda: T.ws[:], first_loads, [V("s_w")])
+    dma("Y", "dv", lambda: T.vt[:], lambda: T.v[:], first_loads, [V("vt")])
 
     iota(V("pi"), [[0, 1]], 0, 1)
+    iota(V("dj"), [[1, 128]], 0, -1)
     iota(V("i16"), [[16, 16]])
     iota(V("j16"), [[0, 16], [1, 16]])
-    iota(V("ones"), [[0, 528]], 1)
-    keep(V("bd0"), V("ones", 0, 512), [[-16, 8], [0, 64]], ALU.is_ge, 0, 1)
+    iota(V("ones"), [[0, 512]], 1)
+    keep(V("bd0"), V("ones"), [[-16, 8], [0, 64]], ALU.is_ge, 0, 1)
     keep(V("bd"), V("bd0"), [[16, 8], [0, 64]], ALU.is_ge, 15, -1)
-    keep(V("zf"), V("ones"), [[1, 528]], ALU.is_equal, -3, -4)
     iota(V("i256"), [[1, C]])
     iota(V("j4"), [[0, 64], [1, 4]])
     iota(V("ia", 0, 80), [[0, 8], [8, 10]])
-    iota(V("ia", 80, 128), [[0, 4], [4, 12]], K // 2)
+    iota(V("ia", 80, 128), [[0, 8], [8, 6]], K // 2)
     iota(V("ia", 128, 148), [[K, 2], [16, 10]], EO_E)
-    iota(V("ia", 148, 160), [[8, 12]], EO_L)
-    fill(V("ct", 4 * (CT_A + 224), 4 * CT_B), 0.0)
+    iota(V("ia", 148, 160), [[128, 2], [16, 6]], EO_L + 32)
+    fill(V("zf"), 0.0)
+    fill(V("ct", 4 * (CT_A + 224), 4 * (CT_E + 16)), 0.0)
     fill(V("ct", 4 * (CT_B + 160), 4 * CT_C), 0.0)
     fill(V("ct", 4 * (CT_C + 96), 4 * CT_D), 0.0)
-    fill(V("ct", 4 * CT_D, 4 * CT_N), 0.0)
+    fill(V("ct", 4 * (CT_D + 32), 4 * (CT_D + 80)), 0.0)
     fill(V("rs", 0, 1), 0.0)
-    for k, (by, low) in enumerate(((0, 15), (4, 1), (0, 1), (1, 7), (2, 3), (0, 3))):
+    for k, (by, low) in enumerate(((0, 15), (4, 1), (1, 7), (2, 3), (0, 3))):
         ts(V("pci", k, k + 1), V("pi"), by, low, ALU.logical_shift_right, ALU.bitwise_and)
-    cp(col(P_L), V("pci", 0, 1))
-    cp(V("pc", 1, 6), V("pci", 1, 6))
+    cp(V("pc", 0, 2), V("pci", 0, 2))
+    cp(V("pc", 2, 5), V("pci", 2, 5))
     cp(V("ul"), V("i16"))
-    quant("ct", CT_E, "ct", 4 * CT_E, 128)
-    quant("land", 3 * M, "ct", 4 * CT_E, 128)
-    quant("ct", CT_D, "ct", 4 * CT_D, 128)
+    quant("ct", CT_E, "zf", 0, 128)
+    quant("land", 3 * M, "zf", 0, 128)
+    quant("ct", CT_D, "zf", 0, 128)
+    ts(V("zf", 3, 512, 4), V("dj"), 0.0, None, ALU.is_equal)
     ts(V("a2l"), V("i16"), 0.5, col(P_LH), ALU.mult, ALU.add)
     affine(col(P_MK), col(P_L), -BIG, 0.0)
-    affine(col(P_CJ), col(P_L), 512.0, -7681.0)
+    act(col(P_Y), col(P_L), ACT.Relu, bias=87040.0, scale=-6144.0)
+    affine(col(P_CJ), col(P_Y), -1.0, -1025.0)
+    affine(col(P_R2), col(P_E), 1.0, 2048.0)
     act(V("mk"), V("j16"), ACT.Abs, bias=col(P_MK), scale=BIG)
     act(V("d0"), V("j16"), ACT.Relu, bias=64 * BIG, scale=-64 * BIG)
-    act(V("tmp", 0, C), V("mk"), ACT.Sign)
+    act(V("tmp", 0, C), V("j16"), ACT.Sign, bias=col(P_MK), scale=BIG)
     affine(V("cj"), V("i16"), 1.0, col(P_CJ))
-    affine(V("w16"), V("tmp", 0, C), 16896.0, -16384.0)
+    affine(V("w16"), V("tmp", 0, C), 5120.0, 1024.0)
     affine(col(P_NQ), col(P_LQ), -1.0, 0.0)
     affine(col(P_EV), col(P_E), -1.0, 1.0)
     affine(col(P_X), col(P_L4), 1.0, -12288.0)
     affine(col(P_O4), col(P_LQ), 4096.0, col(P_X))
-    affine(col(P_OL), col(P_L2), float(M), col(P_LH))
     act(V("tmp", C, 2 * C), V("j4"), ACT.Sign, bias=col(P_NQ))
     act(V("tmp", 2 * C, 3 * C), V("tmp", C, 2 * C), ACT.Abs, scale=17408.0)
     affine(V("w4"), V("tmp", 2 * C, 3 * C), 1.0, -16384.0)
@@ -380,17 +386,16 @@ def rank_program(g, core, T, topo):
         for b in range(4):
             quant("e", (first + b) * 128, tile, 3 - b, 128)
     quant("bd", 0, "bd", 0, 128)
-    affine(V("plf", 0, 80), V("ia", 0, 80), 1.0, col(P_LH))
-    affine(V("plf", 80, 128), V("ia", 80, 128), 1.0, col(P_LQ))
+    affine(V("plf"), V("ia", 0, 128), 1.0, col(P_LH))
     for e in range(2):
         for a in range(4):
             c0 = 40 * e + 10 * a
             affine(V("plf", c0, c0 + 10, **run32(a)), V("ia", 128 + 10 * e, 138 + 10 * e, **run32(a)), 1.0, col(P_L, **run32(a)))
-    for a in range(4):
-        affine(V("plf", 80 + 12 * a, 92 + 12 * a, **run32(a)), V("ia", 148, 160, **run32(a)), 1.0, col(P_OL, **run32(a)))
+            c0 = 80 + 24 * e + 6 * a
+            affine(V("plf", c0, c0 + 6, **run32(a)), V("ia", 148 + 6 * e, 154 + 6 * e, **run32(a)), 1.0, col(P_L, **run32(a)))
     cp(V("pl"), V("plf"))
     affine(col(P_T0), col(P_E), float(K), float(EO_E))
-    affine(col(P_T1), col(P_E), float(M), float(EO_L - K))
+    affine(col(P_T1), col(P_E), 128.0, float(EO_L - 128))
     affine(V("tab", 0, K), V("i256", 0, K), 1.0, col(P_T0))
     affine(V("tab", K, C), V("i256", K, C), 1.0, col(P_T1))
     quant("u", 0, "ut", 0, 128)
@@ -437,14 +442,14 @@ def rank_program(g, core, T, topo):
         mm(0, "bd", 0, "ct", CT_B, 208, False, False)
         mm(0, "bd", 0, "ct", CT_C, 144, False, False)
         mm(0, "bd", 0, "ct", CT_D, 128, False, True)
-        tt(V("rs2"), V("cj"), V("rs"), ALU.subtract)
-        scan(V("uw"), V("w16"), bank(0, 0, C), ALU.add, ALU.max)
-        tt(V("rkf"), V("uw", 15, C, 16), V("rs2"), ALU.add)
-        cp(V("rku"), V("rkf"))
+        tt(V("w16", 15, C, 16), V("cj"), V("rs"), ALU.subtract)
+        scan(V("uw"), bank(0, 0, C), V("w16"), ALU.max, ALU.add, -1.0)
+        ts(V("rku"), V("uw", 15, C, 16), 1024.0, None, ALU.add)
 
-    def wrap4(row, n, off, u0):
-        scan(V("u4", u0, u0 + n), V("w4", 0, n), row, ALU.add, ALU.max)
-        ts(V(off, 0, n // 4), V("u4", u0 + 3, u0 + n, 4), 4.0, col(P_O4), ALU.mult, ALU.add)
+    def wrap4(row, n, off, u0, cut):
+        for c0, c1 in ((cut, n), (0, cut)):
+            scan(V("u4", u0 + c0, u0 + c1), V("w4", c0, c1), V(row[0], row[3] + c0, row[3] + c1), ALU.add, ALU.max)
+            ts(V(off, c0 // 4, c1 // 4), V("u4", u0 + c0 + 3, u0 + c1, 4), 4.0, col(P_O4), ALU.mult, ALU.add)
 
     def sh0(s):
         return 4 * C * s
@@ -476,6 +481,8 @@ def rank_program(g, core, T, topo):
             mm(BK["w"][b], "w", 128 * b, "land", l0, 128, ext=arrived)
         for b in range(4):
             act(V("rel", M * b, M * b + M), bank(BK["w"][b], 0, M), ACT.Relu, scale=0.03125)
+            ts(V("rel", M * b, M * b + M), bank(BK["w"][b], 0, M), 0.0, 0.03125, ALU.max, ALU.mult)
+            either()
         for b in range(4):
             bk = BK["d"][b] if t < R - 1 else 4 + b
             mm(bk, "e", (FULL + b) * 128, "land", l0, 128, ext=arrived)
@@ -488,7 +495,7 @@ def rank_program(g, core, T, topo):
         scatter(V("lrow"), V("rku"), V("i256") if s == 0 else vrow(s - 1))
         act(vrow(s), ind(V("tab" if s < R else "i256"), V("rku")), ACT.Copy)
         n_now = C if s == 0 else K
-        wrap4(V("lrow", 0, n_now), n_now, "off", 0)
+        wrap4(V("lrow", 0, n_now), n_now, "off", 0, 64 if s == R else K // 2)
         b, m, n, eo, y = ["%s%d" % (k, s) for k in ("b", "m", "n", "eo", "y")]
         if s == R:
             gather("V", s, win, 0, 64)
@@ -505,8 +512,8 @@ def rank_program(g, core, T, topo):
         else:
             gather("F", s, win, K, C)
 
-        def out(k, bk, c0, c1, first=0):
-            move("F", V(eo, 4 * c0 + k, 4 * c1, 4), bank(bk, first, first + c1 - c0))
+        def out(k, bk, c0, c1):
+            move("F", V(eo, 4 * c0 + k, 4 * c1, 4), bank(bk, 0, c1 - c0))
 
         def both(bk, k, kind, own, a0, w):
             mm(bk, "e", (kind + k) * 128, own, 0, w, True, False)
@@ -521,13 +528,14 @@ def rank_program(g, core, T, topo):
             for a in (2 * h, 2 * h + 1):
                 move("F", V("r2", e, 2 * K, 2, **run32(a)), bank(bk, K * (a % 2), K * (a % 2) + K, **run32(a)))
 
-        def late(a):
-            c0 = 8 * K + 2 * M * a
-            pick(y, c0, 2 * M, eo, EO_N, V("pl", 80 + 12 * a, 92 + 12 * a))
-            mm(BK["sl"][a], "us", 0, y, c0, 2 * M)
-            move("F", V("r2", 2 * K, 2 * C, **run32(a)), bank(BK["sl"][a], 0, 2 * M, **run32(a)))
+        def late(e, h):
+            c0, bk = 8 * K + 2 * M * (2 * e + h), BK["sl"][2 * e + h]
+            pick(y, c0, 2 * M, eo, EO_L + 128 * e + 128, V("pl", 80 + 24 * e + 12 * h, 92 + 24 * e + 12 * h))
+            mm(bk, "us", 0, y, c0, 2 * M)
+            for a in (2 * h, 2 * h + 1):
+                move("F", V("r2", 2 * K + e, 2 * C, 2, **run32(a)), bank(bk, M * (a % 2), M * (a % 2) + M, **run32(a)))
 
-        ts(V("r2l"), V("rkf"), 2.0, col(P_E), ALU.mult, ALU.add)
+        ts(V("r2l"), V("uw", 15, C, 16), 2.0, col(P_R2), ALU.mult, ALU.add)
         pick(m, 0, K, b, 128, V("a2l", 0, 10))
         pick(m, K, M, b, 128, V("a2l", 10, 16))
         for k, bk in enumerate(BK["a"]):
@@ -551,29 +559,32 @@ def rank_program(g, core, T, topo):
         quant(n, 0, "sh", sh0(s) + 4 * 128, 128)
         for k, bk in enumerate(BK["le"]):
             both(bk, k, EVEN, n, 128, 128)
-            out(k, bk, EO_L, EO_L + M, 32)
+            out(k, bk, EO_L, EO_L + 128)
         for k, bk in enumerate(BK["lo"]):
             both(bk, k, ODD, n, 128, 128)
-            out(k, bk, EO_L + M, EO_N, 32)
-        quant(eo, EO_L, eo, 4 * EO_L, 2 * M)
-        for a in range(4):
-            late(a)
+            out(k, bk, EO_L + 128, EO_N)
+        for e in range(2):
+            quant(eo, EO_L + 128 * e, eo, 4 * (EO_L + 128 * e), 128)
+        for e in range(2):
+            late(e, 0)
+            late(e, 1)
         ranks(False)
 
-    wrap4(vrow(R), C, "off2", C)
+    wrap4(vrow(R), C, "off2", C, 128)
     scatter(V("orow"), V("rku"), V("i256"))
     dma("Y", "dol", lambda: T.ol[:], lambda: T.orow[0:128:16, :], [V("orow")], [])
     h_tile(R - 1)
     last = V("sh", sh0(R), sh0(R) + 4 * C)
     move("V", V("tt", 0, 2 * C), ind(last, V("off2", 0, 32)))
     move("S", V("tt", 2 * C, 4 * C), ind(last, V("off2", 32, 64)))
-    quant("t", 0, "tt", 0, C)
+    for h in range(2):
+        quant("t", 128 * h, "tt", 2 * C * h, 128)
+        mm(2 + h, "v", 0, "t", 128 * h, 128)
+        move("F", V("yt", 128 * h, 128 * h + 128), bank(2 + h, 0, 128))
     dma("Y", "doc", lambda: T.oc[:], lambda: T.q_t[:].bitcast(dt.uint8), [V("q_t")], [])
-    mm(6, "v", 0, "t", 0, C)
 
     def store_scales(k, q):
         dma(q, "ds%d" % k, lambda: T.osc[4 * k:4 * k + 4, :], lambda: T.s_t[32 * k:32 * k + 4, :], [V("s_t")], [])
-    cp(V("yt"), bank(6, 0, C))
     store_scales(0, "S")
     store_scales(1, "S")
     store_scales(2, "S")

@@ -4,47 +4,62 @@ C, M, R = 256, 96, 3
 K = C - M
 F32, BF, U16, I32, X4, U8 = "float32", "bfloat16", "uint16", "int32", "float8_e4m3fn_x4", "uint8"
 BIG = 2.0 ** 90
-CT_A, CT_E, CT_B, CT_C, CT_D, CT_N = 0, 256, 384, 592, 736, 864
-SLOT = {"q": (CT_A, 0), 15: (CT_A, 1), 14: (CT_A, 2), 13: (CT_A, 3), 0: (CT_E, 0)}
-for _k, _base in enumerate((CT_B, CT_C, CT_D)):
-    for _t in range(4):
-        SLOT[12 - 4 * _k - _t] = (_base, _t)
-ON_SCALAR = (15, 14)
-SUM_ON_VECTOR = (4, 3, 2, 1)
-EO_A, EO_E, EO_O, EO_L, EO_N = 0, 128, 128 + K, 128 + 2 * K, 384 + 2 * K
-GATHER, SCATTER, S_FIX, PE_COL, LOAD, SLACK, TRIES = 1.56, 3.8, 80, 0.6, 2400, 120, 5000
-CASES = ((120, 3200, 1.0, 1.0), (80, 2200, 0.8, 0.8), (180, 4500, 1.3, 1.2))
-BK = {"a": (0, 1, 2, 3), "e": (4, 5, 0, 1), "o": (2, 3, 4, 5), "se": (6, 7, 6, 7), "w": (0, 1, 2, 3), "d": (4, 5, 0, 1),
-      "le": (2, 3, 4, 5), "lo": (0, 1, 2, 3), "sl": (4, 5, 6, 7)}
+SEGS = (("q", 11, 10, 9), (15, 14, 13, 12), (8, 7, 6, 5), (4, 3, 2, 1))
+SEG0, SLOT = [0], {}
+for _s in SEGS:
+    for _t, _j in enumerate(_s):
+        SLOT[_j] = (SEG0[-1], _t)
+    SEG0.append(SEG0[-1] + (C if "q" in _s else 16 * max(_s)))
+CT_N = SEG0[-1] + 64
+ON_SCALAR = (15, 14, 13, 12)
+SUM_ON_SCALAR = (3, 2, 1)
+RW = 96
+G_RUNS = 2
+G_TAKES = ((2, 2), (2, 2), (2, 2))
+EO_A, EO_E, EO_O, EO_L, EO_M, EO_N = 0, 128, 128 + K, 128 + 2 * K, 128 + 2 * K + M, 128 + 2 * C
+GT_L = EO_M - EO_O
+GT_N = GT_L + K
+GATHER, SCATTER, S_FIX, PE_COL, LOAD, SLACK = 1.56, 3.8, 80, 0.6, 2400, 120
+TRIES = 60000
+HEAT = 300
+CASES = ((190, 3200, 3000, 1.1, 1.0, 1.1), (130, 2400, 2000, 0.9, 0.85, 1.0), (240, 4200, 5000, 1.4, 1.2, 1.4))
+BANKS = 8
+
+PIECES = [(_a, _e, 0, K) for _e in range(2) for _a in range(G_RUNS - 1, -1, -1)]
+PIECES += [(_a, None, 0, K) for _a in range(G_RUNS, 4)] + [(_a, None, K, M) for _a in range(4)]
+PL, PL_N = {}, 0
+for _p in PIECES:
+    PL[_p] = PL_N
+    PL_N += _p[3] // (8 if _p[1] is None else 16)
 
 SCRATCH = {
     "ps": ("psum", [128, 4096], F32),
     "xt": ("sbuf", [128, 4 * C], BF), "ut": ("sbuf", [128, 512], BF), "vt": ("sbuf", [128, 512], BF),
-    "sh": ("sbuf", [128, 16 * C], BF), "tt": ("sbuf", [128, 4 * C], BF),
-    "ct": ("sbuf", [128, 4 * CT_N], BF), "gs": ("sbuf", [128, 3 * C], BF), "junk": ("sbuf", [128, 2 * C], BF),
-    "ones": ("sbuf", [128, 512], BF), "dj": ("sbuf", [128, 128], F32),
-    "zf": ("sbuf", [128, 528], BF), "ze": ("sbuf", [128, 528], BF), "zo": ("sbuf", [128, 528], BF),
-    "bd0": ("sbuf", [128, 512], BF), "bd": ("sbuf", [128, 512], BF),
-    "pi": ("sbuf", [128, 1], I32), "pci": ("sbuf", [128, 8], I32), "pc": ("sbuf", [128, 16], F32),
+    "sh": ("sbuf", [128, 16 * C + 128], BF), "tt": ("sbuf", [128, 4 * C], BF),
+    "gt": ("sbuf", [128, 4 * GT_N], BF), "gb": ("sbuf", [128, 512], BF),
+    "ct": ("sbuf", [128, 4 * CT_N], BF), "gs": ("sbuf", [128, 6 * C], BF), "junk": ("sbuf", [128, 4 * C], BF),
+    "ones": ("sbuf", [128, 512], BF), "ze": ("sbuf", [128, 1040], BF), "zf": ("sbuf", [128, 528], BF),
+    "bd0": ("sbuf", [128, 512], BF), "bd": ("sbuf", [128, 1024], BF),
+    "pi": ("sbuf", [128, 1], I32), "pci": ("sbuf", [128, 8], I32), "pc": ("sbuf", [128, 24], F32),
     "j16": ("sbuf", [128, C], F32), "j4": ("sbuf", [128, C], F32), "i256": ("sbuf", [128, C], F32),
-    "i16": ("sbuf", [128, 16], F32), "ia": ("sbuf", [128, 160], F32), "plf": ("sbuf", [128, 128], F32),
-    "tmp": ("sbuf", [128, 3 * C], F32), "mk": ("sbuf", [128, C], F32),
+    "i16": ("sbuf", [128, 24], F32), "ia": ("sbuf", [128, PL_N], F32), "plf": ("sbuf", [128, PL_N], F32),
+    "tmp": ("sbuf", [128, 3 * C], F32), "mk": ("sbuf", [128, C], F32), "qm": ("sbuf", [128, C], BF), "qs": ("sbuf", [128, C], BF),
     "d0": ("sbuf", [128, C], F32), "w16": ("sbuf", [128, C], F32), "w4": ("sbuf", [128, C], F32),
-    "tab": ("sbuf", [128, C], F32), "cj": ("sbuf", [128, 16], F32),
-    "ul": ("sbuf", [128, 16], U16), "a2l": ("sbuf", [128, 16], U16), "pl": ("sbuf", [128, 128], U16),
+    "tab": ("sbuf", [128, C], F32), "cj": ("sbuf", [128, 16], F32), "wa": ("sbuf", [128, 16], F32),
+    "ul": ("sbuf", [128, 16], U16), "a2l": ("sbuf", [128, 16], U16), "pl": ("sbuf", [128, PL_N], U16),
     "r2": ("sbuf", [128, 2 * C], F32), "rr": ("sbuf", [128, C], F32), "inj": ("sbuf", [128, C], F32),
-    "zs": ("sbuf", [128, C], F32), "uw": ("sbuf", [128, C], F32), "rs": ("sbuf", [128, 16], F32),
+    "zs": ("sbuf", [128, C], F32), "uw": ("sbuf", [128, C], F32), "rs": ("sbuf", [128, 16 * RW], F32),
     "rku": ("sbuf", [128, 16], U16),
     "r2l": ("sbuf", [128, 16], U16), "vrow": ("sbuf", [128, 4 * C], F32), "lrow": ("sbuf", [128, C], F32),
     "u4": ("sbuf", [128, 2 * C], F32), "off": ("sbuf", [128, 64], U16), "off2": ("sbuf", [128, 64], U16),
+    "ofs": ("sbuf", [128, R * M // 4], U16), "ofg": ("sbuf", [128, R * M // 4], U16),
     "orow": ("sbuf", [128, C], F32), "rel": ("sbuf", [128, 4 * M], F32), "yt": ("sbuf", [128, C], F32),
 }
-_PAIRS = {"x": C, "u": 128, "us": 128, "v": 128, "w": 512, "e": 12 * 128, "bd": 128, "ct": CT_N, "land": 3 * M + 128, "t": C}
-for _t in range(R + 1):
-    _PAIRS["b%d" % _t] = K
+_PAIRS = {"x": C, "u": 128, "us": 256, "v": 128, "w": 512, "e": 12 * 128, "bd": 256, "ct": CT_N, "land": 128, "t": C, "g": R * C + 128}
 for _t in range(R):
-    _PAIRS["m%d" % _t] = C
-    _PAIRS["n%d" % _t] = 128
+    _PAIRS["b%d" % _t] = K
+    _PAIRS["m%d" % _t] = K
+    _PAIRS["n%d" % _t] = 256 + M
     _PAIRS["eo%d" % _t] = EO_N
     _PAIRS["y%d" % _t] = 8 * C
     SCRATCH["eo%d" % _t] = ("sbuf", [128, 4 * EO_N], BF)
@@ -53,7 +68,7 @@ for _n, _w in _PAIRS.items():
     SCRATCH["s_" + _n] = ("sbuf", [128, _w], U8)
 
 DMAS = ["dx", "du", "dv", "dwc", "dws", "dy0", "dol", "doc", "ds0", "ds1", "ds2", "ds3"]
-SEMAPHORES = ["cV", "cS", "cP", "cG", "sent"] + DMAS + ["arr%d" % _t for _t in range(R)]
+SEMAPHORES = ["cV", "cS", "cP", "cG", "sent"] + DMAS + ["arr%s%d" % (_k, _t) for _t in range(R) for _k in "elo"]
 
 
 def V(buf, c0=0, c1=None, step=1, p0=0, p1=128):
@@ -75,18 +90,22 @@ def _mask(v):
     return m
 
 
+def _remote(o):
+    return bool(o[4]) and o[4].startswith("arr")
+
+
 _ORDER = []
 
 
 def arrange(ops):
     if not _ORDER:
         _ORDER.extend(search(ops))
-    return [ops[i] if k == 0 else ops[i][7] for i, k in _ORDER]
+    return [ops[i] if k == 0 else ops[i][7] for i, k in _ORDER[0]], _ORDER[1]
 
 
 def search(ops):
     n = len(ops)
-    seen, before, sends, own = {}, [], [], []
+    seen, before, sends, own = {}, [], {}, []
     for i, o in enumerate(ops):
         deps = {}
         for vs, wr in ((o[2], False), (o[3], True)):
@@ -95,24 +114,24 @@ def search(ops):
                 for (j, w2, p0, p1, m2) in seen.get(v[0], ()):
                     if (m2 & m) and (wr or w2) and p0 < v[2] and v[1] < p1:
                         both_pe = o[0] == "P" and ops[j][0] == "P"
-                        deps[j] = (0, 0, 0) if both_pe else (1, LOAD, 0) if ops[j][4] else (1, 60, 0) if ops[j][0] == "P" else (1, 0, 0)
+                        deps[j] = (0, 0, 0, 0) if both_pe else (1, LOAD, 0, 0) if ops[j][4] else (1, 60, 0, 0) if ops[j][0] == "P" else (1, 0, 0, 0)
         for vs, wr in ((o[2], False), (o[3], True)):
             for v in vs:
                 seen.setdefault(v[0], []).append((i, wr, v[1], v[2], _mask(v)))
         if o[0] == "G":
             if own:
-                deps.setdefault(own[-1], (0, 0, 0))
+                deps.setdefault(own[-1], (0, 0, 0, 0))
             own.append(i)
-        if o[4] == "remote":
-            sends.append(i)
-        if o[5]:
-            deps[sends[-1]] = (1, 0, 1)
+        if _remote(o):
+            sends[o[4]] = (i, 1 if o[4] == min(sends, key=lambda s: sends[s][0], default=o[4]) else 0)
+        for e in o[5]:
+            deps[sends[e[0]][0]] = (1, 0, 1, sends[e[0]][1])
         before.append(deps)
     reach = []
     for i, d in enumerate(before):
         r = 0
         for j in sorted(d, reverse=True):
-            if r >> j & 1 and d[j] == (1, 0, 0):
+            if r >> j & 1 and d[j] == (1, 0, 0, 0):
                 del d[j]
             r |= reach[j] | 1 << j
         reach.append(r)
@@ -121,11 +140,11 @@ def search(ops):
         for j in d:
             after[j].append(i)
     forms = [[o for o in (ops[i], ops[i][7]) if o is not None] for i in range(n)]
-    banks = [[_mask(v) for v in o[2] if v[0] == "ps"] for o in ops]
+    product = [max([v[3] // 512 for v in o[2] + o[3] if v[0] == "ps"] + [-1]) for o in ops]
     cases = []
-    for (wake, flight, pe, ga) in CASES:
-        lag = [[(j, w[0] * wake + w[1] + w[2] * flight) for j, w in d.items()] for d in before]
-        cost = [[o[6] * (pe if o[0] == "P" else 1.0) * (ga if o[8] else 1.0) for o in f] for f in forms]
+    for (wake, flight, once, pe, ga, gp) in CASES:
+        lag = [[(j, w[0] * wake + w[1] + w[2] * flight + w[3] * once) for j, w in d.items()] for d in before]
+        cost = [[o[6] * (pe if o[0] == "P" else gp if o[0] == "G" else 1.0) * (ga if o[8] else 1.0) for o in f] for f in forms]
         cases.append((wake, lag, cost))
     wake, lag, cost = cases[0]
     tail = [0.0] * n
@@ -134,70 +153,138 @@ def search(ops):
         for j, w in lag[i]:
             tail[j] = max(tail[j], w + tail[i])
 
-    def start(i, k, t, free, busy, wake):
-        q = forms[i][k][0]
-        t = max(t, free[q])
-        for m in banks[i]:
-            q2, t2 = busy.get(m, (q, 0.0))
-            if q2 != q:
-                t = max(t, t2 + wake)
-        return t
+    queue_of = [["VSPGY".index(o[0]) for o in f] for f in forms]
+    last = [LOAD if o[4] else 0 for o in ops]
+    uses = {}
+    for x in product:
+        uses[x] = uses.get(x, 0) + 1
 
-    def build(bias, pref):
+    def build():
         left = [len(d) for d in before]
         ready = {i: 0.0 for i in range(n) if not left[i]}
-        free, busy, end, order = {q: 0.0 for q in "VSPGY"}, {}, [0.0] * n, []
+        free, end, seq, form, open_ = [0.0] * 5, [0.0] * n, [], [0] * n, {}
         while ready:
-            cand = [(start(i, k, t0, free, busy, wake), i, k) for i, t0 in ready.items()
-                    for k in range(len(forms[i])) if pref[i] in (-1, k)]
+            cand = [(max(t0, free[q]), i, k) for i, t0 in ready.items() for k, q in enumerate(queue_of[i])
+                    if product[i] < 0 or product[i] in open_ or sum(1 for x in open_.values() if x) < BANKS - 1]
             first = min(cand)
-            q = forms[first[1]][first[2]][0]
-            t, i, k = max([c for c in cand if c[0] <= first[0] + SLACK and forms[c[1]][c[2]][0] == q],
-                          key=lambda c: tail[c[1]] + bias[c[1]])
+            q = queue_of[first[1]][first[2]]
+            t, i, k = max([c for c in cand if c[0] <= first[0] + SLACK and queue_of[c[1]][c[2]] == q], key=lambda c: tail[c[1]])
             end[i] = free[q] = t + cost[i][k]
-            for m in banks[i]:
-                busy[m] = (q, end[i])
-            order.append((i, k))
+            if product[i] >= 0:
+                open_[product[i]] = open_.get(product[i], uses[product[i]]) - 1
+            seq.append(i)
+            form[i] = k
             del ready[i]
             for j in after[i]:
                 left[j] -= 1
                 if not left[j]:
                     ready[j] = max(end[x] + w for x, w in lag[j])
-        return order
+        return seq, form
 
-    def length(order):
-        total = 0.0
-        for wake_, lag_, cost_ in cases:
-            free, busy, end = {q: 0.0 for q in "VSPGY"}, {}, [0.0] * n
-            for i, k in order:
-                q = forms[i][k][0]
-                t = start(i, k, max([end[x] + w for x, w in lag_[i]] + [0.0]), free, busy, wake_)
-                end[i] = free[q] = t + cost_[i][k]
-                for m in banks[i]:
-                    busy[m] = (q, end[i])
-            total += max(end[i] + (LOAD if ops[i][4] else 0) for i in range(n))
-        return total
+    def place(seq):
+        idle, at, left, user, behind = list(range(BANKS)), {}, {}, [-1] * BANKS, {}
+        for i in seq:
+            x = product[i]
+            if x >= 0:
+                if x not in at:
+                    if not idle:
+                        return None, None
+                    at[x], left[x] = idle.pop(0), uses[x]
+                behind[i], user[at[x]] = user[at[x]], i
+                left[x] -= 1
+                if not left[x]:
+                    idle.append(at[x])
+        return at, behind
     seed = [12345]
 
     def rnd(m):
         seed[0] = (seed[0] * 1103515245 + 12345) % 2147483648
         return (seed[0] >> 8) % m
-    bias, pref = [0.0] * n, [-1] * n
-    order = build(bias, pref)
-    best = length(order)
-    for _ in range(TRIES):
-        b2, p2 = list(bias), list(pref)
-        at = rnd(n)
-        for _k in range(1 + rnd(6)):
-            i = order[min(n - 1, at + rnd(40))][0]
-            b2[i] = float(rnd(2001) - 1000)
-            if len(forms[i]) > 1:
-                p2[i] = rnd(3) - 1
-        o2 = build(b2, p2)
-        l2 = length(o2)
-        if l2 <= best:
-            bias, pref, order, best = b2, p2, o2, l2
-    return order
+    seq, form = build()
+    narrow = [i for i, o in enumerate(ops) if o[3] and o[3][0][0] == "lrow"]
+
+    def run(seq, form, at, known, stop=n):
+        total, res, behind = 0.0, [], place(seq)[1]
+        if behind is None:
+            return 1e9, None
+        who = [-1] * 5
+        for p in range(at - 1, -1, -1):
+            q = queue_of[seq[p]][form[seq[p]]]
+            if who[q] < 0:
+                who[q] = seq[p]
+                if min(who) >= 0:
+                    break
+        steps = [(i, form[i], queue_of[i][form[i]], behind.get(i, -1)) for i in seq[at:stop]]
+        steps = [(i, k, q, b if b >= 0 and queue_of[b][form[b]] != q else -1) for i, k, q, b in steps]
+        for c, (wake_, lag_, cost_) in enumerate(cases):
+            end, why = (list(known[c][0]), list(known[c][1])) if known else ([0.0] * n, [-1] * n)
+            by = list(who)
+            free = [end[x] if x >= 0 else 0.0 for x in who]
+            for i, k, q, b in steps:
+                t, w = free[q], -2 - by[q]
+                for j, x in lag_[i]:
+                    if end[j] + x >= t:
+                        t, w = end[j] + x, j
+                if b >= 0 and end[b] + wake_ > t:
+                    t, w = end[b] + wake_, -2 - b
+                end[i] = free[q] = t + cost_[i][k]
+                why[i], by[q] = w, i
+            total += max([e + x for e, x in zip(end, last)]) if stop == n else end[i] - known[c][0][i]
+            res.append((end, why))
+        return total, res
+
+    def chains(seq, known):
+        out = []
+        for end, why in known:
+            i, held = max(range(n), key=lambda x: end[x] + last[x]), []
+            while i != -1:
+                w = why[i]
+                if w <= -2:
+                    w = -2 - w
+                    held.append((w, i))
+                i = w
+            out.append(held)
+        return out, {x: p for p, x in enumerate(seq)}
+    now, known = run(seq, form, 0, None)
+    best = (now, seq, form)
+    held, where = chains(seq, known)
+    for trial in range(TRIES):
+        some = held[rnd(len(cases))]
+        j, i = some[rnd(len(some))]
+        s2, f2, kind, to = seq, form, rnd(10), where[i] + 1
+        if kind < 3:
+            x = (i, j)[rnd(2)]
+            if len(forms[x]) < 2:
+                continue
+            f2 = list(form)
+            f2[x] = 1 - f2[x]
+            at = where[x]
+        elif kind < 7:
+            at = max(0, where[j] - (rnd(12) if rnd(2) else 0))
+            part = seq[at:where[i] + 1]
+            up = [x for x in part if x == i or reach[i] >> x & 1]
+            if j in up:
+                continue
+            s2 = seq[:at] + up + [x for x in part if x not in up] + seq[where[i] + 1:]
+        else:
+            at, to = where[j], min(n, where[i] + 1 + (rnd(30) if rnd(2) else 0))
+            part = seq[at:to]
+            down = [x for x in part if x == j or reach[x] >> j & 1]
+            if i in down:
+                continue
+            s2 = seq[:at] + [x for x in part if x not in down] + down + seq[to:]
+        room = HEAT * (1 - trial / TRIES) * rnd(1000) / 1000
+        stop = [where[x] + 1 for x in narrow if where[x] >= to]
+        if stop and run(s2, f2, at, known, stop[0])[0] > room:
+            continue
+        t2, k2 = run(s2, f2, at, known)
+        if t2 <= now + room:
+            now, seq, form, known = t2, s2, f2, k2
+            held, where = chains(seq, known)
+            if now < best[0]:
+                best = (now, seq, form)
+    order = [(i, best[2][i]) for i in best[1]]
+    return order, place(best[1])[0]
 
 
 def rank_program(g, core, T, topo):
@@ -206,10 +293,19 @@ def rank_program(g, core, T, topo):
         return
     n_ranks = len(T.cores)
     ops = []
+    arriving = [()]
+    banks, products = {}, [0]
+
+    def new(k=None):
+        products[0] += k or 1
+        return products[0] - 1 if k is None else range(products[0] - k, products[0])
 
     def ap(v):
         if not isinstance(v, tuple):
             return v
+        if v[0] == "ps":
+            by = 512 * (banks[v[3] // 512] - v[3] // 512)
+            return T.ps[v[1]:v[2], v[3] + by:v[4] + by]
         if v[0] == "ind":
             return ap(v[1]).indirect(ap(v[2]))
         if v[0] == "ind32":
@@ -229,15 +325,15 @@ def rank_program(g, core, T, topo):
             return 60 + GATHER * 16 * (a[2][4] - a[2][3])
         n = len(range(a[3], a[4], a[5]))
         if q == "V":
-            if SCRATCH[a[0]][2] == BF and SCRATCH[writes[0][0]][2] == BF:
+            if all(SCRATCH[v[0]][2] == BF for v in parts(reads)[:2] + [writes[0]] if v[4] - v[3] > 1):
                 rate *= 0.5
             return max(64, n * rate)
         return (S_FIX + n) if q == "S" else 150 + 2 * n
 
-    def op(q, emit, reads, writes, dma=None, ext=(), cost=None, other=None):
+    def op(q, emit, reads, writes, dma=None, cost=None, other=None):
         if cost is None:
             cost = span(q, reads, writes)
-        ops.append((q, emit, parts(reads), parts(writes), dma, ext, cost, other, bool(reads) and reads[0][0] in ("ind", "ind32")))
+        ops.append((q, emit, parts(reads), parts(writes), dma, arriving[0], cost, other, bool(reads) and reads[0][0] in ("ind", "ind32")))
 
     def ind(win, off):
         return ("ind", win, off)
@@ -250,7 +346,7 @@ def rank_program(g, core, T, topo):
 
     def tt(out, a, b, o):
         op("V", lambda: g.vector.tensor_tensor(ap(out), ap(a), ap(b), o), [a, b], [out],
-           cost=span("V", [b], [out], 1.0 if a[0] == "ps" else 2.0))
+           cost=span("V", [a], [out]) if a[0] == "ind" else span("V", [b], [out], 1.0 if a[0] == "ps" else 2.0))
 
     def cp(out, a):
         op("V", lambda: g.vector.tensor_copy(ap(out), ap(a)), [a], [out])
@@ -283,7 +379,7 @@ def rank_program(g, core, T, topo):
 
     def either():
         on_v, on_s = ops.pop(), ops.pop()
-        ops.append(on_v[:7] + (on_s,) + on_v[8:])
+        ops.append(on_v[:2] + (on_s[2],) + on_v[3:7] + (on_s,) + on_v[8:])
 
     def move(q, out, a):
         if q != "V":
@@ -300,15 +396,18 @@ def rank_program(g, core, T, topo):
             op("G", lambda: g.iota(ap(out), pattern, base, cm, allow_small_or_imprecise_dtypes=True), [], [out])
 
     def keep(out, a, pattern, cmp_, base, cm):
-        op("G", lambda: g.affine_select(ap(out), ap(a), pattern, cmp_, 0.0, base, cm), [a], [out])
+        op("G", lambda: g.affine_select(ap(out), ap(a), pattern, cmp_, 0.0, base, cm), [a], [out], cost=200 + 2 * (a[4] - a[3]))
+
+    def spread(out, a):
+        op("G", lambda: g.partition_broadcast(ap(out), ap(a), out[2]), [a], [out], cost=170 + 4 * (a[4] - a[3]))
 
     def quant(name, c0, tile, e0, n):
         qv, sv, tv = V("q_" + name, c0, c0 + n), V("s_" + name, c0, c0 + n), V(tile, e0, e0 + 4 * n)
         op("V", lambda: g.vector.quantize_mx(ap(qv), ap(sv), ap(tv)), [tv], [qv, sv], cost=15 + 1.06 * n)
 
-    def mm(b, w, w0, x, x0, n, start=True, stop=True, ext=()):
+    def mm(b, w, w0, x, x0, n, start=True, stop=True):
         o, a = bank(b, 0, n), [V("q_" + w, w0, w0 + 128), V("s_" + w, w0, w0 + 128), V("q_" + x, x0, x0 + n), V("s_" + x, x0, x0 + n)]
-        op("P", lambda: g.tensor.matmul_mx(ap(o), ap(a[0]), ap(a[1]), ap(a[2]), ap(a[3]), start, stop), a, [o], ext=ext,
+        op("P", lambda: g.tensor.matmul_mx(ap(o), ap(a[0]), ap(a[1]), ap(a[2]), ap(a[3]), start, stop), a, [o],
            cost=PE_COL * (n + 16))
 
     def pick(dst, d0, n, src, w1, off):
@@ -325,8 +424,19 @@ def rank_program(g, core, T, topo):
 
     def run32(a):
         return dict(p0=32 * a, p1=32 * a + 32)
-    P_L, P_E, P_LH, P_LQ, P_L4, P_MK, P_EV, P_CJ, P_O4, P_T0, P_T1, P_NQ, P_X, P_Y, P_R2 = range(15)
-    FULL, EVEN, ODD = 0, 4, 8
+    (P_L, P_E, P_LH, P_LQ, P_L4, P_L1, P_MK, P_CJ, P_O4, P_T, P_T0, P_T1, P_NQ, P_X, P_Y, P_R2, P_OS, P_Z,
+     P_I1, P_I2) = range(20)
+
+    def unpack(bk, k, ev, e0, od, o0, w):
+        if (ev, e0) == (od, o0):
+            return mm(bk, "e", (8 + k) * 128, ev, e0, w)
+        mm(bk, "e", 2 * k * 128, ev, e0, w, True, False)
+        mm(bk, "e", (2 * k + 1) * 128, od, o0, w, False, True)
+
+    def zero(out):
+        act(out, V("ones", 0, out[4] - out[3]), ACT.Identity, scale=0.0)
+        fill(out, 0.0)
+        either()
 
     first_loads = [V("xt"), V("ut")]
     dma("Y", "dx", lambda: T.xt[:], lambda: T.x[:], [], [V("xt")])
@@ -335,124 +445,154 @@ def rank_program(g, core, T, topo):
     dma("Y", "dws", lambda: T.s_w[:], lambda: T.ws[:], first_loads, [V("s_w")])
     dma("Y", "dv", lambda: T.vt[:], lambda: T.v[:], first_loads, [V("vt")])
 
-    iota(V("pi"), [[0, 1]], 0, 1)
-    iota(V("dj"), [[1, 128]], 0, -1)
-    iota(V("i16"), [[16, 16]])
-    iota(V("j16"), [[0, 16], [1, 16]])
-    iota(V("ones"), [[0, 512]], 1)
-    keep(V("bd0"), V("ones"), [[-16, 8], [0, 64]], ALU.is_ge, 0, 1)
-    keep(V("bd"), V("bd0"), [[16, 8], [0, 64]], ALU.is_ge, 15, -1)
-    iota(V("i256"), [[1, C]])
-    iota(V("j4"), [[0, 64], [1, 4]])
-    iota(V("ia", 0, 80), [[0, 8], [8, 10]])
-    iota(V("ia", 80, 128), [[0, 8], [8, 6]], K // 2)
-    iota(V("ia", 128, 148), [[K, 2], [16, 10]], EO_E)
-    iota(V("ia", 148, 160), [[128, 2], [16, 6]], EO_L + 32)
+    fill(V("ze"), 0.0)
+    fill(V("ones", 0, 128), 1.0)
+    fill(V("ones", 128, 512), 1.0)
     fill(V("zf"), 0.0)
-    fill(V("ct", 4 * (CT_A + 224), 4 * (CT_E + 16)), 0.0)
-    fill(V("ct", 4 * (CT_B + 160), 4 * CT_C), 0.0)
-    fill(V("ct", 4 * (CT_C + 96), 4 * CT_D), 0.0)
-    fill(V("ct", 4 * (CT_D + 32), 4 * (CT_D + 80)), 0.0)
-    fill(V("rs", 0, 1), 0.0)
-    for k, (by, low) in enumerate(((0, 15), (4, 1), (1, 7), (2, 3), (0, 3))):
+    quant("g", R * C, "zf", 0, 128)
+    iota(V("pi"), [[0, 1]], 0, 1)
+    iota(V("i16", 0, 16), [[16, 16]])
+    keep(V("ze", 3, 512, 4), V("ones", 0, 128), [[32, 4], [1016, 2], [1, 16]], ALU.is_equal, 0, -1)
+    keep(V("ze", 515, 1024, 4), V("ones", 0, 128), [[32, 4], [-984, 2], [1, 16]], ALU.is_equal, 1000, -1)
+    iota(V("j16"), [[0, 16], [1, 16]])
+    keep(V("bd0"), V("ones"), [[-16, 8], [0, 64]], ALU.is_ge, 0, 1)
+    keep(V("bd", 0, 512), V("bd0"), [[16, 8], [0, 64]], ALU.is_ge, 15, -1)
+    iota(V("i256"), [[1, C]])
+    keep(V("zf", 3, 512, 4), V("ones", 0, 128), [[1, 128]], ALU.is_equal, 0, -1)
+    iota(V("j4"), [[0, 64], [1, 4]])
+    iota(V("i16", 16, 24), [[32, 4], [0, 2]], 16)
+    kinds = []
+    for p in PIECES:
+        if kinds and kinds[-1][0] == (p[1] is None,) + p[2:]:
+            kinds[-1][2] += 1
+        else:
+            kinds.append([(p[1] is None,) + p[2:], PL[p], 1])
+    for (mixed, i0, n), c0, reps in kinds:
+        w = n // (8 if mixed else 16)
+        iota(V("ia", c0, c0 + w * reps), [[0, reps], [4 if mixed else 8, w]], i0 // 2)
+    for k, seg in enumerate(SEGS):
+        low = 16 * min(j for j in seg if j != "q")
+        zero(V("ct", 4 * (SEG0[k] + low), 4 * (SEG0[k + 1] if k + 1 < len(SEGS) else CT_N)))
+    zero(V("rs", RW - 1, RW))
+    zero(V("gb", 4 * M, 512))
+    zero(V("gt", 4 * K, 4 * GT_L))
+    move("F", V("bd", 512, 1024), V("bd", 0, 512))
+    affine(V("bd", 512, 1024, 4), V("bd", 0, 512, 4), -1.0, 0.0)
+    ts(V("bd", 512, 1024, 4), V("bd", 0, 512, 4), -1.0, None, ALU.mult)
+    either()
+    for k, (by, low) in enumerate(((0, 15), (4, 1), (1, 7), (2, 3), (0, 3), (0, 1))):
         ts(V("pci", k, k + 1), V("pi"), by, low, ALU.logical_shift_right, ALU.bitwise_and)
     cp(V("pc", 0, 2), V("pci", 0, 2))
-    cp(V("pc", 2, 5), V("pci", 2, 5))
-    cp(V("ul"), V("i16"))
-    quant("ct", CT_E, "zf", 0, 128)
-    quant("land", 3 * M, "zf", 0, 128)
-    quant("ct", CT_D, "zf", 0, 128)
-    ts(V("zf", 3, 512, 4), V("dj"), 0.0, None, ALU.is_equal)
-    ts(V("a2l"), V("i16"), 0.5, col(P_LH), ALU.mult, ALU.add)
+    cp(V("pc", 2, 6), V("pci", 2, 6))
+    cp(V("ul", 0, 8), V("i16", 0, 8))
+    cp(V("ul", 8, 16), V("i16", 16, 24))
+    ts(V("a2l"), V("i16", 0, 16), 0.5, col(P_LH), ALU.mult, ALU.add)
     affine(col(P_MK), col(P_L), -BIG, 0.0)
     act(col(P_Y), col(P_L), ACT.Relu, bias=87040.0, scale=-6144.0)
-    affine(col(P_CJ), col(P_Y), -1.0, -1025.0)
+    affine(col(P_Z), col(P_L), 1.0, -1024.0)
+    affine(col(P_CJ), col(P_Y), -1.0, col(P_Z))
     affine(col(P_R2), col(P_E), 1.0, 2048.0)
     act(V("mk"), V("j16"), ACT.Abs, bias=col(P_MK), scale=BIG)
     act(V("d0"), V("j16"), ACT.Relu, bias=64 * BIG, scale=-64 * BIG)
+    act(V("qm"), V("j16"), ACT.Sign)
     act(V("tmp", 0, C), V("j16"), ACT.Sign, bias=col(P_MK), scale=BIG)
-    affine(V("cj"), V("i16"), 1.0, col(P_CJ))
+    affine(V("cj"), V("i16", 0, 16), 1.0, col(P_CJ))
     affine(V("w16"), V("tmp", 0, C), 5120.0, 1024.0)
     affine(col(P_NQ), col(P_LQ), -1.0, 0.0)
-    affine(col(P_EV), col(P_E), -1.0, 1.0)
     affine(col(P_X), col(P_L4), 1.0, -12288.0)
     affine(col(P_O4), col(P_LQ), 4096.0, col(P_X))
     act(V("tmp", C, 2 * C), V("j4"), ACT.Sign, bias=col(P_NQ))
     act(V("tmp", 2 * C, 3 * C), V("tmp", C, 2 * C), ACT.Abs, scale=17408.0)
     affine(V("w4"), V("tmp", 2 * C, 3 * C), 1.0, -16384.0)
-    act(V("ze"), V("zf"), ACT.Identity, scale=col(P_EV))
-    act(V("zo"), V("zf"), ACT.Identity, scale=col(P_E))
-    for first, tile in ((FULL, "zf"), (EVEN, "ze"), (ODD, "zo")):
-        for b in range(4):
-            quant("e", (first + b) * 128, tile, 3 - b, 128)
+    for b in range(4):
+        quant("e", 2 * b * 128, "ze", 3 - b, 256)
+        quant("e", (8 + b) * 128, "zf", 3 - b, 128)
     quant("bd", 0, "bd", 0, 128)
-    affine(V("plf"), V("ia", 0, 128), 1.0, col(P_LH))
-    for e in range(2):
-        for a in range(4):
-            c0 = 40 * e + 10 * a
-            affine(V("plf", c0, c0 + 10, **run32(a)), V("ia", 128 + 10 * e, 138 + 10 * e, **run32(a)), 1.0, col(P_L, **run32(a)))
-            c0 = 80 + 24 * e + 6 * a
-            affine(V("plf", c0, c0 + 6, **run32(a)), V("ia", 148 + 6 * e, 154 + 6 * e, **run32(a)), 1.0, col(P_L, **run32(a)))
-    cp(V("pl"), V("plf"))
+    quant("bd", 128, "bd", 512, 128)
+    single = sum(p[3] // 16 for p in PIECES if p[1] is not None)
+    if single:
+        affine(V("plf", 0, single), V("ia", 0, single), 1.0, col(P_LH))
+    affine(V("plf", single, PL_N), V("ia", single, PL_N), 1.0, col(P_LQ))
+    for k, w in ((P_I1, K), (P_I2, M)):
+        affine(col(k), col(P_L1), float(w), col(P_LH))
+    for p in PIECES:
+        a, e, i0, n = p
+        if e is None:
+            c0 = EO_L if i0 else EO_E
+            affine(V("plf", PL[p], PL[p] + n // 8, **run32(a)), V("i256", c0 // 8, (c0 + n) // 8, **run32(a)), 8.0,
+                   col(P_I2 if i0 else P_I1, **run32(a)))
+        else:
+            c0 = (EO_E, EO_O)[e]
+            affine(V("plf", PL[p], PL[p] + n // 16, **run32(a)), V("i256", c0 // 16, (c0 + n) // 16, **run32(a)), 16.0, col(P_L, **run32(a)))
+    if single:
+        cp(V("pl", 0, single), V("plf", 0, single))
+    cp(V("pl", single, PL_N), V("plf", single, PL_N))
     affine(col(P_T0), col(P_E), float(K), float(EO_E))
-    affine(col(P_T1), col(P_E), 128.0, float(EO_L - 128))
+    affine(col(P_T1), col(P_E), float(M), float(EO_L - K))
+    affine(col(P_OS), col(P_T0), -4.0, col(P_O4))
     affine(V("tab", 0, K), V("i256", 0, K), 1.0, col(P_T0))
     affine(V("tab", K, C), V("i256", K, C), 1.0, col(P_T1))
     quant("u", 0, "ut", 0, 128)
     pick("us", 0, 128, "u", 128, V("ul", 0, 8))
+    if G_RUNS:
+        pick("us", 128, 128, "u", 128, V("ul", 8, 16))
     quant("x", 0, "xt", 0, C)
     quant("v", 0, "vt", 0, 128)
-    mm(6, "us", 0, "x", 0, C)
-    mm(7, "us", 0, "x", 0, C)
+    for_v, for_s = new(2)
+    mm(for_v, "us", 0, "x", 0, C)
+    mm(for_s, "us", 0, "x", 0, C)
 
-    def slot(j, c0, c1):
+    def slot(j, c0, c1, step=1):
         base, t = SLOT[j]
-        return V("ct", 4 * (base + c0) + t, 4 * (base + c1), 4)
+        return V("ct", 4 * (base + c0) + t, 4 * (base + c1), 4 * step)
 
     def key(j):
         return V("zs", 16 * j + 15, 16 * j + 16)
 
     def ranks(first):
+        def row(q, c0, c1):
+            return bank(for_v if q == "V" else for_s, c0, c1) if first else V("rr", c0, c1)
+
+        def scores(c0, c1):
+            return bank(for_v, c0, c1) if first else ind(V("r2"), V("r2l", c0 // 16, c1 // 16))
         for c0, c1 in ((128, C), (0, 128)):
-            if first:
-                tt(V("inj", c0, c1), bank(6, c0, c1), V("mk", c0, c1), ALU.add)
-            else:
-                tt(V("inj", c0, c1), ind(V("r2"), V("r2l", c0 // 16, c1 // 16)), V("mk", c0, c1), ALU.add)
+            tt(V("inj", c0, c1), scores(c0, c1), V("mk", c0, c1), ALU.add)
             scan(V("zs", c0, c1), V("d0", c0, c1), V("inj", c0, c1), ALU.add, ALU.min)
-        act(V("rr"), bank(7, 0, C) if first else ind(V("r2"), V("r2l")), ACT.Copy)
-        for j in range(15, -1, -1):
-            n = 16 * j
-            c0 = 0
+        if not first:
+            act(V("rr"), scores(0, C), ACT.Copy)
+        tt(slot("q", 0, C), scores(0, C), V("zs"), ALU.is_gt)
+        scan(V("qs"), V("qm"), slot("q", 0, C), ALU.mult, ALU.add)
+        tt(V("wa"), V("cj"), V("qs", 15, C, 16), ALU.add)
+        for j in range(15, 0, -1):
+            n, total = 16 * j, V("rs", RW * j + RW - 1, RW * j + RW)
             if j in ON_SCALAR:
                 i = ON_SCALAR.index(j)
-                act(V("gs", i * C, i * C + n), V("rr", 0, n), ACT.Sign, bias=key(j), scale=-1.0)
-                act(slot(j, 0, n), V("gs", i * C, i * C + n), ACT.Relu, acc=V("rs", j, j + 1))
-                c0 = n
-            ts(slot(j, c0, n + 16), V("rr", c0, n + 16), key(j), None, ALU.is_lt)
-            if j in SUM_ON_VECTOR:
-                reduce_add(V("rs", j, j + 1), slot(j, 0, n))
-            elif c0 == 0 and j:
-                act(V("junk", C * (j % 2), C * (j % 2) + n), slot(j, 0, n), ACT.Copy, acc=V("rs", j, j + 1))
-        tt(slot("q", 0, C), V("rr"), V("zs"), ALU.is_equal)
-        quant("ct", CT_A, "ct", 4 * CT_A, 272)
-        quant("ct", CT_B, "ct", 4 * CT_B, 208)
-        quant("ct", CT_C, "ct", 4 * CT_C, 224)
-        mm(0, "bd", 0, "ct", CT_A, 256, True, False)
-        mm(0, "bd", 0, "ct", CT_E, 128, False, False)
-        mm(0, "bd", 0, "ct", CT_B, 208, False, False)
-        mm(0, "bd", 0, "ct", CT_C, 144, False, False)
-        mm(0, "bd", 0, "ct", CT_D, 128, False, True)
-        tt(V("w16", 15, C, 16), V("cj"), V("rs"), ALU.subtract)
-        scan(V("uw"), bank(0, 0, C), V("w16"), ALU.max, ALU.add, -1.0)
+                act(V("gs", i * C, i * C + n), row("S", 0, n), ACT.Sign, bias=key(j), scale=-1.0)
+                act(slot(j, 0, n), V("gs", i * C, i * C + n), ACT.Relu, acc=total)
+                continue
+            ts(slot(j, 0, n), row("V", 0, n), key(j), None, ALU.is_lt)
+            if j in SUM_ON_SCALAR:
+                act(V("junk", C * (j % 4), C * (j % 4) + n), slot(j, 0, n), ACT.Copy, acc=total)
+            elif j <= 4:
+                reduce_add(total, slot(j, 0, n))
+            else:
+                scan(V("rs", RW * j + RW - n // 2, RW * j + RW), slot(j, 0, n, 2), slot(j, 1, n, 2), ALU.add, ALU.add)
+        quant("ct", SEG0[0], "ct", 4 * SEG0[0], SEG0[1] - SEG0[0])
+        quant("ct", SEG0[2], "ct", 4 * SEG0[2], (CT_N if first else SEG0[4]) - SEG0[2])
+        quant("ct", SEG0[1], "ct", 4 * SEG0[1], SEG0[2] - SEG0[1])
+        counts = new()
+        for k in (0, 2, 3, 1):
+            mm(counts, "bd", 128 if k == 0 else 0, "ct", SEG0[k], max(128, SEG0[k + 1] - SEG0[k]), k == 0, k == 1)
+        tt(V("w16", 15, C, 16), V("wa"), V("rs", RW - 1, 16 * RW, RW), ALU.subtract)
+        scan(V("uw"), bank(counts, 0, C), V("w16"), ALU.max, ALU.add, -1024.0)
         ts(V("rku"), V("uw", 15, C, 16), 1024.0, None, ALU.add)
 
-    def wrap4(row, n, off, u0, cut):
-        for c0, c1 in ((cut, n), (0, cut)):
-            scan(V("u4", u0 + c0, u0 + c1), V("w4", c0, c1), V(row[0], row[3] + c0, row[3] + c1), ALU.add, ALU.max)
-            ts(V(off, c0 // 4, c1 // 4), V("u4", u0 + c0 + 3, u0 + c1, 4), 4.0, col(P_O4), ALU.mult, ALU.add)
+    def wrap4(row, off, u0, c0, c1):
+        scan(V("u4", u0 + c0, u0 + c1), V("w4", c0, c1), V(row[0], row[3] + c0, row[3] + c1), ALU.add, ALU.max)
+        ts(V(off, c0 // 4, c1 // 4), V("u4", u0 + c0 + 3, u0 + c1, 4), 4.0, col(P_O4), ALU.mult, ALU.add)
 
     def sh0(s):
-        return 4 * C * s
+        return 4 * C * (R - s)
 
     def vrow(s):
         return V("vrow", C * s, C * s + C)
@@ -460,117 +600,123 @@ def rank_program(g, core, T, topo):
     def gather(q, s, win, c0, c1):
         move(q, V("sh", sh0(s) + 4 * c0, sh0(s) + 4 * c1), ind(win, V("off", c0 // 4, c1 // 4)))
 
-    def send(t):
+    sent = [0]
+
+    def send(t, sem, pairs):
         dst = T.cores[(rank + 1 + t) % n_ranks]
         rid, pid = topo.addr(dst)[:2]
         mask = topo.mask(core, dst)
-        l0 = (R - 1 - t) * M
-        b = "b%d" % (t + 1)
-        op("G", lambda: g.remote_dma(T.q_land[:, l0:l0 + M].bitcast(dt.uint8), T["q_" + b][:, 0:M].bitcast(dt.uint8),
-                                     T.sem["arr%d" % t], T.sem.sent, pid, rid, mask), [V("q_" + b)], [], dma="remote", cost=300)
-        op("G", lambda: g.remote_dma(T.s_land[:, l0:l0 + M], T["s_" + b][:, 0:M],
-                                     T.sem["arr%d" % t], T.sem.sent, pid, rid, mask), [V("s_" + b)], [], dma="remote", cost=300)
-        return 2 * len(topo.engines(core, dst))
+        for out, a in pairs:
+            cast = (lambda v: ap(v).bitcast(dt.uint8)) if SCRATCH[a[0]][2] == X4 else ap
+            op("G", lambda out=out, a=a, cast=cast: g.remote_dma(cast(out), cast(a), T.sem[sem], T.sem.sent, pid, rid, mask),
+               [a], [], dma=sem, cost=300)
+            sent[0] += len(topo.engines(core, dst))
+
+    def arrival(t, sem, calls):
+        return ((sem, calls * len(topo.engines(T.cores[(rank - 1 - t) % n_ranks], core))),)
+
+    def g0(t):
+        return (R - 1 - t) * C
+
+    def send_state(t, sem, c0, pair, p0, n):
+        send(t, sem, [(V(k + "g", g0(t) + c0, g0(t) + c0 + n), V(k + pair, p0, p0 + n)) for k in ("q_", "s_")])
 
     def h_tile(t):
-        src = T.cores[(rank - 1 - t) % n_ranks]
-        arrived = (("arr%d" % t, 2 * len(topo.engines(src, core))),)
-        l0 = (R - 1 - t) * M
-        e0 = sh0(t + 1) + 4 * K
-        for b in range(4):
-            mm(BK["w"][b], "w", 128 * b, "land", l0, 128, ext=arrived)
-        for b in range(4):
-            act(V("rel", M * b, M * b + M), bank(BK["w"][b], 0, M), ACT.Relu, scale=0.03125)
-            ts(V("rel", M * b, M * b + M), bank(BK["w"][b], 0, M), 0.0, 0.03125, ALU.max, ALU.mult)
+        e0, l0 = sh0(t + 1) + 4 * K, t * M // 4
+        arriving[0] = arrival(t, "arro%d" % t, 1)
+        move("V", V("gb", 0, 2 * M), ind(V("gt"), V("ofg", l0, l0 + M // 8)))
+        move("S", V("gb", 2 * M, 4 * M), ind(V("gt"), V("ofg", l0 + M // 8, l0 + M // 4)))
+        arriving[0] = ()
+        quant("land", 0, "gb", 0, 128)
+        for b, bk in enumerate(new(4)):
+            mm(bk, "w", 128 * b, "land", 0, 128)
+            act(V("rel", M * b, M * b + M), bank(bk, 0, M), ACT.Relu, scale=0.03125)
+            ts(V("rel", M * b, M * b + M), bank(bk, 0, M), 0.0, 0.03125, ALU.max, ALU.mult)
             either()
-        for b in range(4):
-            bk = BK["d"][b] if t < R - 1 else 4 + b
-            mm(bk, "e", (FULL + b) * 128, "land", l0, 128, ext=arrived)
+        for b, bk in enumerate(new(4)):
+            unpack(bk, b, "land", 0, "land", 0, 128)
             tt(V("sh", e0 + b, e0 + 4 * M, 4), bank(bk, 0, M), V("rel", M * b, M * b + M), ALU.add)
 
-    sent = 0
     ranks(True)
     for s in range(R + 1):
         win = V("xt") if s == 0 else V("eo%d" % (s - 1))
         scatter(V("lrow"), V("rku"), V("i256") if s == 0 else vrow(s - 1))
         act(vrow(s), ind(V("tab" if s < R else "i256"), V("rku")), ACT.Copy)
-        n_now = C if s == 0 else K
-        wrap4(V("lrow", 0, n_now), n_now, "off", 0, 64 if s == R else K // 2)
         b, m, n, eo, y = ["%s%d" % (k, s) for k in ("b", "m", "n", "eo", "y")]
-        if s == R:
-            gather("V", s, win, 0, 64)
-            gather("S", s, win, 64, 128)
-            gather("S", s, win, 128, K)
-            quant(b, 0, "sh", sh0(s), 128)
-            sent += send(s - 1)
-            break
-        gather("V", s, win, 0, K // 2)
-        gather("S", s, win, K // 2, K)
-        quant(b, 0, "sh", sh0(s), K)
+        wrap4(V("lrow"), "off", 0, 0, K)
         if s > 0:
-            sent += send(s - 1)
-        else:
-            gather("F", s, win, K, C)
+            l0 = (s - 1) * M // 4
+            ts(V("ofs", l0, l0 + M // 4), V("u4", 3, M, 4), 4.0, col(P_OS), ALU.mult, ALU.add)
+            send(s - 1, "arro%d" % (s - 1), [(V("ofg", l0, l0 + M // 4), V("ofs", l0, l0 + M // 4))])
+        gather("V" if s < R else "F", s, win, 0, K // 2)
+        gather("S" if s < R else "F", s, win, K // 2, K)
+        if s == R:
+            break
+        quant(b, 0, "sh", sh0(s), K)
+        send_state(s, "arre%d" % s, 0, b, 0, K)
 
-        def out(k, bk, c0, c1):
-            move("F", V(eo, 4 * c0 + k, 4 * c1, 4), bank(bk, 0, c1 - c0))
+        def parts_of(ev, c_ev, od, c_od, w, c0):
+            for k, bk in enumerate(new(4)):
+                unpack(bk, k, ev, c_ev, od, c_od, w)
+                move("F", V(eo, 4 * c0 + k, 4 * (c0 + w), 4), bank(bk, 0, w))
+            quant(eo, c0, eo, 4 * c0, w)
 
-        def both(bk, k, kind, own, a0, w):
-            mm(bk, "e", (kind + k) * 128, own, 0, w, True, False)
-            mm(bk, "e", (EVEN + ODD - kind + k) * 128, m, a0, w, False, True)
-            two, one = ops.pop(), ops.pop()
-            ops.append(("P", lambda: (one[1](), two[1]())[1], one[2] + two[2], one[3], None, (), one[6] + two[6], None, False))
+        def by_rows(e):
+            runs = range(G_RUNS - 1, -1, -1)
+            c0, w, bk = K * len(runs) * e, K * len(runs), new()
+            p0 = PL[(runs[0], e, 0, K)]
+            pick(y, c0, w, eo, (EO_O, EO_L)[e], V("pl", p0, p0 + w // 16))
+            mm(bk, "us", 128 * e, y, c0, w)
+            return [(V("r2", e, 2 * K, 2, p1=32 * a + 32), bank(bk, K * i, K * i + K, p0=32 * a, p1=32 * a + 1))
+                    for i, a in enumerate(runs)]
 
-        def early(e, h):
-            c0, bk = 640 * e + 320 * h, BK["se"][2 * e + h]
-            pick(y, c0, 320, eo, EO_O + K * e, V("pl", 40 * e + 20 * h, 40 * e + 20 * h + 20))
-            mm(bk, "us", 0, y, c0, 320)
-            for a in (2 * h, 2 * h + 1):
-                move("F", V("r2", e, 2 * K, 2, **run32(a)), bank(bk, K * (a % 2), K * (a % 2) + K, **run32(a)))
+        def by_run(a, i0, w):
+            c0, bk = 2 * K * a if i0 == 0 else 8 * K + 2 * w * a, new()
+            p0 = PL[(a, None, i0, w)]
+            pick(y, c0, 2 * w, eo, EO_L if i0 == 0 else EO_N, V("pl", p0, p0 + w // 8))
+            mm(bk, "us", 0, y, c0, 2 * w)
+            move("F", V("r2", 2 * i0, 2 * (i0 + w), **run32(a)), bank(bk, 0, 2 * w, **run32(a)))
 
-        def late(e, h):
-            c0, bk = 8 * K + 2 * M * (2 * e + h), BK["sl"][2 * e + h]
-            pick(y, c0, 2 * M, eo, EO_L + 128 * e + 128, V("pl", 80 + 24 * e + 12 * h, 92 + 24 * e + 12 * h))
-            mm(bk, "us", 0, y, c0, 2 * M)
-            for a in (2 * h, 2 * h + 1):
-                move("F", V("r2", 2 * K + e, 2 * C, 2, **run32(a)), bank(bk, M * (a % 2), M * (a % 2) + M, **run32(a)))
+        def givers(sems, c_ev, c_od, c0):
+            for k, bk in enumerate(new(4)):
+                arriving[0] = sum([arrival(s, x % s, 2) for x in sems], ())
+                unpack(bk, k, "g", g0(s) + c_ev, "g", g0(s) + c_od, K)
+                arriving[0] = ()
+                move("F", V("gt", 4 * c0 + k, 4 * (c0 + K), 4), bank(bk, 0, K))
 
         ts(V("r2l"), V("uw", 15, C, 16), 2.0, col(P_R2), ALU.mult, ALU.add)
-        pick(m, 0, K, b, 128, V("a2l", 0, 10))
-        pick(m, K, M, b, 128, V("a2l", 10, 16))
-        for k, bk in enumerate(BK["a"]):
-            mm(bk, "e", (FULL + k) * 128, b, 0, 128)
-            out(k, bk, EO_A, EO_E)
-        quant(eo, EO_A, eo, 4 * EO_A, 128)
-        for k, bk in enumerate(BK["e"]):
-            both(bk, k, EVEN, b, 0, K)
-            out(k, bk, EO_E, EO_O)
-        quant(eo, EO_E, eo, 4 * EO_E, K)
-        for k, bk in enumerate(BK["o"]):
-            both(bk, k, ODD, b, 0, K)
-            out(k, bk, EO_O, EO_L)
-        quant(eo, EO_O, eo, 4 * EO_O, K)
-        early(0, 0)
-        early(0, 1)
-        early(1, 0)
-        early(1, 1)
+        pick(m, 0, K, b, 128, V("a2l", 0, K // 16))
+        pick(n, 128, M, b, 128, V("a2l", K // 16, 16))
+        parts_of(b, 0, b, 0, 128, EO_A)
+        parts_of(b, 0, m, 0, K, EO_E)
+        parts_of(m, 0, b, 0, K, EO_O)
+        rows = (by_rows(0), by_rows(1)) if G_RUNS else ([], [])
+        for e in range(2):
+            for a in range(G_RUNS - 1, G_TAKES[s][e] - 1, -1):
+                o, i = rows[e].pop(0)
+                move("F", o[:1] + (32 * a, 32 * a + 32) + o[3:], i[:1] + (32 * a, 32 * a + 32) + i[3:])
+        for x in rows[0][:-1] + rows[1][:1] + rows[0][-1:] + rows[1][1:]:
+            spread(*x)
+        for a in range(G_RUNS, 4):
+            by_run(a, 0, K)
         if s > 0:
             h_tile(s - 1)
+        else:
+            wrap4(V("lrow"), "off", 0, K, C)
+            gather("F", s, win, K, C)
+            zero(V("sh", sh0(0) + 4 * C, sh0(0) + 4 * C + 128))
         quant(n, 0, "sh", sh0(s) + 4 * 128, 128)
-        for k, bk in enumerate(BK["le"]):
-            both(bk, k, EVEN, n, 128, 128)
-            out(k, bk, EO_L, EO_L + 128)
-        for k, bk in enumerate(BK["lo"]):
-            both(bk, k, ODD, n, 128, 128)
-            out(k, bk, EO_L + 128, EO_N)
-        for e in range(2):
-            quant(eo, EO_L + 128 * e, eo, 4 * (EO_L + 128 * e), 128)
-        for e in range(2):
-            late(e, 0)
-            late(e, 1)
+        quant(n, 128 + M, "sh", sh0(s) + 4 * K, 128)
+        send_state(s, "arrl%d" % s, K, n, 128 - M, M)
+        parts_of(n, 128 - M, n, 128, 2 * M, EO_L)
+        for a in range(4):
+            by_run(a, K, M)
+        givers(["arre%d"], 0, 0, 0)
+        givers(["arre%d", "arrl%d"], C - K, K, GT_L)
         ranks(False)
 
-    wrap4(vrow(R), C, "off2", C, 128)
+    wrap4(vrow(R), "off2", C, 128, C)
+    wrap4(vrow(R), "off2", C, 0, 128)
     scatter(V("orow"), V("rku"), V("i256"))
     dma("Y", "dol", lambda: T.ol[:], lambda: T.orow[0:128:16, :], [V("orow")], [])
     h_tile(R - 1)
@@ -579,8 +725,9 @@ def rank_program(g, core, T, topo):
     move("S", V("tt", 2 * C, 4 * C), ind(last, V("off2", 32, 64)))
     for h in range(2):
         quant("t", 128 * h, "tt", 2 * C * h, 128)
-        mm(2 + h, "v", 0, "t", 128 * h, 128)
-        move("F", V("yt", 128 * h, 128 * h + 128), bank(2 + h, 0, 128))
+        bk = new()
+        mm(bk, "v", 0, "t", 128 * h, 128)
+        move("F", V("yt", 128 * h, 128 * h + 128), bank(bk, 0, 128))
     dma("Y", "doc", lambda: T.oc[:], lambda: T.q_t[:].bitcast(dt.uint8), [V("q_t")], [])
 
     def store_scales(k, q):
@@ -591,7 +738,12 @@ def rank_program(g, core, T, topo):
     store_scales(3, "Y")
     dma("Y", "dy0", lambda: T.y[:], lambda: T.yt[:], [V("yt")], [])
 
-    ops = arrange(ops)
+    ops, at = arrange(ops)
+    banks.update(at)
+
+    def placed(vs):
+        return [v[:3] + (512 * at[v[3] // 512], 512 * at[v[3] // 512] + 512, 1) if v[0] == "ps" else v for v in vs]
+    ops = [o[:2] + (placed(o[2]), placed(o[3])) + o[4:] for o in ops]
 
     src = [o[4] if o[4] else o[0] for o in ops]
     seen = {}
@@ -638,7 +790,7 @@ def rank_program(g, core, T, topo):
         for j in waits[i]:
             queue[q].wait_ge(T.sem[value[j][0]], value[j][1])
         ins = o[1]()
-        if sem == "remote":
+        if _remote(o):
             continue
         if sem:
             ins.then_inc(T.sem[sem], 16)
@@ -647,7 +799,7 @@ def rank_program(g, core, T, topo):
             count[q] += 1
             ins.then_inc(T.sem["c" + q], 1)
             value[i] = ("c" + q, count[q])
-    g.wait_ge(T.sem.sent, sent)
+    g.wait_ge(T.sem.sent, sent[0])
     for o in ops:
-        if o[4] and o[4] != "remote":
+        if o[4] and not _remote(o):
             g.wait_ge(T.sem[o[4]], 16)

@@ -1,4 +1,4 @@
-from concourse.mybir import dt, AluOpType as ALU, ActivationFunctionType as ACT, AxisListType as AX
+from concourse.mybir import dt, AluOpType as ALU, ActivationFunctionType as ACT
 
 C, M, R = 256, 96, 3
 K = C - M
@@ -11,18 +11,39 @@ for _s in SEGS:
         SLOT[_j] = (SEG0[-1], _t)
     SEG0.append(SEG0[-1] + (C if "q" in _s else 16 * max(_s)))
 CT_N = SEG0[-1] + 64
-ON_SCALAR = (15, 14, 13, 12)
-SUM_ON_SCALAR = (3, 2, 1)
-RW = 96
+RW = 16 * min(SEGS[1])
+W0 = RW * (RW // 2 - 9)
+SHORT = 5
+KEYS = ((192, 256), (128, 192), (0, 128))
 G_RUNS = 2
 G_TAKES = ((2, 2), (2, 2), (2, 2))
 EO_A, EO_E, EO_O, EO_L, EO_M, EO_N = 0, 128, 128 + K, 128 + 2 * K, 128 + 2 * K + M, 128 + 2 * C
 GT_L = EO_M - EO_O
 GT_N = GT_L + K
-GATHER, SCATTER, S_FIX, PE_COL, LOAD, SLACK = 1.56, 3.8, 80, 0.6, 2400, 120
-TRIES = 60000
-HEAT = 300
-CASES = ((190, 3200, 3000, 1.1, 1.0, 1.1), (130, 2400, 2000, 0.9, 0.85, 1.0), (240, 4200, 5000, 1.4, 1.2, 1.4))
+GATHER, SCATTER, S_FIX, PE_COL, LOAD = 1.56, 3.8, 80, 0.6, 2400
+START = {"first": (0, "V"), "lanes": (800, "V"), "zf": (1500, "V"), "zeros g": (1800, "V"),
+         "zeros ct": ((1000, 2400, 2500, 3350), "S"), "zeros": ((10350, 26600, 27100), "V"), "negate": (5000, "V"), "ul": (8600, "V"),
+         "masks": (1500, "S"), "weights": (3400, "S"), "wrap": (7600, "S"), "eo tiles": ((2000, 2300, 3400, 3450), "V"),
+         "full tiles": ((8250, 8750, 9050, 10300), "V"), "bd": (5400, "V"), "lists": (9300, "S"), "pl": (11800, "V"), "tab": (7610, "S"),
+         "v": (45300, "V"), "u": (2600, "V"), "us": (11000, "V"), "scores": (3300, "V")}
+ROUND = {"scatter": (0, "V"), "r2l": (1100, "V"), "off": (1260, "V"), "ofs": (1261, "V"), "gather": (1950, "VS"), "b": (2730, "V"),
+         "m": (3150, "V"), "A": (3150, "VSVS", 90, 4320), "E": (3600, "VSVS", 210, 5100), "O": (4350, "VSVS", 210, 6750),
+         "gb": (5430, "V"), "land": (6030, "V"), "W": (6410, "SSSV"), "D": (6760, "V"), "add": (7400, "V"), "n": (8030, "V"),
+         "L": (8410, "SSVV", 250, 10110), "rows": ((6190, 8340), "V", (7130, 9500)), "spread": (7500, "V"),
+         "early": ((7000, 8900), "S", (8000, 9700)), "late": ((10560, 11520), "SVSV", (11750, 12130)),
+         "givers": ((16750, 18650), "S"), "off2": (2600, "V"), "out": (8000, "V"),
+         "inj": ((12950, 13110, 13400), "V"), "zs": ((13340, 13670, 13860), "V"), "q": ((14310, 15050, 15600), "V"), "sign": ((13830, 15030), "S"),
+         "above": ((13850, 14800, 15350), "V"), "sums": ((15950, 16650, 16250), "V"), "w": (16850, "V"),
+         "ct": ((15150, 15750, 16400), "V"), "uw": (17350, "V"), "rku": (17850, "V"), "next": (18150, "V")}
+FIRST = {"rest": (1260, "V"), "gather rest": (2500, "S"), "n": (3950, "V"), "O": (4350, "VSVS", 210, 6100), "L": (5200, "SSVV", 250, 7300),
+         "rows": ((5500, 6700), "V", (6300, 7500)), "spread": (6800, "V"), "early": ((7500, 8050), "V", (8300, 8850)),
+         "late": ((8600, 9560), "SVSV", (9800, 10150)), "next": (18150, "V")}
+TRIES = 90000
+HEAT = 150
+SEED = 1
+ASIDE = 40
+EARLY = 0.004
+CASES = ((230, 3000, 3000, 1.0, 1.0, 1.0), (190, 2300, 2000, 0.9, 0.85, 1.0), (280, 4000, 5000, 1.4, 1.2, 1.4))
 BANKS = 8
 
 PIECES = [(_a, _e, 0, K) for _e in range(2) for _a in range(G_RUNS - 1, -1, -1)]
@@ -37,18 +58,18 @@ SCRATCH = {
     "xt": ("sbuf", [128, 4 * C], BF), "ut": ("sbuf", [128, 512], BF), "vt": ("sbuf", [128, 512], BF),
     "sh": ("sbuf", [128, 16 * C + 128], BF), "tt": ("sbuf", [128, 4 * C], BF),
     "gt": ("sbuf", [128, 4 * GT_N], BF), "gb": ("sbuf", [128, 512], BF),
-    "ct": ("sbuf", [128, 4 * CT_N], BF), "gs": ("sbuf", [128, 6 * C], BF), "junk": ("sbuf", [128, 4 * C], BF),
+    "ct": ("sbuf", [128, 4 * CT_N], BF), "gs": ("sbuf", [128, 6 * C], BF),
     "ones": ("sbuf", [128, 512], BF), "ze": ("sbuf", [128, 1040], BF), "zf": ("sbuf", [128, 528], BF),
     "bd0": ("sbuf", [128, 512], BF), "bd": ("sbuf", [128, 1024], BF),
     "pi": ("sbuf", [128, 1], I32), "pci": ("sbuf", [128, 8], I32), "pc": ("sbuf", [128, 24], F32),
     "j16": ("sbuf", [128, C], F32), "j4": ("sbuf", [128, C], F32), "i256": ("sbuf", [128, C], F32),
     "i16": ("sbuf", [128, 24], F32), "ia": ("sbuf", [128, PL_N], F32), "plf": ("sbuf", [128, PL_N], F32),
     "tmp": ("sbuf", [128, 3 * C], F32), "mk": ("sbuf", [128, C], F32), "qm": ("sbuf", [128, C], BF), "qs": ("sbuf", [128, C], BF),
-    "d0": ("sbuf", [128, C], F32), "w16": ("sbuf", [128, C], F32), "w4": ("sbuf", [128, C], F32),
+    "d0": ("sbuf", [128, C], F32), "w16": ("sbuf", [128, W0 + C], F32), "w4": ("sbuf", [128, C], F32),
     "tab": ("sbuf", [128, C], F32), "cj": ("sbuf", [128, 16], F32), "wa": ("sbuf", [128, 16], F32),
     "ul": ("sbuf", [128, 16], U16), "a2l": ("sbuf", [128, 16], U16), "pl": ("sbuf", [128, PL_N], U16),
     "r2": ("sbuf", [128, 2 * C], F32), "rr": ("sbuf", [128, C], F32), "inj": ("sbuf", [128, C], F32),
-    "zs": ("sbuf", [128, C], F32), "uw": ("sbuf", [128, C], F32), "rs": ("sbuf", [128, 16 * RW], F32),
+    "zs": ("sbuf", [128, C], F32), "uw": ("sbuf", [128, C], F32), "rs": ("sbuf", [128, 16], F32),
     "rku": ("sbuf", [128, 16], U16),
     "r2l": ("sbuf", [128, 16], U16), "vrow": ("sbuf", [128, 4 * C], F32), "lrow": ("sbuf", [128, C], F32),
     "u4": ("sbuf", [128, 2 * C], F32), "off": ("sbuf", [128, 64], U16), "off2": ("sbuf", [128, 64], U16),
@@ -67,7 +88,7 @@ for _n, _w in _PAIRS.items():
     SCRATCH["q_" + _n] = ("sbuf", [128, _w], X4)
     SCRATCH["s_" + _n] = ("sbuf", [128, _w], U8)
 
-DMAS = ["dx", "du", "dv", "dwc", "dws", "dy0", "dol", "doc", "ds0", "ds1", "ds2", "ds3"]
+DMAS = ["dx", "du", "dv", "dwc", "dws", "dy0", "dy1", "dol", "doc0", "doc1", "ds0", "ds1", "ds2", "ds3"]
 SEMAPHORES = ["cV", "cS", "cP", "cG", "sent"] + DMAS + ["arr%s%d" % (_k, _t) for _t in range(R) for _k in "elo"]
 
 
@@ -105,7 +126,7 @@ def arrange(ops):
 
 def search(ops):
     n = len(ops)
-    seen, before, sends, own = {}, [], {}, []
+    seen, before, sends = {}, [], {}
     for i, o in enumerate(ops):
         deps = {}
         for vs, wr in ((o[2], False), (o[3], True)):
@@ -118,14 +139,11 @@ def search(ops):
         for vs, wr in ((o[2], False), (o[3], True)):
             for v in vs:
                 seen.setdefault(v[0], []).append((i, wr, v[1], v[2], _mask(v)))
-        if o[0] == "G":
-            if own:
-                deps.setdefault(own[-1], (0, 0, 0, 0))
-            own.append(i)
         if _remote(o):
-            sends[o[4]] = (i, 1 if o[4] == min(sends, key=lambda s: sends[s][0], default=o[4]) else 0)
+            sends.setdefault(o[4], []).append(i)
         for e in o[5]:
-            deps[sends[e[0]][0]] = (1, 0, 1, sends[e[0]][1])
+            for j in sends[e[0]]:
+                deps[j] = (1, 0, 1, 1 if e[0] == list(sends)[0] else 0)
         before.append(deps)
     reach = []
     for i, d in enumerate(before):
@@ -146,13 +164,6 @@ def search(ops):
         lag = [[(j, w[0] * wake + w[1] + w[2] * flight + w[3] * once) for j, w in d.items()] for d in before]
         cost = [[o[6] * (pe if o[0] == "P" else gp if o[0] == "G" else 1.0) * (ga if o[8] else 1.0) for o in f] for f in forms]
         cases.append((wake, lag, cost))
-    wake, lag, cost = cases[0]
-    tail = [0.0] * n
-    for i in range(n - 1, -1, -1):
-        tail[i] += cost[i][0] + (LOAD if ops[i][4] else 0)
-        for j, w in lag[i]:
-            tail[j] = max(tail[j], w + tail[i])
-
     queue_of = [["VSPGY".index(o[0]) for o in f] for f in forms]
     last = [LOAD if o[4] else 0 for o in ops]
     uses = {}
@@ -161,25 +172,19 @@ def search(ops):
 
     def build():
         left = [len(d) for d in before]
-        ready = {i: 0.0 for i in range(n) if not left[i]}
-        free, end, seq, form, open_ = [0.0] * 5, [0.0] * n, [], [0] * n, {}
+        ready, seq, open_ = [i for i in range(n) if not left[i]], [], {}
         while ready:
-            cand = [(max(t0, free[q]), i, k) for i, t0 in ready.items() for k, q in enumerate(queue_of[i])
-                    if product[i] < 0 or product[i] in open_ or sum(1 for x in open_.values() if x) < BANKS - 1]
-            first = min(cand)
-            q = queue_of[first[1]][first[2]]
-            t, i, k = max([c for c in cand if c[0] <= first[0] + SLACK and queue_of[c[1]][c[2]] == q], key=lambda c: tail[c[1]])
-            end[i] = free[q] = t + cost[i][k]
+            i = min([i for i in ready if product[i] < 0 or product[i] in open_ or sum(1 for x in open_.values() if x) < BANKS],
+                    key=lambda i: ops[i][9])
             if product[i] >= 0:
                 open_[product[i]] = open_.get(product[i], uses[product[i]]) - 1
             seq.append(i)
-            form[i] = k
-            del ready[i]
+            ready.remove(i)
             for j in after[i]:
                 left[j] -= 1
                 if not left[j]:
-                    ready[j] = max(end[x] + w for x, w in lag[j])
-        return seq, form
+                    ready.append(j)
+        return seq, [1 if o[7] and o[10] == "S" else 0 for o in ops]
 
     def place(seq):
         idle, at, left, user, behind = list(range(BANKS)), {}, {}, [-1] * BANKS, {}
@@ -195,7 +200,7 @@ def search(ops):
                 if not left[x]:
                     idle.append(at[x])
         return at, behind
-    seed = [12345]
+    seed = [SEED]
 
     def rnd(m):
         seed[0] = (seed[0] * 1103515245 + 12345) % 2147483648
@@ -229,7 +234,7 @@ def search(ops):
                     t, w = end[b] + wake_, -2 - b
                 end[i] = free[q] = t + cost_[i][k]
                 why[i], by[q] = w, i
-            total += max([e + x for e, x in zip(end, last)]) if stop == n else end[i] - known[c][0][i]
+            total += max([e + x for e, x in zip(end, last)]) + EARLY * sum(end) if stop == n else end[i] - known[c][0][i]
             res.append((end, why))
         return total, res
 
@@ -251,6 +256,11 @@ def search(ops):
     for trial in range(TRIES):
         some = held[rnd(len(cases))]
         j, i = some[rnd(len(some))]
+        if rnd(100) < ASIDE:
+            i = rnd(n)
+            j = -2 - known[rnd(len(cases))][1][i]
+            if j < 0:
+                continue
         s2, f2, kind, to = seq, form, rnd(10), where[i] + 1
         if kind < 3:
             x = (i, j)[rnd(2)]
@@ -296,6 +306,12 @@ def rank_program(g, core, T, topo):
     arriving = [()]
     banks, products = {}, [0]
 
+    plan = [0, 0, "V", START]
+
+    def when(step, k=0, more=0):
+        at, queues = (plan[3].get(step) or ROUND[step])[:2]
+        plan[1:3] = (at[k] if isinstance(at, tuple) else at) + more, queues[k % len(queues)]
+
     def new(k=None):
         products[0] += k or 1
         return products[0] - 1 if k is None else range(products[0] - k, products[0])
@@ -333,7 +349,9 @@ def rank_program(g, core, T, topo):
     def op(q, emit, reads, writes, dma=None, cost=None, other=None):
         if cost is None:
             cost = span(q, reads, writes)
-        ops.append((q, emit, parts(reads), parts(writes), dma, arriving[0], cost, other, bool(reads) and reads[0][0] in ("ind", "ind32")))
+        ops.append((q, emit, parts(reads), parts(writes), dma, arriving[0], cost, other, bool(reads) and reads[0][0] in ("ind", "ind32"),
+                    plan[0] + plan[1], plan[2]))
+        plan[1] += 1
 
     def ind(win, off):
         return ("ind", win, off)
@@ -355,10 +373,7 @@ def rank_program(g, core, T, topo):
         op("V", lambda: g.vector.tensor_copy(ap(ind(win, off)), ap(a)), [a, off], [win], cost=60 + SCATTER * C)
 
     def scan(out, a, b, o0, o1, init=0.0):
-        op("V", lambda: g.vector.tensor_tensor_scan(ap(out), ap(a), ap(b), init, o0, o1), [a, b], [out])
-
-    def reduce_add(out, a):
-        op("V", lambda: g.vector.tensor_reduce(ap(out), ap(a), AX.X, ALU.add), [a], [out])
+        op("V", lambda: g.vector.tensor_tensor_scan(ap(out), ap(a), ap(b), ap(init), o0, o1), [a, b, init], [out])
 
     def fill(out, c):
         op("V", lambda: g.vector.memset(ap(out), c), [], [out])
@@ -445,16 +460,19 @@ def rank_program(g, core, T, topo):
     dma("Y", "dws", lambda: T.s_w[:], lambda: T.ws[:], first_loads, [V("s_w")])
     dma("Y", "dv", lambda: T.vt[:], lambda: T.v[:], first_loads, [V("vt")])
 
+    iota(V("pi"), [[0, 1]], 0, 1)
     fill(V("ze"), 0.0)
     fill(V("ones", 0, 128), 1.0)
     fill(V("ones", 128, 512), 1.0)
-    fill(V("zf"), 0.0)
-    quant("g", R * C, "zf", 0, 128)
-    iota(V("pi"), [[0, 1]], 0, 1)
     iota(V("i16", 0, 16), [[16, 16]])
+    when("zf")
+    fill(V("zf"), 0.0)
+    when("zeros g")
+    quant("g", R * C, "zf", 0, 128)
+    when("lanes")
+    iota(V("j16"), [[0, 16], [1, 16]])
     keep(V("ze", 3, 512, 4), V("ones", 0, 128), [[32, 4], [1016, 2], [1, 16]], ALU.is_equal, 0, -1)
     keep(V("ze", 515, 1024, 4), V("ones", 0, 128), [[32, 4], [-984, 2], [1, 16]], ALU.is_equal, 1000, -1)
-    iota(V("j16"), [[0, 16], [1, 16]])
     keep(V("bd0"), V("ones"), [[-16, 8], [0, 64]], ALU.is_ge, 0, 1)
     keep(V("bd", 0, 512), V("bd0"), [[16, 8], [0, 64]], ALU.is_ge, 15, -1)
     iota(V("i256"), [[1, C]])
@@ -471,33 +489,40 @@ def rank_program(g, core, T, topo):
         w = n // (8 if mixed else 16)
         iota(V("ia", c0, c0 + w * reps), [[0, reps], [4 if mixed else 8, w]], i0 // 2)
     for k, seg in enumerate(SEGS):
+        when("zeros ct", k)
         low = 16 * min(j for j in seg if j != "q")
         zero(V("ct", 4 * (SEG0[k] + low), 4 * (SEG0[k + 1] if k + 1 < len(SEGS) else CT_N)))
-    zero(V("rs", RW - 1, RW))
-    zero(V("gb", 4 * M, 512))
-    zero(V("gt", 4 * K, 4 * GT_L))
-    move("F", V("bd", 512, 1024), V("bd", 0, 512))
-    affine(V("bd", 512, 1024, 4), V("bd", 0, 512, 4), -1.0, 0.0)
-    ts(V("bd", 512, 1024, 4), V("bd", 0, 512, 4), -1.0, None, ALU.mult)
+    zero(V("rs", 0, 1))
+    for k, v in enumerate((V("sh", 16 * C, 16 * C + 128), V("gb", 4 * M, 512), V("gt", 4 * K, 4 * GT_L))):
+        when("zeros", k)
+        zero(v)
+    when("negate")
+    affine(V("bd", 512, 1024), V("bd", 0, 512), -1.0, 0.0)
+    ts(V("bd", 512, 1024), V("bd", 0, 512), -1.0, None, ALU.mult)
     either()
+    when("lanes")
     for k, (by, low) in enumerate(((0, 15), (4, 1), (1, 7), (2, 3), (0, 3), (0, 1))):
         ts(V("pci", k, k + 1), V("pi"), by, low, ALU.logical_shift_right, ALU.bitwise_and)
     cp(V("pc", 0, 2), V("pci", 0, 2))
     cp(V("pc", 2, 6), V("pci", 2, 6))
     cp(V("ul", 0, 8), V("i16", 0, 8))
+    when("ul")
     cp(V("ul", 8, 16), V("i16", 16, 24))
     ts(V("a2l"), V("i16", 0, 16), 0.5, col(P_LH), ALU.mult, ALU.add)
+    when("masks")
     affine(col(P_MK), col(P_L), -BIG, 0.0)
     act(col(P_Y), col(P_L), ACT.Relu, bias=87040.0, scale=-6144.0)
     affine(col(P_Z), col(P_L), 1.0, -1024.0)
+    act(V("d0"), V("j16"), ACT.Relu, bias=64 * BIG, scale=-64 * BIG)
+    act(V("mk"), V("j16"), ACT.Abs, bias=col(P_MK), scale=BIG)
     affine(col(P_CJ), col(P_Y), -1.0, col(P_Z))
     affine(col(P_R2), col(P_E), 1.0, 2048.0)
-    act(V("mk"), V("j16"), ACT.Abs, bias=col(P_MK), scale=BIG)
-    act(V("d0"), V("j16"), ACT.Relu, bias=64 * BIG, scale=-64 * BIG)
-    act(V("qm"), V("j16"), ACT.Sign)
+    when("weights")
     act(V("tmp", 0, C), V("j16"), ACT.Sign, bias=col(P_MK), scale=BIG)
+    act(V("qm"), V("j16"), ACT.Sign)
     affine(V("cj"), V("i16", 0, 16), 1.0, col(P_CJ))
-    affine(V("w16"), V("tmp", 0, C), 5120.0, 1024.0)
+    affine(V("w16", W0), V("tmp", 0, C), 5120.0, 1024.0)
+    when("wrap")
     affine(col(P_NQ), col(P_LQ), -1.0, 0.0)
     affine(col(P_X), col(P_L4), 1.0, -12288.0)
     affine(col(P_O4), col(P_LQ), 4096.0, col(P_X))
@@ -505,10 +530,14 @@ def rank_program(g, core, T, topo):
     act(V("tmp", 2 * C, 3 * C), V("tmp", C, 2 * C), ACT.Abs, scale=17408.0)
     affine(V("w4"), V("tmp", 2 * C, 3 * C), 1.0, -16384.0)
     for b in range(4):
+        when("eo tiles", b)
         quant("e", 2 * b * 128, "ze", 3 - b, 256)
+        when("full tiles", b)
         quant("e", (8 + b) * 128, "zf", 3 - b, 128)
+    when("bd")
     quant("bd", 0, "bd", 0, 128)
     quant("bd", 128, "bd", 512, 128)
+    when("lists")
     single = sum(p[3] // 16 for p in PIECES if p[1] is not None)
     if single:
         affine(V("plf", 0, single), V("ia", 0, single), 1.0, col(P_LH))
@@ -524,20 +553,26 @@ def rank_program(g, core, T, topo):
         else:
             c0 = (EO_E, EO_O)[e]
             affine(V("plf", PL[p], PL[p] + n // 16, **run32(a)), V("i256", c0 // 16, (c0 + n) // 16, **run32(a)), 16.0, col(P_L, **run32(a)))
+    when("pl")
     if single:
         cp(V("pl", 0, single), V("plf", 0, single))
     cp(V("pl", single, PL_N), V("plf", single, PL_N))
+    when("tab")
     affine(col(P_T0), col(P_E), float(K), float(EO_E))
     affine(col(P_T1), col(P_E), float(M), float(EO_L - K))
     affine(col(P_OS), col(P_T0), -4.0, col(P_O4))
     affine(V("tab", 0, K), V("i256", 0, K), 1.0, col(P_T0))
     affine(V("tab", K, C), V("i256", K, C), 1.0, col(P_T1))
+    when("v")
+    quant("v", 0, "vt", 0, 128)
+    when("u")
     quant("u", 0, "ut", 0, 128)
+    quant("x", 0, "xt", 0, C)
     pick("us", 0, 128, "u", 128, V("ul", 0, 8))
+    when("us")
     if G_RUNS:
         pick("us", 128, 128, "u", 128, V("ul", 8, 16))
-    quant("x", 0, "xt", 0, C)
-    quant("v", 0, "vt", 0, 128)
+    when("scores")
     for_v, for_s = new(2)
     mm(for_v, "us", 0, "x", 0, C)
     mm(for_s, "us", 0, "x", 0, C)
@@ -555,40 +590,53 @@ def rank_program(g, core, T, topo):
 
         def scores(c0, c1):
             return bank(for_v, c0, c1) if first else ind(V("r2"), V("r2l", c0 // 16, c1 // 16))
-        for c0, c1 in ((128, C), (0, 128)):
+        for k, (c0, c1) in enumerate(KEYS):
+            when("inj", k)
             tt(V("inj", c0, c1), scores(c0, c1), V("mk", c0, c1), ALU.add)
+            when("zs", k)
             scan(V("zs", c0, c1), V("d0", c0, c1), V("inj", c0, c1), ALU.add, ALU.min)
+        when("inj")
         if not first:
             act(V("rr"), scores(0, C), ACT.Copy)
+        when("q", 0)
         tt(slot("q", 0, C), scores(0, C), V("zs"), ALU.is_gt)
+        when("q", 1)
         scan(V("qs"), V("qm"), slot("q", 0, C), ALU.mult, ALU.add)
+        when("q", 2)
         tt(V("wa"), V("cj"), V("qs", 15, C, 16), ALU.add)
         for j in range(15, 0, -1):
-            n, total = 16 * j, V("rs", RW * j + RW - 1, RW * j + RW)
-            if j in ON_SCALAR:
-                i = ON_SCALAR.index(j)
+            n, end = 16 * j, W0 + 16 * j + 16
+            if j in SEGS[1]:
+                i = SEGS[1].index(j)
+                when("sign", 0, 300 * i)
                 act(V("gs", i * C, i * C + n), row("S", 0, n), ACT.Sign, bias=key(j), scale=-1.0)
-                act(slot(j, 0, n), V("gs", i * C, i * C + n), ACT.Relu, acc=total)
-                continue
-            ts(slot(j, 0, n), row("V", 0, n), key(j), None, ALU.is_lt)
-            if j in SUM_ON_SCALAR:
-                act(V("junk", C * (j % 4), C * (j % 4) + n), slot(j, 0, n), ACT.Copy, acc=total)
-            elif j <= 4:
-                reduce_add(total, slot(j, 0, n))
+                when("sign", 1, 300 * i)
+                act(slot(j, 0, n), V("gs", i * C, i * C + n), ACT.Relu, acc=V("rs", j, j + 1))
             else:
-                scan(V("rs", RW * j + RW - n // 2, RW * j + RW), slot(j, 0, n, 2), slot(j, 1, n, 2), ALU.add, ALU.add)
-        quant("ct", SEG0[0], "ct", 4 * SEG0[0], SEG0[1] - SEG0[0])
-        quant("ct", SEG0[2], "ct", 4 * SEG0[2], (CT_N if first else SEG0[4]) - SEG0[2])
-        quant("ct", SEG0[1], "ct", 4 * SEG0[1], SEG0[2] - SEG0[1])
+                when("above", 0 if j > 8 else 1 if j > 4 else 2, -j)
+                ts(slot(j, 0, n), row("V", 0, n), key(j), -1.0, ALU.is_lt, ALU.mult)
+                when("sums", 0 if j > 7 else 1 if j >= SHORT else 2, -j)
+                if j < SHORT:
+                    act(V("gs", 4 * C + 8 * j * (j - 1), 4 * C + 8 * j * (j + 1)), slot(j, 0, n), ACT.Abs, acc=V("rs", j, j + 1))
+                else:
+                    scan(V("w16", end - 1 - RW * (n // 2 - 1), end, RW), slot(j, 0, n, 2), slot(j, 1, n, 2), ALU.add, ALU.add, V("wa", j, j + 1))
+        when("w")
+        for j0, j1 in ((min(SEGS[1]), 16), (0, SHORT)):
+            tt(V("w16", W0 + 16 * j0 + 15, W0 + 16 * j1, 16), V("wa", j0, j1), V("rs", j0, j1), ALU.subtract)
+        for k, (c0, c1) in enumerate(((SEG0[0], SEG0[1]), (SEG0[2], CT_N if first else SEG0[4]), (SEG0[1], SEG0[2]))):
+            when("ct", k)
+            quant("ct", c0, "ct", 4 * c0, c1 - c0)
         counts = new()
         for k in (0, 2, 3, 1):
-            mm(counts, "bd", 128 if k == 0 else 0, "ct", SEG0[k], max(128, SEG0[k + 1] - SEG0[k]), k == 0, k == 1)
-        tt(V("w16", 15, C, 16), V("wa"), V("rs", RW - 1, 16 * RW, RW), ALU.subtract)
-        scan(V("uw"), bank(counts, 0, C), V("w16"), ALU.max, ALU.add, -1024.0)
+            mm(counts, "bd", 0 if k == 1 else 128, "ct", SEG0[k], max(128, SEG0[k + 1] - SEG0[k]), k == 0, k == 1)
+        when("uw")
+        scan(V("uw"), bank(counts, 0, C), V("w16", W0), ALU.max, ALU.add, -1024.0)
+        when("rku")
         ts(V("rku"), V("uw", 15, C, 16), 1024.0, None, ALU.add)
 
-    def wrap4(row, off, u0, c0, c1):
-        scan(V("u4", u0 + c0, u0 + c1), V("w4", c0, c1), V(row[0], row[3] + c0, row[3] + c1), ALU.add, ALU.max)
+    def wrap4(row, off, u0, c0, c1, cut=None):
+        for a, b in ((c0, cut), (cut, c1)) if cut else ((c0, c1),):
+            scan(V("u4", u0 + a, u0 + b), V("w4", a, b), V(row[0], row[3] + a, row[3] + b), ALU.add, ALU.max)
         ts(V(off, c0 // 4, c1 // 4), V("u4", u0 + c0 + 3, u0 + c1, 4), 4.0, col(P_O4), ALU.mult, ALU.add)
 
     def sh0(s):
@@ -624,103 +672,139 @@ def rank_program(g, core, T, topo):
     def h_tile(t):
         e0, l0 = sh0(t + 1) + 4 * K, t * M // 4
         arriving[0] = arrival(t, "arro%d" % t, 1)
+        when("gb")
         move("V", V("gb", 0, 2 * M), ind(V("gt"), V("ofg", l0, l0 + M // 8)))
         move("S", V("gb", 2 * M, 4 * M), ind(V("gt"), V("ofg", l0 + M // 8, l0 + M // 4)))
         arriving[0] = ()
+        when("land")
         quant("land", 0, "gb", 0, 128)
         for b, bk in enumerate(new(4)):
+            when("W", b, 90 * b)
             mm(bk, "w", 128 * b, "land", 0, 128)
+            when("W", b, 380 + 180 * b)
             act(V("rel", M * b, M * b + M), bank(bk, 0, M), ACT.Relu, scale=0.03125)
             ts(V("rel", M * b, M * b + M), bank(bk, 0, M), 0.0, 0.03125, ALU.max, ALU.mult)
             either()
         for b, bk in enumerate(new(4)):
+            when("D", 0, 90 * b)
             unpack(bk, b, "land", 0, "land", 0, 128)
+            when("add", 0, 100 * b)
             tt(V("sh", e0 + b, e0 + 4 * M, 4), bank(bk, 0, M), V("rel", M * b, M * b + M), ALU.add)
 
+    plan[0] = 4000 - ROUND["inj"][0][0]
     ranks(True)
     for s in range(R + 1):
+        when("next")
+        plan[0], plan[3] = plan[0] + plan[1], FIRST if s == 0 else {}
+        when("scatter")
         win = V("xt") if s == 0 else V("eo%d" % (s - 1))
         scatter(V("lrow"), V("rku"), V("i256") if s == 0 else vrow(s - 1))
         act(vrow(s), ind(V("tab" if s < R else "i256"), V("rku")), ACT.Copy)
         b, m, n, eo, y = ["%s%d" % (k, s) for k in ("b", "m", "n", "eo", "y")]
-        wrap4(V("lrow"), "off", 0, 0, K)
+        when("off")
+        wrap4(V("lrow"), "off", 0, 0, K, M if s else None)
+        when("ofs")
         if s > 0:
             l0 = (s - 1) * M // 4
             ts(V("ofs", l0, l0 + M // 4), V("u4", 3, M, 4), 4.0, col(P_OS), ALU.mult, ALU.add)
             send(s - 1, "arro%d" % (s - 1), [(V("ofg", l0, l0 + M // 4), V("ofs", l0, l0 + M // 4))])
-        gather("V" if s < R else "F", s, win, 0, K // 2)
-        gather("S" if s < R else "F", s, win, K // 2, K)
+        when("gather")
+        gather("V", s, win, 0, K // 2)
+        gather("S", s, win, K // 2, K)
         if s == R:
             break
+        when("b")
         quant(b, 0, "sh", sh0(s), K)
         send_state(s, "arre%d" % s, 0, b, 0, K)
 
-        def parts_of(ev, c_ev, od, c_od, w, c0):
+        def also(step, k):
+            return (plan[3].get(step) or ROUND[step])[k]
+
+        def parts_of(step, ev, c_ev, od, c_od, w, c0):
             for k, bk in enumerate(new(4)):
+                when(step, k, also(step, 2) * k)
                 unpack(bk, k, ev, c_ev, od, c_od, w)
+                when(step, k, also(step, 2) * (k + 1) + 290)
                 move("F", V(eo, 4 * c0 + k, 4 * (c0 + w), 4), bank(bk, 0, w))
+            plan[1] = also(step, 3)
             quant(eo, c0, eo, 4 * c0, w)
 
         def by_rows(e):
             runs = range(G_RUNS - 1, -1, -1)
             c0, w, bk = K * len(runs) * e, K * len(runs), new()
             p0 = PL[(runs[0], e, 0, K)]
+            when("rows", e)
             pick(y, c0, w, eo, (EO_O, EO_L)[e], V("pl", p0, p0 + w // 16))
+            plan[1] = also("rows", 2)[e]
             mm(bk, "us", 128 * e, y, c0, w)
             return [(V("r2", e, 2 * K, 2, p1=32 * a + 32), bank(bk, K * i, K * i + K, p0=32 * a, p1=32 * a + 1))
                     for i, a in enumerate(runs)]
 
-        def by_run(a, i0, w):
-            c0, bk = 2 * K * a if i0 == 0 else 8 * K + 2 * w * a, new()
-            p0 = PL[(a, None, i0, w)]
-            pick(y, c0, 2 * w, eo, EO_L if i0 == 0 else EO_N, V("pl", p0, p0 + w // 8))
-            mm(bk, "us", 0, y, c0, 2 * w)
-            move("F", V("r2", 2 * i0, 2 * (i0 + w), **run32(a)), bank(bk, 0, 2 * w, **run32(a)))
+        def by_run(a0, runs, i0, w):
+            c0 = 2 * K * a0 if i0 == 0 else 8 * K + 2 * w * a0
+            p0 = PL[(a0, None, i0, w)]
+            step = "late" if i0 else "early"
+            when(step, a0 % 2)
+            pick(y, c0, 2 * w * runs, eo, EO_L if i0 == 0 else EO_N, V("pl", p0, p0 + w * runs // 8))
+            for k, bk in enumerate(new(runs)):
+                plan[1] = also(step, 2)[a0 % 2] + 125 * k
+                mm(bk, "us", 0, y, c0 + 2 * w * k, 2 * w)
+                plan[1:3] = plan[1] + 420, also(step, 1)[(a0 + k) % len(also(step, 1))]
+                move("F", V("r2", 2 * i0, 2 * (i0 + w), **run32(a0 + k)), bank(bk, 0, 2 * w, **run32(a0 + k)))
 
         def givers(sems, c_ev, c_od, c0):
             for k, bk in enumerate(new(4)):
                 arriving[0] = sum([arrival(s, x % s, 2) for x in sems], ())
+                when("givers", len(sems) - 1, 240 * k - 500)
                 unpack(bk, k, "g", g0(s) + c_ev, "g", g0(s) + c_od, K)
                 arriving[0] = ()
+                when("givers", len(sems) - 1, 240 * k)
                 move("F", V("gt", 4 * c0 + k, 4 * (c0 + K), 4), bank(bk, 0, K))
 
+        when("r2l")
         ts(V("r2l"), V("uw", 15, C, 16), 2.0, col(P_R2), ALU.mult, ALU.add)
+        when("m")
         pick(m, 0, K, b, 128, V("a2l", 0, K // 16))
         pick(n, 128, M, b, 128, V("a2l", K // 16, 16))
-        parts_of(b, 0, b, 0, 128, EO_A)
-        parts_of(b, 0, m, 0, K, EO_E)
-        parts_of(m, 0, b, 0, K, EO_O)
+        parts_of("A", b, 0, b, 0, 128, EO_A)
+        parts_of("E", b, 0, m, 0, K, EO_E)
+        parts_of("O", m, 0, b, 0, K, EO_O)
         rows = (by_rows(0), by_rows(1)) if G_RUNS else ([], [])
         for e in range(2):
             for a in range(G_RUNS - 1, G_TAKES[s][e] - 1, -1):
                 o, i = rows[e].pop(0)
                 move("F", o[:1] + (32 * a, 32 * a + 32) + o[3:], i[:1] + (32 * a, 32 * a + 32) + i[3:])
-        for x in rows[0][:-1] + rows[1][:1] + rows[0][-1:] + rows[1][1:]:
+        for k, x in enumerate(rows[0] + rows[1]):
+            when("spread", 0, 1000 * k)
             spread(*x)
         for a in range(G_RUNS, 4):
-            by_run(a, 0, K)
+            by_run(a, 1, 0, K)
         if s > 0:
             h_tile(s - 1)
         else:
+            when("rest")
             wrap4(V("lrow"), "off", 0, K, C)
+            when("gather rest")
             gather("F", s, win, K, C)
-            zero(V("sh", sh0(0) + 4 * C, sh0(0) + 4 * C + 128))
+        when("n")
         quant(n, 0, "sh", sh0(s) + 4 * 128, 128)
         quant(n, 128 + M, "sh", sh0(s) + 4 * K, 128)
         send_state(s, "arrl%d" % s, K, n, 128 - M, M)
-        parts_of(n, 128 - M, n, 128, 2 * M, EO_L)
-        for a in range(4):
-            by_run(a, K, M)
+        parts_of("L", n, 128 - M, n, 128, 2 * M, EO_L)
+        by_run(0, 3, K, M)
+        by_run(3, 1, K, M)
         givers(["arre%d"], 0, 0, 0)
         givers(["arre%d", "arrl%d"], C - K, K, GT_L)
         ranks(False)
 
+    when("off2")
     wrap4(vrow(R), "off2", C, 128, C)
     wrap4(vrow(R), "off2", C, 0, 128)
     scatter(V("orow"), V("rku"), V("i256"))
     dma("Y", "dol", lambda: T.ol[:], lambda: T.orow[0:128:16, :], [V("orow")], [])
     h_tile(R - 1)
     last = V("sh", sh0(R), sh0(R) + 4 * C)
+    when("out")
     move("V", V("tt", 0, 2 * C), ind(last, V("off2", 0, 32)))
     move("S", V("tt", 2 * C, 4 * C), ind(last, V("off2", 32, 64)))
     for h in range(2):
@@ -728,15 +812,17 @@ def rank_program(g, core, T, topo):
         bk = new()
         mm(bk, "v", 0, "t", 128 * h, 128)
         move("F", V("yt", 128 * h, 128 * h + 128), bank(bk, 0, 128))
-    dma("Y", "doc", lambda: T.oc[:], lambda: T.q_t[:].bitcast(dt.uint8), [V("q_t")], [])
+        dma("Y", "doc%d" % h, lambda h=h: T.oc[:, 512 * h:512 * h + 512], lambda h=h: T.q_t[:, 128 * h:128 * h + 128].bitcast(dt.uint8),
+            [V("q_t", 128 * h, 128 * h + 128)], [])
+        dma("Y", "dy%d" % h, lambda h=h: T.y[:, 128 * h:128 * h + 128], lambda h=h: T.yt[:, 128 * h:128 * h + 128],
+            [V("yt", 128 * h, 128 * h + 128)], [])
 
     def store_scales(k, q):
         dma(q, "ds%d" % k, lambda: T.osc[4 * k:4 * k + 4, :], lambda: T.s_t[32 * k:32 * k + 4, :], [V("s_t")], [])
     store_scales(0, "S")
     store_scales(1, "S")
     store_scales(2, "S")
-    store_scales(3, "Y")
-    dma("Y", "dy0", lambda: T.y[:], lambda: T.yt[:], [V("yt")], [])
+    store_scales(3, "S")
 
     ops, at = arrange(ops)
     banks.update(at)

from concourse.mybir import dt, AluOpType as ALU, ActivationFunctionType as ACT

C, M, R = 256, 96, 3
K = C - M
F32, BF, U16, I32, X4, U8 = "float32", "bfloat16", "uint16", "int32", "float8_e4m3fn_x4", "uint8"
BIG = 2.0 ** 90
SEGS = (("q", 11, 10, 9), (15, 14, 13, 12), (8, 7, 6, 5), (4, 3, 2, 1))
SEG0, SLOT = [0], {}
for _s in SEGS:
    for _t, _j in enumerate(_s):
        SLOT[_j] = (SEG0[-1], _t)
    SEG0.append(SEG0[-1] + (C if "q" in _s else 16 * max(_s)))
CT_N = SEG0[-1] + 64
RW = 16 * min(SEGS[1])
W0 = RW * (RW // 2 - 9)
SHORT = 5
KEYS = ((192, 256), (128, 192), (0, 128))
G_RUNS = 2
G_TAKES = ((2, 2), (2, 2), (2, 2))
EO_A, EO_E, EO_O, EO_L, EO_M, EO_N = 0, 128, 128 + K, 128 + 2 * K, 128 + 2 * K + M, 128 + 2 * C
GT_L = EO_M - EO_O
GT_N = GT_L + K
GATHER, SCATTER, S_FIX, PE_COL, LOAD = 1.56, 3.8, 80, 0.6, 2400
START = {"first": (0, "V"), "lanes": (800, "V"), "zf": (1500, "V"), "zeros g": (1800, "V"),
         "zeros ct": ((1000, 2400, 2500, 3350), "S"), "zeros": ((10350, 26600, 27100), "V"), "negate": (5000, "V"), "ul": (8600, "V"),
         "masks": (1500, "S"), "weights": (3400, "S"), "wrap": (7600, "S"), "eo tiles": ((2000, 2300, 3400, 3450), "V"),
         "full tiles": ((8250, 8750, 9050, 10300), "V"), "bd": (5400, "V"), "lists": (9300, "S"), "pl": (11800, "V"), "tab": (7610, "S"),
         "v": (45300, "V"), "u": (2600, "V"), "us": (11000, "V"), "scores": (3300, "V")}
ROUND = {"scatter": (0, "V"), "r2l": (1100, "V"), "off": (1260, "V"), "ofs": (1261, "V"), "gather": (1950, "VS"), "b": (2730, "V"),
         "m": (3150, "V"), "A": (3150, "VSVS", 90, 4320), "E": (3600, "VSVS", 210, 5100), "O": (4350, "VSVS", 210, 6750),
         "gb": (5430, "V"), "land": (6030, "V"), "W": (6410, "SSSV"), "D": (6760, "V"), "add": (7400, "V"), "n": (8030, "V"),
         "L": (8410, "SSVV", 250, 10110), "rows": ((6190, 8340), "V", (7130, 9500)), "spread": (7500, "V"),
         "early": ((7000, 8900), "S", (8000, 9700)), "late": ((10560, 11520), "SVSV", (11750, 12130)),
         "givers": ((16750, 18650), "S"), "off2": (2600, "V"), "out": (8000, "V"),
         "inj": ((12950, 13110, 13400), "V"), "zs": ((13340, 13670, 13860), "V"), "q": ((14310, 15050, 15600), "V"), "sign": ((13830, 15030), "S"),
         "above": ((13850, 14800, 15350), "V"), "sums": ((15950, 16650, 16250), "V"), "w": (16850, "V"),
         "ct": ((15150, 15750, 16400), "V"), "uw": (17350, "V"), "rku": (17850, "V"), "next": (18150, "V")}
FIRST = {"rest": (1260, "V"), "gather rest": (2500, "S"), "n": (3950, "V"), "O": (4350, "VSVS", 210, 6100), "L": (5200, "SSVV", 250, 7300),
         "rows": ((5500, 6700), "V", (6300, 7500)), "spread": (6800, "V"), "early": ((7500, 8050), "V", (8300, 8850)),
         "late": ((8600, 9560), "SVSV", (9800, 10150)), "next": (18150, "V")}
TRIES = 90000
HEAT = 150
SEED = 1
ASIDE = 40
EARLY = 0.004
CASES = ((230, 3000, 3000, 1.0, 1.0, 1.0), (190, 2300, 2000, 0.9, 0.85, 1.0), (280, 4000, 5000, 1.4, 1.2, 1.4))
BANKS = 8

PIECES = [(_a, _e, 0, K) for _e in range(2) for _a in range(G_RUNS - 1, -1, -1)]
PIECES += [(_a, None, 0, K) for _a in range(G_RUNS, 4)] + [(_a, None, K, M) for _a in range(4)]
PL, PL_N = {}, 0
for _p in PIECES:
    PL[_p] = PL_N
    PL_N += _p[3] // (8 if _p[1] is None else 16)

SCRATCH = {
    "ps": ("psum", [128, 4096], F32),
    "xt": ("sbuf", [128, 4 * C], BF), "ut": ("sbuf", [128, 512], BF), "vt": ("sbuf", [128, 512], BF),
    "sh": ("sbuf", [128, 16 * C + 128], BF), "tt": ("sbuf", [128, 4 * C], BF),
    "gt": ("sbuf", [128, 4 * GT_N], BF), "gb": ("sbuf", [128, 512], BF),
    "ct": ("sbuf", [128, 4 * CT_N], BF), "gs": ("sbuf", [128, 6 * C], BF),
    "ones": ("sbuf", [128, 512], BF), "ze": ("sbuf", [128, 1040], BF), "zf": ("sbuf", [128, 528], BF),
    "bd0": ("sbuf", [128, 512], BF), "bd": ("sbuf", [128, 1024], BF),
    "pi": ("sbuf", [128, 1], I32), "pci": ("sbuf", [128, 8], I32), "pc": ("sbuf", [128, 24], F32),
    "j16": ("sbuf", [128, C], F32), "j4": ("sbuf", [128, C], F32), "i256": ("sbuf", [128, C], F32),
    "i16": ("sbuf", [128, 24], F32), "ia": ("sbuf", [128, PL_N], F32), "plf": ("sbuf", [128, PL_N], F32),
    "tmp": ("sbuf", [128, 3 * C], F32), "mk": ("sbuf", [128, C], F32), "qm": ("sbuf", [128, C], BF), "qs": ("sbuf", [128, C], BF),
    "d0": ("sbuf", [128, C], F32), "w16": ("sbuf", [128, W0 + C], F32), "w4": ("sbuf", [128, C], F32),
    "tab": ("sbuf", [128, C], F32), "cj": ("sbuf", [128, 16], F32), "wa": ("sbuf", [128, 16], F32),
    "ul": ("sbuf", [128, 16], U16), "a2l": ("sbuf", [128, 16], U16), "pl": ("sbuf", [128, PL_N], U16),
    "r2": ("sbuf", [128, 2 * C], F32), "rr": ("sbuf", [128, C], F32), "inj": ("sbuf", [128, C], F32),
    "zs": ("sbuf", [128, C], F32), "uw": ("sbuf", [128, C], F32), "rs": ("sbuf", [128, 16], F32),
    "rku": ("sbuf", [128, 16], U16),
    "r2l": ("sbuf", [128, 16], U16), "vrow": ("sbuf", [128, 4 * C], F32), "lrow": ("sbuf", [128, C], F32),
    "u4": ("sbuf", [128, 2 * C], F32), "off": ("sbuf", [128, 64], U16), "off2": ("sbuf", [128, 64], U16),
    "ofs": ("sbuf", [128, R * M // 4], U16), "ofg": ("sbuf", [128, R * M // 4], U16),
    "orow": ("sbuf", [128, C], F32), "rel": ("sbuf", [128, 4 * M], F32), "yt": ("sbuf", [128, C], F32),
}
_PAIRS = {"x": C, "u": 128, "us": 256, "v": 128, "w": 512, "e": 12 * 128, "bd": 256, "ct": CT_N, "land": 128, "t": C, "g": R * C + 128}
for _t in range(R):
    _PAIRS["b%d" % _t] = K
    _PAIRS["m%d" % _t] = K
    _PAIRS["n%d" % _t] = 256 + M
    _PAIRS["eo%d" % _t] = EO_N
    _PAIRS["y%d" % _t] = 8 * C
    SCRATCH["eo%d" % _t] = ("sbuf", [128, 4 * EO_N], BF)
for _n, _w in _PAIRS.items():
    SCRATCH["q_" + _n] = ("sbuf", [128, _w], X4)
    SCRATCH["s_" + _n] = ("sbuf", [128, _w], U8)

DMAS = ["dx", "du", "dv", "dwc", "dws", "dy0", "dy1", "dol", "doc0", "doc1", "ds0", "ds1", "ds2", "ds3"]
SEMAPHORES = ["cV", "cS", "cP", "cG", "sent"] + DMAS + ["arr%s%d" % (_k, _t) for _t in range(R) for _k in "elo"]


def V(buf, c0=0, c1=None, step=1, p0=0, p1=128):
    return (buf, p0, p1, c0, SCRATCH[buf][1][1] if c1 is None else c1, step)


def bank(b, c0, c1, step=1, p0=0, p1=128):
    return V("ps", 512 * b + c0, 512 * b + c1, step, p0, p1)


def _mask(v):
    if v[0] == "ps":
        return 1 << (v[3] // 512)
    if v[5] == 1:
        return ((1 << (v[4] - v[3])) - 1) << v[3]
    m = 0
    for c in range(v[3], v[4], v[5]):
        m |= 1 << c
    return m


def _remote(o):
    return bool(o[4]) and o[4].startswith("arr")


_ORDER = []


def arrange(ops):
    if not _ORDER:
        _ORDER.extend(search(ops))
    return [ops[i] if k == 0 else ops[i][7] for i, k in _ORDER[0]], _ORDER[1]


def search(ops):
    n = len(ops)
    seen, before, sends = {}, [], {}
    for i, o in enumerate(ops):
        deps = {}
        for vs, wr in ((o[2], False), (o[3], True)):
            for v in vs:
                m = _mask(v)
                for (j, w2, p0, p1, m2) in seen.get(v[0], ()):
                    if (m2 & m) and (wr or w2) and p0 < v[2] and v[1] < p1:
                        both_pe = o[0] == "P" and ops[j][0] == "P"
                        deps[j] = (0, 0, 0, 0) if both_pe else (1, LOAD, 0, 0) if ops[j][4] else (1, 60, 0, 0) if ops[j][0] == "P" else (1, 0, 0, 0)
        for vs, wr in ((o[2], False), (o[3], True)):
            for v in vs:
                seen.setdefault(v[0], []).append((i, wr, v[1], v[2], _mask(v)))
        if _remote(o):
            sends.setdefault(o[4], []).append(i)
        for e in o[5]:
            for j in sends[e[0]]:
                deps[j] = (1, 0, 1, 1 if e[0] == list(sends)[0] else 0)
        before.append(deps)
    reach = []
    for i, d in enumerate(before):
        r = 0
        for j in sorted(d, reverse=True):
            if r >> j & 1 and d[j] == (1, 0, 0, 0):
                del d[j]
            r |= reach[j] | 1 << j
        reach.append(r)
    after = [[] for _ in ops]
    for i, d in enumerate(before):
        for j in d:
            after[j].append(i)
    forms = [[o for o in (ops[i], ops[i][7]) if o is not None] for i in range(n)]
    product = [max([v[3] // 512 for v in o[2] + o[3] if v[0] == "ps"] + [-1]) for o in ops]
    cases = []
    for (wake, flight, once, pe, ga, gp) in CASES:
        lag = [[(j, w[0] * wake + w[1] + w[2] * flight + w[3] * once) for j, w in d.items()] for d in before]
        cost = [[o[6] * (pe if o[0] == "P" else gp if o[0] == "G" else 1.0) * (ga if o[8] else 1.0) for o in f] for f in forms]
        cases.append((wake, lag, cost))
    queue_of = [["VSPGY".index(o[0]) for o in f] for f in forms]
    last = [LOAD if o[4] else 0 for o in ops]
    uses = {}
    for x in product:
        uses[x] = uses.get(x, 0) + 1

    def build():
        left = [len(d) for d in before]
        ready, seq, open_ = [i for i in range(n) if not left[i]], [], {}
        while ready:
            i = min([i for i in ready if product[i] < 0 or product[i] in open_ or sum(1 for x in open_.values() if x) < BANKS],
                    key=lambda i: ops[i][9])
            if product[i] >= 0:
                open_[product[i]] = open_.get(product[i], uses[product[i]]) - 1
            seq.append(i)
            ready.remove(i)
            for j in after[i]:
                left[j] -= 1
                if not left[j]:
                    ready.append(j)
        return seq, [1 if o[7] and o[10] == "S" else 0 for o in ops]

    def place(seq):
        idle, at, left, user, behind = list(range(BANKS)), {}, {}, [-1] * BANKS, {}
        for i in seq:
            x = product[i]
            if x >= 0:
                if x not in at:
                    if not idle:
                        return None, None
                    at[x], left[x] = idle.pop(0), uses[x]
                behind[i], user[at[x]] = user[at[x]], i
                left[x] -= 1
                if not left[x]:
                    idle.append(at[x])
        return at, behind
    seed = [SEED]

    def rnd(m):
        seed[0] = (seed[0] * 1103515245 + 12345) % 2147483648
        return (seed[0] >> 8) % m
    seq, form = build()
    narrow = [i for i, o in enumerate(ops) if o[3] and o[3][0][0] == "lrow"]

    def run(seq, form, at, known, stop=n):
        total, res, behind = 0.0, [], place(seq)[1]
        if behind is None:
            return 1e9, None
        who = [-1] * 5
        for p in range(at - 1, -1, -1):
            q = queue_of[seq[p]][form[seq[p]]]
            if who[q] < 0:
                who[q] = seq[p]
                if min(who) >= 0:
                    break
        steps = [(i, form[i], queue_of[i][form[i]], behind.get(i, -1)) for i in seq[at:stop]]
        steps = [(i, k, q, b if b >= 0 and queue_of[b][form[b]] != q else -1) for i, k, q, b in steps]
        for c, (wake_, lag_, cost_) in enumerate(cases):
            end, why = (list(known[c][0]), list(known[c][1])) if known else ([0.0] * n, [-1] * n)
            by = list(who)
            free = [end[x] if x >= 0 else 0.0 for x in who]
            for i, k, q, b in steps:
                t, w = free[q], -2 - by[q]
                for j, x in lag_[i]:
                    if end[j] + x >= t:
                        t, w = end[j] + x, j
                if b >= 0 and end[b] + wake_ > t:
                    t, w = end[b] + wake_, -2 - b
                end[i] = free[q] = t + cost_[i][k]
                why[i], by[q] = w, i
            total += max([e + x for e, x in zip(end, last)]) + EARLY * sum(end) if stop == n else end[i] - known[c][0][i]
            res.append((end, why))
        return total, res

    def chains(seq, known):
        out = []
        for end, why in known:
            i, held = max(range(n), key=lambda x: end[x] + last[x]), []
            while i != -1:
                w = why[i]
                if w <= -2:
                    w = -2 - w
                    held.append((w, i))
                i = w
            out.append(held)
        return out, {x: p for p, x in enumerate(seq)}
    now, known = run(seq, form, 0, None)
    best = (now, seq, form)
    held, where = chains(seq, known)
    for trial in range(TRIES):
        some = held[rnd(len(cases))]
        j, i = some[rnd(len(some))]
        if rnd(100) < ASIDE:
            i = rnd(n)
            j = -2 - known[rnd(len(cases))][1][i]
            if j < 0:
                continue
        s2, f2, kind, to = seq, form, rnd(10), where[i] + 1
        if kind < 3:
            x = (i, j)[rnd(2)]
            if len(forms[x]) < 2:
                continue
            f2 = list(form)
            f2[x] = 1 - f2[x]
            at = where[x]
        elif kind < 7:
            at = max(0, where[j] - (rnd(12) if rnd(2) else 0))
            part = seq[at:where[i] + 1]
            up = [x for x in part if x == i or reach[i] >> x & 1]
            if j in up:
                continue
            s2 = seq[:at] + up + [x for x in part if x not in up] + seq[where[i] + 1:]
        else:
            at, to = where[j], min(n, where[i] + 1 + (rnd(30) if rnd(2) else 0))
            part = seq[at:to]
            down = [x for x in part if x == j or reach[x] >> j & 1]
            if i in down:
                continue
            s2 = seq[:at] + [x for x in part if x not in down] + down + seq[to:]
        room = HEAT * (1 - trial / TRIES) * rnd(1000) / 1000
        stop = [where[x] + 1 for x in narrow if where[x] >= to]
        if stop and run(s2, f2, at, known, stop[0])[0] > room:
            continue
        t2, k2 = run(s2, f2, at, known)
        if t2 <= now + room:
            now, seq, form, known = t2, s2, f2, k2
            held, where = chains(seq, known)
            if now < best[0]:
                best = (now, seq, form)
    order = [(i, best[2][i]) for i in best[1]]
    return order, place(best[1])[0]


def rank_program(g, core, T, topo):
    rank = T.rank_of(core)
    if rank is None:
        return
    n_ranks = len(T.cores)
    ops = []
    arriving = [()]
    banks, products = {}, [0]

    plan = [0, 0, "V", START]

    def when(step, k=0, more=0):
        at, queues = (plan[3].get(step) or ROUND[step])[:2]
        plan[1:3] = (at[k] if isinstance(at, tuple) else at) + more, queues[k % len(queues)]

    def new(k=None):
        products[0] += k or 1
        return products[0] - 1 if k is None else range(products[0] - k, products[0])

    def ap(v):
        if not isinstance(v, tuple):
            return v
        if v[0] == "ps":
            by = 512 * (banks[v[3] // 512] - v[3] // 512)
            return T.ps[v[1]:v[2], v[3] + by:v[4] + by]
        if v[0] == "ind":
            return ap(v[1]).indirect(ap(v[2]))
        if v[0] == "ind32":
            return ap(v[1]).bitcast(dt.uint32).indirect(ap(v[2]))
        return T[v[0]][v[1]:v[2], v[3]:v[4]:v[5]] if v[5] != 1 else T[v[0]][v[1]:v[2], v[3]:v[4]]

    def parts(vs):
        out = []
        for v in vs:
            if isinstance(v, tuple):
                out += [v[1], v[2]] if v[0] in ("ind", "ind32") else [v]
        return out

    def span(q, reads, writes, rate=1.0):
        a = reads[0] if reads else writes[0]
        if a[0] in ("ind", "ind32"):
            return 60 + GATHER * 16 * (a[2][4] - a[2][3])
        n = len(range(a[3], a[4], a[5]))
        if q == "V":
            if all(SCRATCH[v[0]][2] == BF for v in parts(reads)[:2] + [writes[0]] if v[4] - v[3] > 1):
                rate *= 0.5
            return max(64, n * rate)
        return (S_FIX + n) if q == "S" else 150 + 2 * n

    def op(q, emit, reads, writes, dma=None, cost=None, other=None):
        if cost is None:
            cost = span(q, reads, writes)
        ops.append((q, emit, parts(reads), parts(writes), dma, arriving[0], cost, other, bool(reads) and reads[0][0] in ("ind", "ind32"),
                    plan[0] + plan[1], plan[2]))
        plan[1] += 1

    def ind(win, off):
        return ("ind", win, off)

    def ts(out, a, s1, s2, o0, o1=None):
        if o1 is None:
            op("V", lambda: g.vector.tensor_scalar(ap(out), ap(a), ap(s1), None, o0), [a, s1], [out])
        else:
            op("V", lambda: g.vector.tensor_scalar(ap(out), ap(a), ap(s1), ap(s2), o0, o1), [a, s1, s2], [out])

    def tt(out, a, b, o):
        op("V", lambda: g.vector.tensor_tensor(ap(out), ap(a), ap(b), o), [a, b], [out],
           cost=span("V", [a], [out]) if a[0] == "ind" else span("V", [b], [out], 1.0 if a[0] == "ps" else 2.0))

    def cp(out, a):
        op("V", lambda: g.vector.tensor_copy(ap(out), ap(a)), [a], [out])

    def scatter(win, off, a):
        op("V", lambda: g.vector.tensor_copy(ap(ind(win, off)), ap(a)), [a, off], [win], cost=60 + SCATTER * C)

    def scan(out, a, b, o0, o1, init=0.0):
        op("V", lambda: g.vector.tensor_tensor_scan(ap(out), ap(a), ap(b), ap(init), o0, o1), [a, b, init], [out])

    def fill(out, c):
        op("V", lambda: g.vector.memset(ap(out), c), [], [out])

    def act(out, a, f, bias=None, scale=None, acc=None):
        kw = {}
        if bias is not None:
            kw["bias"] = bias
        if scale is not None:
            kw["scale"] = scale
        if acc is not None:
            kw["accum_out"] = acc
        op("S", lambda: g.scalar.activation(ap(out), ap(a), f, **{k: ap(x) for k, x in kw.items()}),
           [a, bias, scale], [out, acc])

    def affine(out, a, scale, bias):
        act(out, a, ACT.Identity, bias=bias, scale=scale)

    def either():
        on_v, on_s = ops.pop(), ops.pop()
        ops.append(on_v[:2] + (on_s[2],) + on_v[3:7] + (on_s,) + on_v[8:])

    def move(q, out, a):
        if q != "V":
            act(out, a, ACT.Copy)
        if q != "S":
            cp(out, a)
        if q == "F":
            either()

    def iota(out, pattern, base=0, cm=0):
        if SCRATCH[out[0]][2] == I32:
            op("G", lambda: g.iota(ap(out), pattern, base, cm), [], [out])
        else:
            op("G", lambda: g.iota(ap(out), pattern, base, cm, allow_small_or_imprecise_dtypes=True), [], [out])

    def keep(out, a, pattern, cmp_, base, cm):
        op("G", lambda: g.affine_select(ap(out), ap(a), pattern, cmp_, 0.0, base, cm), [a], [out], cost=200 + 2 * (a[4] - a[3]))

    def spread(out, a):
        op("G", lambda: g.partition_broadcast(ap(out), ap(a), out[2]), [a], [out], cost=170 + 4 * (a[4] - a[3]))

    def quant(name, c0, tile, e0, n):
        qv, sv, tv = V("q_" + name, c0, c0 + n), V("s_" + name, c0, c0 + n), V(tile, e0, e0 + 4 * n)
        op("V", lambda: g.vector.quantize_mx(ap(qv), ap(sv), ap(tv)), [tv], [qv, sv], cost=15 + 1.06 * n)

    def mm(b, w, w0, x, x0, n, start=True, stop=True):
        o, a = bank(b, 0, n), [V("q_" + w, w0, w0 + 128), V("s_" + w, w0, w0 + 128), V("q_" + x, x0, x0 + n), V("s_" + x, x0, x0 + n)]
        op("P", lambda: g.tensor.matmul_mx(ap(o), ap(a[0]), ap(a[1]), ap(a[2]), ap(a[3]), start, stop), a, [o],
           cost=PE_COL * (n + 16))

    def pick(dst, d0, n, src, w1, off):
        o, w = V("q_" + dst, d0, d0 + n), ("ind32", V("q_" + src, 0, w1), off)
        op("V", lambda: g.vector.tensor_copy(ap(o).bitcast(dt.uint32), ap(w)), [w], [o])
        move("S", V("s_" + dst, d0, d0 + n), ind(V("s_" + src, 0, w1), off))

    def dma(q, sem, out, in_, reads, writes):
        eng = g.sync if q == "Y" else g.scalar
        op(q, lambda: eng.dma_start(out(), in_()), reads, writes, dma=sem, cost=50)

    def col(k, **p):
        return V("pc", k, k + 1, **p)

    def run32(a):
        return dict(p0=32 * a, p1=32 * a + 32)
    (P_L, P_E, P_LH, P_LQ, P_L4, P_L1, P_MK, P_CJ, P_O4, P_T, P_T0, P_T1, P_NQ, P_X, P_Y, P_R2, P_OS, P_Z,
     P_I1, P_I2) = range(20)

    def unpack(bk, k, ev, e0, od, o0, w):
        if (ev, e0) == (od, o0):
            return mm(bk, "e", (8 + k) * 128, ev, e0, w)
        mm(bk, "e", 2 * k * 128, ev, e0, w, True, False)
        mm(bk, "e", (2 * k + 1) * 128, od, o0, w, False, True)

    def zero(out):
        act(out, V("ones", 0, out[4] - out[3]), ACT.Identity, scale=0.0)
        fill(out, 0.0)
        either()

    first_loads = [V("xt"), V("ut")]
    dma("Y", "dx", lambda: T.xt[:], lambda: T.x[:], [], [V("xt")])
    dma("S", "du", lambda: T.ut[:], lambda: T.u[:], [], [V("ut")])
    dma("Y", "dwc", lambda: T.q_w[:].bitcast(dt.uint8), lambda: T.wc[:], first_loads, [V("q_w")])
    dma("Y", "dws", lambda: T.s_w[:], lambda: T.ws[:], first_loads, [V("s_w")])
    dma("Y", "dv", lambda: T.vt[:], lambda: T.v[:], first_loads, [V("vt")])

    iota(V("pi"), [[0, 1]], 0, 1)
    fill(V("ze"), 0.0)
    fill(V("ones", 0, 128), 1.0)
    fill(V("ones", 128, 512), 1.0)
    iota(V("i16", 0, 16), [[16, 16]])
    when("zf")
    fill(V("zf"), 0.0)
    when("zeros g")
    quant("g", R * C, "zf", 0, 128)
    when("lanes")
    iota(V("j16"), [[0, 16], [1, 16]])
    keep(V("ze", 3, 512, 4), V("ones", 0, 128), [[32, 4], [1016, 2], [1, 16]], ALU.is_equal, 0, -1)
    keep(V("ze", 515, 1024, 4), V("ones", 0, 128), [[32, 4], [-984, 2], [1, 16]], ALU.is_equal, 1000, -1)
    keep(V("bd0"), V("ones"), [[-16, 8], [0, 64]], ALU.is_ge, 0, 1)
    keep(V("bd", 0, 512), V("bd0"), [[16, 8], [0, 64]], ALU.is_ge, 15, -1)
    iota(V("i256"), [[1, C]])
    keep(V("zf", 3, 512, 4), V("ones", 0, 128), [[1, 128]], ALU.is_equal, 0, -1)
    iota(V("j4"), [[0, 64], [1, 4]])
    iota(V("i16", 16, 24), [[32, 4], [0, 2]], 16)
    kinds = []
    for p in PIECES:
        if kinds and kinds[-1][0] == (p[1] is None,) + p[2:]:
            kinds[-1][2] += 1
        else:
            kinds.append([(p[1] is None,) + p[2:], PL[p], 1])
    for (mixed, i0, n), c0, reps in kinds:
        w = n // (8 if mixed else 16)
        iota(V("ia", c0, c0 + w * reps), [[0, reps], [4 if mixed else 8, w]], i0 // 2)
    for k, seg in enumerate(SEGS):
        when("zeros ct", k)
        low = 16 * min(j for j in seg if j != "q")
        zero(V("ct", 4 * (SEG0[k] + low), 4 * (SEG0[k + 1] if k + 1 < len(SEGS) else CT_N)))
    zero(V("rs", 0, 1))
    for k, v in enumerate((V("sh", 16 * C, 16 * C + 128), V("gb", 4 * M, 512), V("gt", 4 * K, 4 * GT_L))):
        when("zeros", k)
        zero(v)
    when("negate")
    affine(V("bd", 512, 1024), V("bd", 0, 512), -1.0, 0.0)
    ts(V("bd", 512, 1024), V("bd", 0, 512), -1.0, None, ALU.mult)
    either()
    when("lanes")
    for k, (by, low) in enumerate(((0, 15), (4, 1), (1, 7), (2, 3), (0, 3), (0, 1))):
        ts(V("pci", k, k + 1), V("pi"), by, low, ALU.logical_shift_right, ALU.bitwise_and)
    cp(V("pc", 0, 2), V("pci", 0, 2))
    cp(V("pc", 2, 6), V("pci", 2, 6))
    cp(V("ul", 0, 8), V("i16", 0, 8))
    when("ul")
    cp(V("ul", 8, 16), V("i16", 16, 24))
    ts(V("a2l"), V("i16", 0, 16), 0.5, col(P_LH), ALU.mult, ALU.add)
    when("masks")
    affine(col(P_MK), col(P_L), -BIG, 0.0)
    act(col(P_Y), col(P_L), ACT.Relu, bias=87040.0, scale=-6144.0)
    affine(col(P_Z), col(P_L), 1.0, -1024.0)
    act(V("d0"), V("j16"), ACT.Relu, bias=64 * BIG, scale=-64 * BIG)
    act(V("mk"), V("j16"), ACT.Abs, bias=col(P_MK), scale=BIG)
    affine(col(P_CJ), col(P_Y), -1.0, col(P_Z))
    affine(col(P_R2), col(P_E), 1.0, 2048.0)
    when("weights")
    act(V("tmp", 0, C), V("j16"), ACT.Sign, bias=col(P_MK), scale=BIG)
    act(V("qm"), V("j16"), ACT.Sign)
    affine(V("cj"), V("i16", 0, 16), 1.0, col(P_CJ))
    affine(V("w16", W0), V("tmp", 0, C), 5120.0, 1024.0)
    when("wrap")
    affine(col(P_NQ), col(P_LQ), -1.0, 0.0)
    affine(col(P_X), col(P_L4), 1.0, -12288.0)
    affine(col(P_O4), col(P_LQ), 4096.0, col(P_X))
    act(V("tmp", C, 2 * C), V("j4"), ACT.Sign, bias=col(P_NQ))
    act(V("tmp", 2 * C, 3 * C), V("tmp", C, 2 * C), ACT.Abs, scale=17408.0)
    affine(V("w4"), V("tmp", 2 * C, 3 * C), 1.0, -16384.0)
    for b in range(4):
        when("eo tiles", b)
        quant("e", 2 * b * 128, "ze", 3 - b, 256)
        when("full tiles", b)
        quant("e", (8 + b) * 128, "zf", 3 - b, 128)
    when("bd")
    quant("bd", 0, "bd", 0, 128)
    quant("bd", 128, "bd", 512, 128)
    when("lists")
    single = sum(p[3] // 16 for p in PIECES if p[1] is not None)
    if single:
        affine(V("plf", 0, single), V("ia", 0, single), 1.0, col(P_LH))
    affine(V("plf", single, PL_N), V("ia", single, PL_N), 1.0, col(P_LQ))
    for k, w in ((P_I1, K), (P_I2, M)):
        affine(col(k), col(P_L1), float(w), col(P_LH))
    for p in PIECES:
        a, e, i0, n = p
        if e is None:
            c0 = EO_L if i0 else EO_E
            affine(V("plf", PL[p], PL[p] + n // 8, **run32(a)), V("i256", c0 // 8, (c0 + n) // 8, **run32(a)), 8.0,
                   col(P_I2 if i0 else P_I1, **run32(a)))
        else:
            c0 = (EO_E, EO_O)[e]
            affine(V("plf", PL[p], PL[p] + n // 16, **run32(a)), V("i256", c0 // 16, (c0 + n) // 16, **run32(a)), 16.0, col(P_L, **run32(a)))
    when("pl")
    if single:
        cp(V("pl", 0, single), V("plf", 0, single))
    cp(V("pl", single, PL_N), V("plf", single, PL_N))
    when("tab")
    affine(col(P_T0), col(P_E), float(K), float(EO_E))
    affine(col(P_T1), col(P_E), float(M), float(EO_L - K))
    affine(col(P_OS), col(P_T0), -4.0, col(P_O4))
    affine(V("tab", 0, K), V("i256", 0, K), 1.0, col(P_T0))
    affine(V("tab", K, C), V("i256", K, C), 1.0, col(P_T1))
    when("v")
    quant("v", 0, "vt", 0, 128)
    when("u")
    quant("u", 0, "ut", 0, 128)
    quant("x", 0, "xt", 0, C)
    pick("us", 0, 128, "u", 128, V("ul", 0, 8))
    when("us")
    if G_RUNS:
        pick("us", 128, 128, "u", 128, V("ul", 8, 16))
    when("scores")
    for_v, for_s = new(2)
    mm(for_v, "us", 0, "x", 0, C)
    mm(for_s, "us", 0, "x", 0, C)

    def slot(j, c0, c1, step=1):
        base, t = SLOT[j]
        return V("ct", 4 * (base + c0) + t, 4 * (base + c1), 4 * step)

    def key(j):
        return V("zs", 16 * j + 15, 16 * j + 16)

    def ranks(first):
        def row(q, c0, c1):
            return bank(for_v if q == "V" else for_s, c0, c1) if first else V("rr", c0, c1)

        def scores(c0, c1):
            return bank(for_v, c0, c1) if first else ind(V("r2"), V("r2l", c0 // 16, c1 // 16))
        for k, (c0, c1) in enumerate(KEYS):
            when("inj", k)
            tt(V("inj", c0, c1), scores(c0, c1), V("mk", c0, c1), ALU.add)
            when("zs", k)
            scan(V("zs", c0, c1), V("d0", c0, c1), V("inj", c0, c1), ALU.add, ALU.min)
        when("inj")
        if not first:
            act(V("rr"), scores(0, C), ACT.Copy)
        when("q", 0)
        tt(slot("q", 0, C), scores(0, C), V("zs"), ALU.is_gt)
        when("q", 1)
        scan(V("qs"), V("qm"), slot("q", 0, C), ALU.mult, ALU.add)
        when("q", 2)
        tt(V("wa"), V("cj"), V("qs", 15, C, 16), ALU.add)
        for j in range(15, 0, -1):
            n, end = 16 * j, W0 + 16 * j + 16
            if j in SEGS[1]:
                i = SEGS[1].index(j)
                when("sign", 0, 300 * i)
                act(V("gs", i * C, i * C + n), row("S", 0, n), ACT.Sign, bias=key(j), scale=-1.0)
                when("sign", 1, 300 * i)
                act(slot(j, 0, n), V("gs", i * C, i * C + n), ACT.Relu, acc=V("rs", j, j + 1))
            else:
                when("above", 0 if j > 8 else 1 if j > 4 else 2, -j)
                ts(slot(j, 0, n), row("V", 0, n), key(j), -1.0, ALU.is_lt, ALU.mult)
                when("sums", 0 if j > 7 else 1 if j >= SHORT else 2, -j)
                if j < SHORT:
                    act(V("gs", 4 * C + 8 * j * (j - 1), 4 * C + 8 * j * (j + 1)), slot(j, 0, n), ACT.Abs, acc=V("rs", j, j + 1))
                else:
                    scan(V("w16", end - 1 - RW * (n // 2 - 1), end, RW), slot(j, 0, n, 2), slot(j, 1, n, 2), ALU.add, ALU.add, V("wa", j, j + 1))
        when("w")
        for j0, j1 in ((min(SEGS[1]), 16), (0, SHORT)):
            tt(V("w16", W0 + 16 * j0 + 15, W0 + 16 * j1, 16), V("wa", j0, j1), V("rs", j0, j1), ALU.subtract)
        for k, (c0, c1) in enumerate(((SEG0[0], SEG0[1]), (SEG0[2], CT_N if first else SEG0[4]), (SEG0[1], SEG0[2]))):
            when("ct", k)
            quant("ct", c0, "ct", 4 * c0, c1 - c0)
        counts = new()
        for k in (0, 2, 3, 1):
            mm(counts, "bd", 0 if k == 1 else 128, "ct", SEG0[k], max(128, SEG0[k + 1] - SEG0[k]), k == 0, k == 1)
        when("uw")
        scan(V("uw"), bank(counts, 0, C), V("w16", W0), ALU.max, ALU.add, -1024.0)
        when("rku")
        ts(V("rku"), V("uw", 15, C, 16), 1024.0, None, ALU.add)

    def wrap4(row, off, u0, c0, c1, cut=None):
        for a, b in ((c0, cut), (cut, c1)) if cut else ((c0, c1),):
            scan(V("u4", u0 + a, u0 + b), V("w4", a, b), V(row[0], row[3] + a, row[3] + b), ALU.add, ALU.max)
        ts(V(off, c0 // 4, c1 // 4), V("u4", u0 + c0 + 3, u0 + c1, 4), 4.0, col(P_O4), ALU.mult, ALU.add)

    def sh0(s):
        return 4 * C * (R - s)

    def vrow(s):
        return V("vrow", C * s, C * s + C)

    def gather(q, s, win, c0, c1):
        move(q, V("sh", sh0(s) + 4 * c0, sh0(s) + 4 * c1), ind(win, V("off", c0 // 4, c1 // 4)))

    sent = [0]

    def send(t, sem, pairs):
        dst = T.cores[(rank + 1 + t) % n_ranks]
        rid, pid = topo.addr(dst)[:2]
        mask = topo.mask(core, dst)
        for out, a in pairs:
            cast = (lambda v: ap(v).bitcast(dt.uint8)) if SCRATCH[a[0]][2] == X4 else ap
            op("G", lambda out=out, a=a, cast=cast: g.remote_dma(cast(out), cast(a), T.sem[sem], T.sem.sent, pid, rid, mask),
               [a], [], dma=sem, cost=300)
            sent[0] += len(topo.engines(core, dst))

    def arrival(t, sem, calls):
        return ((sem, calls * len(topo.engines(T.cores[(rank - 1 - t) % n_ranks], core))),)

    def g0(t):
        return (R - 1 - t) * C

    def send_state(t, sem, c0, pair, p0, n):
        send(t, sem, [(V(k + "g", g0(t) + c0, g0(t) + c0 + n), V(k + pair, p0, p0 + n)) for k in ("q_", "s_")])

    def h_tile(t):
        e0, l0 = sh0(t + 1) + 4 * K, t * M // 4
        arriving[0] = arrival(t, "arro%d" % t, 1)
        when("gb")
        move("V", V("gb", 0, 2 * M), ind(V("gt"), V("ofg", l0, l0 + M // 8)))
        move("S", V("gb", 2 * M, 4 * M), ind(V("gt"), V("ofg", l0 + M // 8, l0 + M // 4)))
        arriving[0] = ()
        when("land")
        quant("land", 0, "gb", 0, 128)
        for b, bk in enumerate(new(4)):
            when("W", b, 90 * b)
            mm(bk, "w", 128 * b, "land", 0, 128)
            when("W", b, 380 + 180 * b)
            act(V("rel", M * b, M * b + M), bank(bk, 0, M), ACT.Relu, scale=0.03125)
            ts(V("rel", M * b, M * b + M), bank(bk, 0, M), 0.0, 0.03125, ALU.max, ALU.mult)
            either()
        for b, bk in enumerate(new(4)):
            when("D", 0, 90 * b)
            unpack(bk, b, "land", 0, "land", 0, 128)
            when("add", 0, 100 * b)
            tt(V("sh", e0 + b, e0 + 4 * M, 4), bank(bk, 0, M), V("rel", M * b, M * b + M), ALU.add)

    plan[0] = 4000 - ROUND["inj"][0][0]
    ranks(True)
    for s in range(R + 1):
        when("next")
        plan[0], plan[3] = plan[0] + plan[1], FIRST if s == 0 else {}
        when("scatter")
        win = V("xt") if s == 0 else V("eo%d" % (s - 1))
        scatter(V("lrow"), V("rku"), V("i256") if s == 0 else vrow(s - 1))
        act(vrow(s), ind(V("tab" if s < R else "i256"), V("rku")), ACT.Copy)
        b, m, n, eo, y = ["%s%d" % (k, s) for k in ("b", "m", "n", "eo", "y")]
        when("off")
        wrap4(V("lrow"), "off", 0, 0, K, M if s else None)
        when("ofs")
        if s > 0:
            l0 = (s - 1) * M // 4
            ts(V("ofs", l0, l0 + M // 4), V("u4", 3, M, 4), 4.0, col(P_OS), ALU.mult, ALU.add)
            send(s - 1, "arro%d" % (s - 1), [(V("ofg", l0, l0 + M // 4), V("ofs", l0, l0 + M // 4))])
        when("gather")
        gather("V", s, win, 0, K // 2)
        gather("S", s, win, K // 2, K)
        if s == R:
            break
        when("b")
        quant(b, 0, "sh", sh0(s), K)
        send_state(s, "arre%d" % s, 0, b, 0, K)

        def also(step, k):
            return (plan[3].get(step) or ROUND[step])[k]

        def parts_of(step, ev, c_ev, od, c_od, w, c0):
            for k, bk in enumerate(new(4)):
                when(step, k, also(step, 2) * k)
                unpack(bk, k, ev, c_ev, od, c_od, w)
                when(step, k, also(step, 2) * (k + 1) + 290)
                move("F", V(eo, 4 * c0 + k, 4 * (c0 + w), 4), bank(bk, 0, w))
            plan[1] = also(step, 3)
            quant(eo, c0, eo, 4 * c0, w)

        def by_rows(e):
            runs = range(G_RUNS - 1, -1, -1)
            c0, w, bk = K * len(runs) * e, K * len(runs), new()
            p0 = PL[(runs[0], e, 0, K)]
            when("rows", e)
            pick(y, c0, w, eo, (EO_O, EO_L)[e], V("pl", p0, p0 + w // 16))
            plan[1] = also("rows", 2)[e]
            mm(bk, "us", 128 * e, y, c0, w)
            return [(V("r2", e, 2 * K, 2, p1=32 * a + 32), bank(bk, K * i, K * i + K, p0=32 * a, p1=32 * a + 1))
                    for i, a in enumerate(runs)]

        def by_run(a0, runs, i0, w):
            c0 = 2 * K * a0 if i0 == 0 else 8 * K + 2 * w * a0
            p0 = PL[(a0, None, i0, w)]
            step = "late" if i0 else "early"
            when(step, a0 % 2)
            pick(y, c0, 2 * w * runs, eo, EO_L if i0 == 0 else EO_N, V("pl", p0, p0 + w * runs // 8))
            for k, bk in enumerate(new(runs)):
                plan[1] = also(step, 2)[a0 % 2] + 125 * k
                mm(bk, "us", 0, y, c0 + 2 * w * k, 2 * w)
                plan[1:3] = plan[1] + 420, also(step, 1)[(a0 + k) % len(also(step, 1))]
                move("F", V("r2", 2 * i0, 2 * (i0 + w), **run32(a0 + k)), bank(bk, 0, 2 * w, **run32(a0 + k)))

        def givers(sems, c_ev, c_od, c0):
            for k, bk in enumerate(new(4)):
                arriving[0] = sum([arrival(s, x % s, 2) for x in sems], ())
                when("givers", len(sems) - 1, 240 * k - 500)
                unpack(bk, k, "g", g0(s) + c_ev, "g", g0(s) + c_od, K)
                arriving[0] = ()
                when("givers", len(sems) - 1, 240 * k)
                move("F", V("gt", 4 * c0 + k, 4 * (c0 + K), 4), bank(bk, 0, K))

        when("r2l")
        ts(V("r2l"), V("uw", 15, C, 16), 2.0, col(P_R2), ALU.mult, ALU.add)
        when("m")
        pick(m, 0, K, b, 128, V("a2l", 0, K // 16))
        pick(n, 128, M, b, 128, V("a2l", K // 16, 16))
        parts_of("A", b, 0, b, 0, 128, EO_A)
        parts_of("E", b, 0, m, 0, K, EO_E)
        parts_of("O", m, 0, b, 0, K, EO_O)
        rows = (by_rows(0), by_rows(1)) if G_RUNS else ([], [])
        for e in range(2):
            for a in range(G_RUNS - 1, G_TAKES[s][e] - 1, -1):
                o, i = rows[e].pop(0)
                move("F", o[:1] + (32 * a, 32 * a + 32) + o[3:], i[:1] + (32 * a, 32 * a + 32) + i[3:])
        for k, x in enumerate(rows[0] + rows[1]):
            when("spread", 0, 1000 * k)
            spread(*x)
        for a in range(G_RUNS, 4):
            by_run(a, 1, 0, K)
        if s > 0:
            h_tile(s - 1)
        else:
            when("rest")
            wrap4(V("lrow"), "off", 0, K, C)
            when("gather rest")
            gather("F", s, win, K, C)
        when("n")
        quant(n, 0, "sh", sh0(s) + 4 * 128, 128)
        quant(n, 128 + M, "sh", sh0(s) + 4 * K, 128)
        send_state(s, "arrl%d" % s, K, n, 128 - M, M)
        parts_of("L", n, 128 - M, n, 128, 2 * M, EO_L)
        by_run(0, 3, K, M)
        by_run(3, 1, K, M)
        givers(["arre%d"], 0, 0, 0)
        givers(["arre%d", "arrl%d"], C - K, K, GT_L)
        ranks(False)

    when("off2")
    wrap4(vrow(R), "off2", C, 128, C)
    wrap4(vrow(R), "off2", C, 0, 128)
    scatter(V("orow"), V("rku"), V("i256"))
    dma("Y", "dol", lambda: T.ol[:], lambda: T.orow[0:128:16, :], [V("orow")], [])
    h_tile(R - 1)
    last = V("sh", sh0(R), sh0(R) + 4 * C)
    when("out")
    move("V", V("tt", 0, 2 * C), ind(last, V("off2", 0, 32)))
    move("S", V("tt", 2 * C, 4 * C), ind(last, V("off2", 32, 64)))
    for h in range(2):
        quant("t", 128 * h, "tt", 2 * C * h, 128)
        bk = new()
        mm(bk, "v", 0, "t", 128 * h, 128)
        move("F", V("yt", 128 * h, 128 * h + 128), bank(bk, 0, 128))
        dma("Y", "doc%d" % h, lambda h=h: T.oc[:, 512 * h:512 * h + 512], lambda h=h: T.q_t[:, 128 * h:128 * h + 128].bitcast(dt.uint8),
            [V("q_t", 128 * h, 128 * h + 128)], [])
        dma("Y", "dy%d" % h, lambda h=h: T.y[:, 128 * h:128 * h + 128], lambda h=h: T.yt[:, 128 * h:128 * h + 128],
            [V("yt", 128 * h, 128 * h + 128)], [])

    def store_scales(k, q):
        dma(q, "ds%d" % k, lambda: T.osc[4 * k:4 * k + 4, :], lambda: T.s_t[32 * k:32 * k + 4, :], [V("s_t")], [])
    store_scales(0, "S")
    store_scales(1, "S")
    store_scales(2, "S")
    store_scales(3, "S")

    ops, at = arrange(ops)
    banks.update(at)

    def placed(vs):
        return [v[:3] + (512 * at[v[3] // 512], 512 * at[v[3] // 512] + 512, 1) if v[0] == "ps" else v for v in vs]
    ops = [o[:2] + (placed(o[2]), placed(o[3])) + o[4:] for o in ops]

    src = [o[4] if o[4] else o[0] for o in ops]
    seen = {}
    know = {q: {} for q in "VSPGY"}
    clock, waits, needed = [], [], set()
    for i, o in enumerate(ops):
        q, deps = o[0], set()
        for vs, wr in ((o[2], False), (o[3], True)):
            for v in vs:
                mk_ = _mask(v)
                psum = v[0] == "ps"
                for (j, w2, p0, p1, m2) in seen.get(v[0], ()):
                    if not (m2 & mk_):
                        continue
                    if psum:
                        if src[j] != q:
                            deps.add(j)
                    elif (wr or w2) and p0 < v[2] and v[1] < p1:
                        deps.add(j)
        for vs, wr in ((o[2], False), (o[3], True)):
            for v in vs:
                seen.setdefault(v[0], []).append((i, wr, v[1], v[2], _mask(v)))
        best = {}
        for j in deps:
            best[src[j]] = max(best.get(src[j], -1), j)
        mine = []
        for j in sorted(best.values(), reverse=True):
            if know[q].get(src[j], -1) < j:
                mine.append(j)
                know[q][src[j]] = j
                for k2, x in clock[j].items():
                    know[q][k2] = max(know[q].get(k2, -1), x)
        needed.update(mine)
        waits.append(mine)
        clock.append(dict(know[q]))
    queue = {"V": g.vector, "S": g.scalar, "P": g.tensor, "G": g, "Y": g.sync}
    count, value, waited = {q: 0 for q in "VSPG"}, {}, set()
    for i, o in enumerate(ops):
        q, sem = o[0], o[4]
        for e in o[5]:
            if (q, e) not in waited:
                waited.add((q, e))
                queue[q].wait_ge(T.sem[e[0]], e[1])
        for j in waits[i]:
            queue[q].wait_ge(T.sem[value[j][0]], value[j][1])
        ins = o[1]()
        if _remote(o):
            continue
        if sem:
            ins.then_inc(T.sem[sem], 16)
            value[i] = (sem, 16)
        elif i in needed:
            count[q] += 1
            ins.then_inc(T.sem["c" + q], 1)
            value[i] = ("c" + q, count[q])
    g.wait_ge(T.sem.sent, sent[0])
    for o in ops:
        if o[4] and not _remote(o):
            g.wait_ge(T.sem[o[4]], 16)
